import numpy as np, ml_dtypes
CORES = [16,17,18,19,32,33,34,35]
N = 8
BF = ml_dtypes.bfloat16
def gentries(a):
    return np.ascontiguousarray(a.reshape(8, 16, -1).transpose(0, 2, 1)).reshape(8, -1)
def gtable(e):
    e = np.asarray(e); return np.ascontiguousarray(e.reshape(8, -1, 16).transpose(0, 2, 1)).reshape(128, -1).astype(np.int32)
V, Q, T, S, HOP = 2048, 256, 2, 2, 3
TH, TAU = 1020, (1020, 1530)
def toward(rng, shape, hub, share):
    h = hub[np.arange(8).reshape((1, 8) + (1,) * (len(shape) - 2)), rng.integers(0, hub.shape[1], shape)]
    return np.where(rng.random(shape) < share, h, rng.integers(0, V, shape))
def parts(rng):
    hub = rng.integers(0, V, (8, 32))
    X = rng.integers(0, 256, (N, 8, 16, V)); E = toward(rng, (N, 8, 16, V), hub, 0.1)
    v = toward(rng, (N, 8, Q), hub, 0.2); z = rng.integers(0, 256, (N, 8, 16, Q)); L = toward(rng, (N, 8, 16, Q), hub, 0.3)
    return X, E, v, z, L
def pack(X, E, v, z, L):
    return {"X": np.ascontiguousarray(X.reshape(N, 128, V)).astype(np.float32).astype(BF), "E": np.ascontiguousarray(E.reshape(N, 128, V)).astype(np.int32),
            "v0": np.stack([gtable(a) for a in v]), "z0": np.ascontiguousarray(z.reshape(N, 128, Q)).astype(np.float32).astype(BF), "L0": np.ascontiguousarray(L.reshape(N, 128, Q)).astype(np.int32)}
def setup_inputs(rng):
    return pack(*parts(rng))
def skew(rng, shape):
    col = shape[:2] + (1, shape[3])
    x = np.minimum((np.exp2(8 * rng.random(col)) * rng.random(shape)).astype(np.int64), 255)
    return np.where(rng.random(shape) < 0.5 * rng.integers(0, 2, col), 255 - x, x)
def lean(rng, shape):
    u = rng.random(shape); i = np.minimum((V * u * u * u).astype(np.int64), V - 1)
    return np.where(rng.random(shape[:2] + (1,) * (len(shape) - 2)) < 0.5, V - 1 - i, i)
def setup_inputs_spread(rng):
    return pack(skew(rng, (N, 8, 16, V)), lean(rng, (N, 8, 16, V)), lean(rng, (N, 8, Q)), skew(rng, (N, 8, 16, Q)), lean(rng, (N, 8, 16, Q)))
def setup_inputs_ends(rng):
    X, E, v, z, L = parts(rng)
    X = 255 * (rng.random(X.shape) < rng.choice(np.array([0.1, 0.5, 0.9]), (N, 8, 1, V))).astype(np.int64)
    z = 255 * (rng.random(z.shape) < rng.choice(np.array([0.0, 0.25, 0.5, 0.75, 1.0]), (N, 8, 1, Q))).astype(np.int64)
    E, v, L = [np.where(rng.random(a.shape) < 0.75, (V - 1) * rng.integers(0, 2, a.shape), a) for a in (E, v, L)]
    X[..., [0, 1, V - 3]] = 0; X[..., [2, V - 2, V - 1]] = 255
    for g in range(8):
        tie, full = (V - 1, V - 2) if g % 2 == 0 else (V - 2, V - 1)
        E[:, g, :, tie] = np.array([2, V - 1, V - 2, V - 1] * 4); E[:, g, :, full] = V - 1
        E[:, g, :, 1] = np.array([V - 3, 0, 1, 0] * 4); E[:, g, :, V - 3] = 0; E[:, g, :, 2] = np.array([V - 1, 2] * 8)
        if g % 4 != 2: E[:, g, 0, 0] = V - 1; E[:, g, 1, 0] = 0
    v[..., Q - 1] = V - 1; v[..., Q - 2] = V - 2; z[..., Q - 2:] = 0; L[..., Q - 2:] = V - 1; L[:, :, 15, Q - 2:] = 0
    v[..., 0] = 1; z[..., 0] = 255; v[..., 1] = 1; z[..., 1] = 0
    return pack(X, E, v, z, L)
def setup_inputs_corners(rng):
    X, E, v, z, L = parts(rng); own = np.arange(V); kinds = rng.permutation(8); h = V // 2
    for g in range(8):
        e, l, k = E[:, g], L[:, g], int(kinds[g])
        if k == 0: e[:] = own
        elif k == 1: e[:, 0::2] = (own + 1) % V; e[:, 1::2] = (own - 1) % V
        elif k == 2: e[:] = 0; e[:, 0] = V - 1
        elif k == 3:
            w = int(rng.choice(np.array([0, V - 1, h]))); l[:] = w; z[:, g] = 0
            e[:, 1] = e[:, 0]
            e[:, 0::2, w] = 5; e[:, 1::2, w] = 6; X[:, g, :, 5] = 255; X[:, g, :, 6] = 0
        elif k == 4: v[:, g] = V - 1; l[:] = V - 1
        elif k == 5:
            few = rng.permutation(h)[:64]; x = X[:, g]; x[:] = rng.integers(70, 256, x.shape)
            x[:, :, few[:32]] = rng.integers(240, 256, (N, 16, 32)); x[:, :, few[32:]] = rng.integers(70, 81, (N, 16, 32))
            e[:] = rng.integers(0, h, e.shape); e[:, 1, :h] = e[:, 0, :h]; z[:, g] = 0
            e[:, 0, h:] = few[rng.integers(0, 32, (N, V - h))]; e[:, 1, h:] = few[rng.integers(32, 64, (N, V - h))]
            l[:, :15] = rng.integers(0, h, (N, 15, Q)); l[:, 15] = rng.integers(h, V, (N, Q))
        elif k == 6: z[:, g] = 255; z[int(rng.integers(0, N)), g] = 0
        else:
            c = V // 4; o = rng.permutation(V).reshape(4, c); x = X[:, g]; z[:, g] = 255
            for i in range(4): e[:, :, o[i]] = o[i][rng.integers(0, c, (N, 16, c))]
            x[:, :, o[0]] = rng.integers(0, 64, (N, 16, c))
            x[:, :, o[1]] = rng.integers(252, 256, (N, 16, c)); x[:, :5, o[1]] = rng.integers(0, 16, (N, 5, c))
            x[:, :, o[2]] = np.array([0] * 5 + [255] * 2 + [215] * 2 + [255] * 7)[:, None]
            x[:, :, o[3]] = np.array([0] * 4 + [254] + [255] * 11)[:, None]
    v[..., 0] = 0; v[..., Q - 1] = V - 1
    return pack(X, E, v, z, L)
def setup_inputs_crowd(rng):
    X, E, v, z, L = parts(rng); A = T * S
    kinds = np.stack([rng.permutation(np.array([0, 1, 2, 4])), rng.permutation(np.array([0, 1, 3, 4]))], axis=1).reshape(-1)
    for g in range(8):
        k = int(kinds[g])
        if k == 4: continue
        h = V // 2; four = np.array([0, V - 1, 1 + 2 * int(rng.integers(0, V // 4)), h + 2 * int(rng.integers(0, V // 4))])
        o = rng.permutation(np.setdiff1d(np.arange(V), four))
        hi = np.concatenate([four, o[:h - 4]]); lo = o[h - 4:]
        w = X[:, g]; w[:, :, hi] = rng.integers(240, 256, (N, 16, h)); w[:, :, lo] = rng.integers(70, 81, (N, 16, h))
        z[:, g] = rng.integers(0, 4, (N, 16, Q))
        e = E[:, g]; e[:, :2] = lo[rng.integers(0, h, (N, 2, V))]
        if k < 2:
            hs = hi[:4]; names = np.repeat(hs[(np.arange(N) + int(rng.integers(0, 4))) % 4][:, None], Q, axis=1)
            if k == 1:
                miss = rng.integers(0, Q, N); miss[int(rng.integers(0, N))] = Q - 1; names[np.arange(N), miss] = -1
        elif k == 2:
            hs = hi[:4]; names = rng.choice(hs, (N, Q))
        else:
            hs = hi[rng.permutation(h)[:Q]]; names = np.stack([rng.permutation(hs) for _ in range(N)])
        n = len(hs)
        a = e[:, 0::2]; a[:, :, hs] = hi[rng.integers(4 if k < 2 else 0, h, (N, 8, n))]
        b = e[:, 1::2]; b[:, :, hs] = lo[rng.integers(0, h, (N, 8, n))]
        l = lo[rng.integers(0, h, (N, 16, Q))]
        here = np.argsort(np.argsort(rng.random((N, 16 - A, Q)), axis=1), axis=1) < T
        l[:, A:] = np.where(here & (names >= 0)[:, None], names[:, None], l[:, A:])
        L[:, g] = l
    return pack(X, E, v, z, L)
def setup_inputs_ties(rng):
    X, E, v, z, L = parts(rng); h = V // 2; o = rng.permutation(V); tw = np.zeros(V, np.int64); tw[o[:h]] = o[h:]; tw[o[h:]] = o[:h]
    X = 51 * rng.integers(0, 6, X.shape); z = 51 * rng.integers(0, 6, z.shape); X[..., o[:h]] = X[..., o[h:]]
    E[:, :, 8:] = tw[E[:, :, :8]]; E = np.ascontiguousarray(E[:, :, rng.permutation(16)])
    X[..., V - 2] = 0; X[:, :, 12:, V - 2] = 255; X[..., V - 4] = 0
    E[..., V - 1] = V - 2; E[..., V - 2] = V - 2; E[..., V - 3] = V - 4; E[:, :, 0, V - 3] = V - 2
    v[..., Q - 2:] = V - 1; z[..., Q - 2:] = 0; z[:, :, 0, Q - 2] = 51; L[..., Q - 2:] = V - 3
    return pack(X, E, v, z, L)
def check_inputs(d):
    bad = []
    for k, lo, hi in (("X", 0, 255), ("E", 0, V - 1), ("v0", 0, V - 1), ("z0", 0, 255), ("L0", 0, V - 1)):
        a = np.asarray(d[k]).astype(np.float64)
        if not (np.min(a) >= lo and np.max(a) <= hi and np.all(a == np.floor(a))): bad.append("range of " + k)
    return bad
def pick(tab, ix):
    return np.take_along_axis(tab, ix[:, None, :], 2)
def reference(X, E, v0, z0, L0):
    x = X.astype(np.float32).astype(np.int64).reshape(N, 8, 16, V); e = E.astype(np.int64).reshape(N, 8, 16, V)
    v = np.stack([gentries(a) for a in v0]).astype(np.int64)
    z = z0.astype(np.float32).astype(np.int64).reshape(N, 8, 16, Q); L = L0.astype(np.int64).reshape(N, 8, 16, Q)
    wt = (2 * np.arange(16) + 1)[None, :, None]
    for t in range(T):
        mark = np.zeros((N, 8, V), bool)
        for r in range(N):
            p = (r + HOP * t) % N; s = (p + HOP) % N; zr = z[r].copy(); vr = v[r].copy(); ll = L[r].copy()
            for step in range(S):
                c = pick(e[p], vr)
                far = np.add.reduce(np.abs(pick(x[p], c.reshape(8, -1)).reshape(8, 16, 16, Q) - zr[:, :, None, :]), axis=1)
                k = np.argmin(far, axis=1)
                vr = np.take_along_axis(c, k[:, None, :], 1)[:, 0]; ll[:, S * t + step] = vr
            like = np.min(far, axis=1) <= TH; xv = pick(x[p], vr)
            flat = ll.reshape(8, -1); a = np.take_along_axis(e[s][:, 0], flat, 1); b = np.take_along_axis(e[s][:, 1], flat, 1)
            zz = np.tile(zr, (1, 1, 16))
            gap = np.add.reduce(np.abs(np.maximum(pick(x[s], a), zz) - np.maximum(pick(x[s], b), zz)), axis=1).reshape(8, 16, Q)
            fail = gap > TAU[t]; some = np.any(fail, axis=1); f = np.argmax(fail, axis=1)
            cut = ~like & some; none = ~like & ~some
            u = np.take_along_axis(ll, f[:, None, :], 1)[:, 0]; base = np.take_along_axis(a.reshape(8, 16, Q), f[:, None, :], 1)[:, 0]
            gi, qi = np.nonzero(cut)
            mark[s, gi, u[gi, qi]] = True; ll[gi, f[gi, qi], qi] = base[gi, qi]
            half = (zr + xv) >> 1; h = np.add.reduce(half * wt, axis=1) & (V - 1)
            L[r] = ll; v[r] = np.where(cut, base, np.where(none, h, vr))
            z[r] = np.where(like[:, None, :], np.abs(zr - xv), np.where(none[:, None, :], half, zr))
        e = np.where(mark[:, :, None, :], np.roll(e, -1, axis=2), e)
    ya = np.add.reduce(e * (np.arange(16) + 1)[None, None, :, None], axis=2)
    return {"yv": v.astype(np.float32), "yz": z.reshape(N, 128, Q).astype(np.float32), "yl": L.reshape(N, 128, Q).astype(np.float32), "ya": ya.astype(np.float32)}

@@ -1,0 +1,648 @@
+import numpy as np
+from concourse.mybir import AluOpType as OP, AxisListType, ActivationFunctionType as AF
+
+F, B, I, U = "float32", "bfloat16", "int32", "uint16"
+SB = {
+    "eS": (2048, I), "xS": (2048, B), "zA": (256, B), "LA": (256, I), "vA": (16, I), "ef": (2048, F),
+    "t0": (128, I), "t1": (128, I), "t2": (128, I), "tf": (384, F), "elf": (384, F), "el": (256, U), "el2": (256, U),
+    "e0r": (128, I), "e1r": (128, I), "ys": (256, F), "s01": (256, F), "dy0": (128, F), "dy1": (128, F),
+    "iD": (256, I), "iA": (256, I), "iC": (8, I), "iN": (256, I), "zl": (256, U), "col": (32, F), "mg": (128, F),
+    "kk": (256, F), "io128": (128, B), "io16": (16, F), "jm": (16, F), "g16": (16, F), "gp": (16, F), "io2k": (2048, F),
+    "ck": (256, B), "ones": (128, B), "maskJ": (256, F), "Ib": (128, B), "nIb": (128, B), "If": (128, F), "nIf": (128, F),
+    "PHI": (256, B), "P16": (256, B), "W16": (16, B), "B8p": (8, B), "B8n": (8, B), "W8h": (8, B), "BB": (128, B),
+    "BBf": (128, F), "Sel0f": (128, F), "S8f": (8, F), "B8f": (8, F), "BW0": (128, B), "BW1": (128, B), "BD0": (128, F),
+    "BD1": (128, F), "BH": (2048, B), "IJ": (2048, B), "RST": (256, F), "RS01": (256, F), "WY": (16, F),
+    "XA": (2048, B), "XB": (2048, B), "HI": (2048, B), "LO": (2048, B), "MARK": (2048, B),
+    "zx0": (4096, B), "zx1": (4096, B), "df": (4096, B), "ab": (4096, B), "c16": (256, U), "cf": (256, F), "H": (256, B),
+    "mk": (256, B), "R": (512, F), "wi": (32, I), "wa": (32, I), "wb": (32, B), "wT": (128, B), "mj": (256, F),
+    "sc": (256, F), "vlA": (16, U), "v1o0": (16, U), "v2o0": (16, U), "v1o1": (16, U), "v2o1": (16, U), "xo0": (256, B),
+    "xo1": (256, B), "vlB": (16, U),
+    "sh": (1024, B), "sl": (1024, B), "mh": (4096, B), "ml": (4096, B), "eh": (512, B), "en": (512, B), "Lb": (256, F),
+    "r1": (256, F), "r2": (256, F), "v2n": (256, F), "KL": (256, F), "Ln": (256, F), "ab2": (256, B), "hf": (256, I),
+    "hb": (256, B), "like": (256, B), "tl": (256, B), "w": (256, B), "fk": (256, F), "fk2": (256, F), "R2": (256, F),
+    "qs": (160, F), "qi": (64, I), "kT": (128, F), "ui": (32, I), "ul": (16, U), "cutE": (256, B), "oh": (256, F),
+    "ce": (256, F), "ce2": (256, F), "smk": (256, F), "e2": (256, F), "KL2": (256, F), "OH": (4096, B),
+    "m0": (128, B), "m1": (128, B), "mi": (64, I), "mf": (64, F), "dl": (256, F), "dm": (256, F), "mlf": (128, F),
+    "Lo0": (256, U), "zo1": (256, B), "Lo1": (256, U), "zo2": (256, B), "Lo2": (256, U), "vo2": (16, F),
+    "zB": (256, B), "LB": (256, U), "v1i0": (16, U), "v2i0": (16, U), "xi0": (256, B), "zC": (256, B), "LC": (256, U),
+    "v1i1": (16, U), "v2i1": (16, U), "xi1": (256, B), "zF": (256, B), "LF": (256, U), "vF": (16, F),
+    "yzs": (256, F), "yls": (256, F), "yvs": (128, F), "yas": (128, F), "ya1": (128, F), "ya2": (128, F), "ya3": (128, F),
+    "ya4": (128, F), "ya5": (128, F),
+}
+PS = {"K0": 512, "K1": 512, "G": 512, "N0": 512, "N1": 512, "N2": 512, "Q0": 512, "Q1": 512}
+SCRATCH = {}
+PLACE = {}
+_use = {F: 0, B: 0, I: 0, U: 0}
+for _n, (_w, _d) in SB.items():
+    if _w > 600:
+        SCRATCH[_n] = ("sbuf", [128, _w], _d)
+        PLACE[_n] = (_n, 0)
+    else:
+        PLACE[_n] = ("all_" + _d, _use[_d])
+        _use[_d] += -(-_w // 32) * 32
+for _d in _use:
+    SCRATCH["all_" + _d] = ("sbuf", [128, _use[_d]], _d)
+for _n, _w in PS.items():
+    SCRATCH[_n] = ("psum", [128, _w], "float32")
+SEMAPHORES = ["cV", "cS", "cT", "cG"] + ["d%d" % i for i in range(30)] + ["a%d" % i for i in range(16)] + ["l%d" % i for i in range(16)]
+
+
+def rank_program(g, core, T, topo):
+    rank = T.rank_of(core)
+    if rank is None:
+        return
+    nR = len(T.cores)
+    HOP = 3
+    SHARE = 32
+    TH, TAU = 1020, (1020, 1530)
+    nxt, home = T.cores[(rank + HOP) % nR], T.cores[(rank - 2 * HOP) % nR]
+
+    QS = {"V": g.vector, "S": g.scalar, "T": g.tensor, "G": g, "Y": g.sync}
+    SEMQ = {"V": "cV", "S": "cS", "T": "cT", "G": "cG"}
+    count = {}
+    known = {q: {} for q in QS}
+    toks = []
+    hist = {}
+
+    def track(name):
+        if name not in hist:
+            hist[name] = {"w": np.full(SB[name][0] if name in SB else 1, -1), "r": {}}
+        return hist[name]
+
+    def cols(r):
+        return slice(0, 1) if r[0] in PS else slice(r[1], r[2], r[3])
+
+    def need(q, reads, writes):
+        ids = set()
+        for r in reads + writes:
+            h = track(r[0])
+            ps = r[0] in PS
+            new = set(int(i) for i in np.unique(h["w"][cols(r)]))
+            if ps or r in writes:
+                for k, arr in h["r"].items():
+                    if not (ps and k == q and r not in writes):
+                        new.update(int(i) for i in np.unique(arr[cols(r)]))
+            if ps and q == "T":
+                new = {i for i in new if i < 0 or toks[i][3] != "T"}
+            ids |= new
+        ids.discard(-1)
+        kn = known[q]
+        want = {}
+        for i in ids:
+            s, v = toks[i][0], toks[i][1]
+            if s[0] == "d":
+                v = count[s]
+            if kn.get(s, 0) < v:
+                want[s] = max(want.get(s, 0), v)
+        for s in list(want):
+            for i in ids:
+                s2 = toks[i][0]
+                if s2 != s and s2 in want and toks[i][2].get(s, 0) >= want[s] and toks[i][1] <= want[s2]:
+                    want.pop(s, None)
+                    break
+        for s, v in want.items():
+            QS[q].wait_ge(T.sem[s], v)
+            kn[s] = max(kn.get(s, 0), v)
+        for i in ids:
+            for s, v in toks[i][2].items():
+                kn[s] = max(kn.get(s, 0), v)
+            if toks[i][0][0] != "d":
+                kn[toks[i][0]] = max(kn.get(toks[i][0], 0), toks[i][1])
+
+    def done(q, sem, inc, reads, writes, snap=None):
+        count[sem] = count.get(sem, 0) + inc
+        toks.append((sem, count[sem], dict(known[q]) if snap is None else snap, q))
+        t = len(toks) - 1
+        for r in writes:
+            track(r[0])["w"][cols(r)] = t
+        for r in reads:
+            h = track(r[0])
+            key = q if sem in SEMQ.values() else sem
+            if key not in h["r"]:
+                h["r"][key] = np.full(len(h["w"]), -1)
+            h["r"][key][cols(r)] = t
+
+    def R(name, a=0, b=None, st=1, p=None):
+        if b is None:
+            b = SB[name][0] if name in SB else PS[name]
+        return (name, a, b, st, p)
+
+    def IND(win, off):
+        return ("ind", win, off)
+
+    def ap(r):
+        if r[0] == "ind":
+            return ap(r[1]).indirect(ap(r[2]))
+        n, a, b, st, p = r
+        if n in PLACE:
+            n, at = PLACE[n]
+            a, b = a + at, b + at
+        c = slice(a, b) if st == 1 else slice(a, b, st)
+        return T[n][:, c] if p is None else T[n][0:p, c]
+
+    def flat(rs):
+        out = []
+        for r in rs:
+            if isinstance(r, tuple):
+                if r[0] == "ind":
+                    out += [r[1], r[2]]
+                else:
+                    out.append(r)
+        return out
+
+    def val(s):
+        return ap(s) if isinstance(s, tuple) else s
+
+    def do(q, reads, writes, fn):
+        reads, writes = flat(reads), flat(writes)
+        need(q, reads, writes)
+        fn().then_inc(T.sem[SEMQ[q]], 1)
+        done(q, SEMQ[q], 1, reads, writes)
+
+    def tt(out, a, b, op):
+        do("V", [a, b], [out], lambda: g.vector.tensor_tensor(ap(out), ap(a), ap(b), op))
+
+    def ts(out, a, s1, op0, s2=None, op1=None):
+        if op1 is None:
+            do("V", [a, s1], [out], lambda: g.vector.tensor_scalar(ap(out), ap(a), val(s1), None, op0))
+        else:
+            do("V", [a, s1, s2], [out], lambda: g.vector.tensor_scalar(ap(out), ap(a), val(s1), val(s2), op0, op1))
+
+    def cp(out, a):
+        do("V", [a], [out], lambda: g.vector.tensor_copy(ap(out), ap(a)))
+
+    def scan(out, d0, d1, init, op0, op1):
+        do("V", [d0, d1], [out], lambda: g.vector.tensor_tensor_scan(ap(out), ap(d0), ap(d1), init, op0, op1))
+
+    def act(out, a, f, bias=None, scale=None):
+        def fn():
+            if bias is None and scale is None:
+                return g.scalar.activation(ap(out), ap(a), f)
+            if bias is None:
+                return g.scalar.activation(ap(out), ap(a), f, scale=val(scale))
+            return g.scalar.activation(ap(out), ap(a), f, bias=val(bias), scale=val(scale))
+        do("S", [a, bias, scale], [out], fn)
+
+    def mm(out, l, r, start=True, stop=True):
+        do("T", [l, r], [out], lambda: g.tensor.matmul(ap(out), ap(l), ap(r), start, stop))
+
+    def iota(out, pat, base, cm):
+        if SB[out[0]][1] != I:
+            do("G", [], [out], lambda: g.iota(ap(out), pat, base, cm, allow_small_or_imprecise_dtypes=True))
+        else:
+            do("G", [], [out], lambda: g.iota(ap(out), pat, base, cm))
+
+    nd, nm = [0], [0]
+
+    def newsem():
+        nd[0] += 1
+        return "d%d" % (nd[0] - 1)
+
+    def dma(q, out, in_, reads, writes, sem=None):
+        sem = sem or newsem()
+        need(q, reads, writes)
+        QS[q].dma_start(out, in_).then_inc(T.sem[sem], 16)
+        done(q, sem, 16, reads, writes)
+        return sem
+
+    def send(src, dst, to):
+        k = nm[0]
+        nm[0] += 1
+        engs = topo.engines(core, to)[:8]
+        rid, pid, _s = topo.addr(to)
+        need("G", [src], [])
+        g.remote_dma(out_ap=ap(dst), in_ap=ap(src), remote_sem=T.sem["a%d" % k], local_sem=T.sem["l%d" % k], pid=pid,
+                     routing_id=rid, dma_engine_mask=sum(1 << e for e in engs))
+        done("G", "l%d" % k, len(engs), [src], [])
+        done("G", "a%d" % k, len(engs), [], [dst], {})
+
+    def C(i):
+        return R("col", i, i + 1)
+
+    SH, AN = OP.arith_shift_right, OP.bitwise_and
+    EQ, MU, AD, SU, MX, MN, LE, GT, LT = OP.is_equal, OP.mult, OP.add, OP.subtract, OP.max, OP.min, OP.is_le, OP.is_gt, OP.is_lt
+
+    def expand(zx, z, pieces):
+        w = 256 // pieces
+        for c in range(pieces):
+            act(R(zx, 16 * w * c, 16 * w * c + 16 * w), IND(R(z), R("zl", w * c, w * c + w)), AF.Copy)
+
+    dma("Y", ap(R("vA")), T.v0[:], [], [R("vA")])
+    dma("S", ap(R("zA")), T.z0[:], [], [R("zA")])
+    dma("Y", ap(R("eS")), T.E[:], [], [R("eS")])
+    dma("Y", ap(R("xS")), T.X[:], [], [R("xS")])
+    for k in range(3):
+        s = newsem()
+        for gg in range(8):
+            c = R("t%d" % k, 16 * gg, 16 * gg + 16)
+            dma("Y", ap(c), T.E[16 * gg + k, :], [], [c], s)
+    dma("Y", ap(R("LA")), T.L0[:], [], [R("LA")])
+    dma("Y", ap(R("e0r")), T.E[0::16, :], [], [R("e0r")])
+    dma("Y", ap(R("e1r")), T.E[1::16, :], [], [R("e1r")])
+
+    iota(R("iC", 0, 1), [[0, 1]], 0, 1)
+    iota(R("iN"), [[1, 256]], 0, 0)
+    iota(R("iD"), [[1, 256]], 128, -1)
+    iota(R("mg"), [[1, 8], [0, 16]], 0, 0)
+    iota(R("gp"), [[0, 2], [1, 8]], 0, 0)
+    iota(R("kk"), [[0, 16], [1, 16]], 0, 0)
+    iota(R("ck"), [[144, 2], [0, 8], [256, 16]], 0, 0)
+    cp(R("zl"), R("iN"))
+    expand("zx0", "zA", 4)
+    send(R("zA"), R("zB"), nxt)
+    iota(R("io128"), [[1, 128]], 0, 0)
+    iota(R("g16"), [[0, 2], [16, 8]], 0, 0)
+    iota(R("io16"), [[1, 16]], 0, 0)
+    iota(R("io2k"), [[1, 2048]], 0, 0)
+    ts(R("iC", 1, 2), R("iC", 0, 1), 4, SH)
+    ts(R("iC", 2, 3), R("iC", 0, 1), 15, AN)
+    ts(R("iC", 3, 4), R("iC", 0, 1), 7, AN)
+    ts(R("iC", 4, 5), R("iC", 0, 1), 3, SH, 1, AN)
+    ts(R("iC", 5, 6), R("iC", 0, 1), 3, SH)
+    cp(R("col", 1, 6), R("iC", 1, 6))
+    PG, PK, P7, KY, P8 = C(1), C(2), C(3), C(4), C(5)
+    ts(C(6), PK, 2.0, MU, 1.0, AD)
+    for k in range(4):
+        ts(C(8 + k), PK, float(k), EQ)
+    ts(C(7), C(8), 4096.0, MU)
+    ts(C(12), PK, 2048.0, MU)
+    ts(C(13), PK, 2.0, OP.is_ge)
+    tt(C(20), C(10), C(11), AD)
+    ts(C(14), C(20), -1.0, MU, 1.0, AD)
+    ts(C(15), PK, -2048.0, MU)
+    tt(C(16), C(9), C(8), SU)
+    ts(C(17), KY, -15.0, MU, 16.0, AD)
+    for h in range(2):
+        ts(C(18 + h), PG, float(h), EQ, C(17), MU)
+        ts(C(21 + h), P8, float(h), EQ)
+    ts(C(23), PK, 1.0, AD)
+    act(R("ones"), R("mg"), AF.Identity, 1.0, 0.0)
+    ts(R("If"), R("iD", 0, 128), 128.0, EQ)
+    ts(R("W16"), R("gp"), PG, EQ, 4096.0, MU)
+    ts(R("PHI", 0, 128), R("If"), 0.125, MU)
+    ts(R("PHI", 128, 256), R("If"), -2.0, MU)
+    ts(R("RS01"), R("kk"), 0.0, GT)
+    ts(R("RST"), R("RS01"), -67108864.0, MU, 33554432.0, AD)
+    cp(R("Ib"), R("If"))
+    ts(R("iA"), R("iD"), 15, AN)
+    ts(R("maskJ"), R("iA"), 0.0, EQ)
+    for h in range(2):
+        ts(R("BW%d" % h), R("mg"), P7, EQ, C(18 + h), MU)
+        ts(R("BD%d" % h), R("mg"), P7, EQ, C(21 + h), MU)
+    ts(R("BBf"), R("mg"), PG, EQ)
+    cp(R("BB"), R("BBf"))
+    ts(R("B8p"), R("gp", 0, 8), PG, EQ)
+    ts(R("B8n"), R("gp", 0, 8), PG, EQ, -1.0, MU)
+    ts(R("W8h"), R("gp", 0, 8), PG, EQ, C(6), MU)
+    ts(R("B8f"), R("gp", 0, 8), PG, EQ)
+    ts(R("S8f"), R("gp", 0, 8), PG, EQ, C(8), MU)
+    ts(R("nIb"), R("If"), -1.0, MU)
+    ts(R("nIf"), R("If"), -1.0, MU)
+    ts(R("Sel0f"), R("BBf"), C(8), MU)
+    ts(R("WY", 0, 8), R("gp", 0, 8), PG, EQ, C(23), MU)
+    ts(R("WY", 8, 16), R("gp", 0, 8), PG, EQ)
+    ts(R("jm"), R("io16"), PK, EQ)
+    for b in range(2):
+        ts(R("P16", 128 * b, 128 * b + 128), R("If"), C(7), MU)
+    cp(R("vlA"), R("vA"))
+
+    def lists(part):
+        if part == 0:
+            for k in range(3):
+                cp(R("tf", 128 * k, 128 * k + 128), R("t%d" % k))
+                mm(R("Q0", 128 * k, 128 * k + 128), R("tf", 128 * k, 128 * k + 128), R("If"))
+        else:
+            cp(R("elf"), R("Q0", 0, 384))
+            cp(R("el"), R("elf", 0, 256))
+
+    def selectors(part):
+        for j in range(16):
+            c = (128 * j, 128 * j + 128)
+            if part == 0:
+                ts(R("IJ", *c), R("Ib"), R("jm", j, j + 1), MU)
+            else:
+                act(R("BH", *c), R("BB"), AF.Copy, None, R("jm", j, j + 1))
+
+    def tables(el, piece):
+        h, k = piece % 2, piece // 2
+        act(R("XB" if k else "XA", 1024 * h, 1024 * h + 1024), IND(R("xS"), R(el, 128 * k + 64 * h, 128 * k + 64 * h + 64)), AF.Copy)
+
+    def hilo(h):
+        a = (1024 * h, 1024 * h + 1024)
+        tt(R("HI", *a), R("XA", *a), R("XB", *a), MX)
+        tt(R("LO", *a), R("XA", *a), R("XB", *a), MN)
+
+    def yasum(part):
+        if part == 0:
+            for hi in range(16):
+                mm(R("Q1", hi, 256, 16), R("ef", 128 * hi, 128 * hi + 128), R("WY"))
+        else:
+            for b in range(2):
+                mm(R("Q1", 128 * b, 128 * b + 128), R("ys", 128 * b, 128 * b + 128), R("If"))
+        act(R("s01" if part else "ys"), R("Q1", 0, 256), AF.Copy)
+
+    def tolist(bank, out, add, low=False):
+        tt(R("mj"), R(bank, 0, 256), R("maskJ"), MU)
+        scan(R("sc"), R("RS01"), R("mj"), 0.0, MU, AD)
+        if low:
+            cp(R("ui", 0, 16), R("sc", 15, 256, 16))
+            ts(R("ui", 16, 32), R("ui", 0, 16), 2047, AN)
+            cp(R(out), R("ui", 16, 32))
+        else:
+            ts(R(out), R("sc", 15, 256, 16), add, AD)
+
+    def walk(vl, zx, out, marked, sfill, vfill):
+        cp(R("c16"), IND(R("eS"), R(vl)))
+        if vl == "vlA":
+            cp(R("ef"), R("eS"))
+        act(R("cf"), IND(R("ef"), R(vl)), AF.Copy)
+        act(R("H"), R("cf"), AF.Identity, 1024.0, 0.5)
+        if marked:
+            act(R("mk"), IND(R("MARK"), R(vl)), AF.Copy)
+        for ch in range(4):
+            a = (1024 * ch, 1024 * ch + 1024)
+            tt(R("df", *a), IND(R("xS"), R("c16", 64 * ch, 64 * ch + 64)), R(zx, *a), SU)
+            act(R("ab", *a), R("df", *a), AF.Abs)
+            sfill(ch)
+            if ch % 2 == 1:
+                h = ch // 2
+                kb = "K%d" % h
+                n = (128 * h, 128 * h + 128)
+                mm(R(kb, 0, 256), R("ones", 0, 128, 1, 1), R("ck", 0, 256, 1, 1), True, False)
+                mm(R(kb, 0, 256), R("H", *n), R("PHI"), False, False)
+                mm(R(kb, 128, 256), R("cf", *n), R("If"), False, False)
+                if marked:
+                    mm(R(kb, 0, 256), R("mk", *n), R("P16"), False, False)
+                for k in range(16):
+                    mm(R(kb, k, 256, 16), R("ab", 2048 * h + k, 2048 * h + 2048, 16), R("W16"), False, k == 15)
+        vfill()
+        for h in range(2):
+            scan(R("R", 256 * h, 256 * h + 256), R("RST"), R("K%d" % h, 0, 256), 0.0, MX, MN)
+        ts(R("wi"), R("R", 15, 512, 16), -128.0, AD)
+        ts(R("wa"), R("wi"), 255, AN)
+        cp(R("wb"), R("wa"))
+        mm(R("Q0", 0, 128, 1, 32), R("wb"), R("Ib"))
+        cp(R("wT", 0, 128, 1, 32), R("Q0", 0, 128, 1, 32))
+        for h in range(2):
+            mm(R("N0", 128 * h, 128 * h + 128), R("BW%d" % h, 0, 128, 1, 32), R("wT", 0, 128, 1, 32))
+        tolist("N0", out, -16.0)
+
+    def gapS(L16, zx):
+        e0 = 4096 - 16 * SHARE
+        for tab, sb in (("HI", "sh"), ("LO", "sl")):
+            act(R(sb, 0, 16 * SHARE), IND(R(tab), R(L16, 256 - SHARE, 256)), AF.Copy)
+        i = 0
+        for sb, dst in (("sh", "mh"), ("sl", "ml")):
+            for c in range(0, 16 * SHARE, 512):
+                kb = "K%d" % (i % 2)
+                i += 1
+                w = min(512, 16 * SHARE - c)
+                mm(R(kb, 0, w), R("Ib"), R(sb, c, c + w), True, False)
+                mm(R(kb, 0, w), R("nIb"), R(zx, e0 + c, e0 + c + w), False, True)
+                act(R(dst, e0 + c, e0 + c + w), R(kb, 0, w), AF.Relu)
+
+    def gap(t, L16, zx, h):
+        for c in range(2):
+            n0, n1 = 128 * h + 64 * c, min(128 * h + 64 * c + 64, 256 - SHARE)
+            if n0 < n1:
+                a = (16 * n0, 16 * n1)
+                tt(R("mh", *a), IND(R("HI"), R(L16, n0, n1)), R(zx, *a), MX)
+                tt(R("ml", *a), IND(R("LO"), R(L16, n0, n1)), R(zx, *a), MX)
+        for k in range(16):
+            if k // 2 != t:
+                o = R("G", 128 * h + k, 128 * h + 128, 16)
+                mm(o, R("mh", 2048 * h + k, 2048 * h + 2048, 16), R("B8p"), True, False)
+                mm(o, R("ml", 2048 * h + k, 2048 * h + 2048, 16), R("B8n"), False, True)
+
+    def Q(i):
+        return R("qs", 16 * i, 16 * i + 16)
+
+    def prep(t, z, v1, v2, xi):
+        act(R("r1"), IND(R("io2k"), R(v1)), AF.Copy, None, C(8 + 2 * t))
+        act(R("v2n"), IND(R("io2k"), R(v2)), AF.Copy)
+        act(R("r2"), R("v2n"), AF.Copy, None, C(9 + 2 * t))
+        mm(R("Q0", 0, 256), R("If"), R("Lb"), True, False)
+        mm(R("Q0", 0, 256), R("If"), R("r1"), False, False)
+        mm(R("Q0", 0, 256), R("If"), R("r2"), False, True)
+        act(R("KL"), R("Q0", 0, 256), AF.Copy)
+        act(R("Ln"), R("Q0", 0, 256), AF.Identity, C(15), 1.0)
+        mm(R("N1", 0, 256), R("Ib"), R(xi), True, False)
+        mm(R("N1", 0, 256), R("nIb"), R(z), False, True)
+        mm(R("N2", 0, 256), R("Ib"), R(xi), True, False)
+        mm(R("N2", 0, 256), R("Ib"), R(z), False, True)
+
+    def entries(t, z, v1, v2):
+        for e, vl in enumerate((v1, v2)):
+            a = (256 * e, 256 * e + 256)
+            tt(R("eh", *a), IND(R("HI"), R(vl)), R(z), MX)
+            tt(R("en", *a), IND(R("LO"), R(vl)), R(z), MX)
+            for h in range(2):
+                n = (256 * e + 128 * h, 256 * e + 128 * h + 128)
+                o = R("G", 128 * h + 2 * t + e, 128 * h + 128, 16)
+                mm(o, R("eh", *n), R("B8p"), True, False)
+                mm(o, R("en", *n), R("B8n"), False, True)
+
+    def prep2():
+        act(R("ab2"), R("N1", 0, 256), AF.Abs)
+        ts(R("hf"), R("N2", 0, 256), 0.5, MU, -0.25, AD)
+        cp(R("hb"), R("hf"))
+        for h in range(2):
+            n = (128 * h, 128 * h + 128)
+            mm(R("Q1", 8 * h, 8 * h + 8), R("ab2", *n), R("B8p"))
+            mm(R("Q1", 16 + 8 * h, 24 + 8 * h), R("hb", *n), R("W8h"))
+            mm(R("Q1", 32 + 8 * h, 40 + 8 * h), R("v2n", *n), R("S8f"))
+        mm(R("N1", 0, 256), R("BB"), R("ab2"))
+        mm(R("N2", 0, 256), R("Ib"), R("ab2"), True, False)
+        mm(R("N2", 0, 256), R("nIb"), R("hb"), False, True)
+        for h in range(2):
+            mm(R("K0", 128 * h, 128 * h + 128), R("KL", 128 * h, 128 * h + 128), R("If"))
+
+    def prep3(z):
+        act(Q(0), R("Q1", 0, 16), AF.Relu, 32768.0 * (TH + 1), -32768.0)
+        act(Q(2), Q(0), AF.Sign)
+        cp(R("qi", 0, 16), R("Q1", 16, 32))
+        ts(R("qi", 16, 32), R("qi", 0, 16), 2047, AN)
+        tt(Q(3), R("Q1", 32, 48), R("qi", 16, 32), SU)
+        tt(Q(4), Q(3), Q(2), MU)
+        tt(Q(5), Q(4), R("qi", 16, 32), AD)
+        ts(R("like"), R("N1", 0, 256), float(TH), LE)
+        mm(R("N1", 0, 256), R("nIf"), R("Ln"), True, False)
+        tt(R("tl"), R("N2", 0, 256), R("like"), MU)
+        mm(R("N2", 0, 256), R("Ib"), R(z), True, False)
+        mm(R("N2", 0, 256), R("nIb"), R("hb"), False, False)
+        mm(R("N2", 0, 256), R("nIb"), R("tl"), False, True)
+
+    def onehots(c0, c1):
+        for c in range(c0, c1):
+            ts(R("OH", 256 * c, 256 * c + 128), R("io128"), R("mf", c, c + 1), EQ)
+            ts(R("OH", 256 * c + 128, 256 * c + 256), R("io128"), R("mf", 16 + c, 17 + c), EQ)
+
+    def counts(bank):
+        for c in range(16):
+            mm(R(bank, 0, 128), R("OH", 256 * c, 256 * c + 128), R("OH", 256 * c + 128, 256 * c + 256), c == 0, c == 15)
+
+    def spread(bank):
+        cp(R("kT", 0, 128, 1, 16), R("Q0", 0, 128, 1, 16))
+        for h in range(2):
+            mm(R(bank, 128 * h, 128 * h + 128), R("BD%d" % h, 0, 128, 1, 16), R("kT", 0, 128, 1, 16))
+
+    def newlog(Lo):
+        tt(R("e2"), R("N1", 0, 256), R("oh"), MU)
+        tt(R("KL2"), R("Ln"), R("e2"), AD)
+        cp(R(Lo), R("KL2"))
+
+    def decide(t, zo):
+        ts(R("fk"), R("G", 0, 256), float(TAU[t]), LE, 32768.0, MU)
+        tt(R("fk2"), R("K0", 0, 256), R("fk"), AD)
+        scan(R("R2"), R("RST"), R("fk2"), 0.0, MX, MN)
+        tt(Q(6), R("R2", 15, 256, 16), Q(0), MX)
+        mm(R("Q0", 0, 128, 1, 16), Q(6), R("If"))
+        cp(R("mi", 0, 16), Q(6))
+        ts(R("mi", 16, 32), R("mi", 0, 16), 7, SH, 15, AN)
+        ts(R("mi", 32, 48), R("mi", 0, 16), 127, AN)
+        ts(Q(7), Q(6), 32768.0, LT)
+        spread("N0")
+        ts(Q(8), Q(7), -1000.0, MU, 1000.0, AD)
+        tt(Q(9), R("mi", 16, 32), R("g16"), AD)
+        tt(R("mf", 0, 16), Q(9), Q(8), AD)
+        cp(R("mf", 16, 32), R("mi", 32, 48))
+        onehots(0, 5 if t == 0 else 2)
+        tolist("N0", "ul", 0.0, True)
+        if t == 1:
+            act(R("smk"), IND(R("MARK"), R("ul")), AF.Identity, C(8), C(16))
+            cp(R("ce"), IND(R("eS"), R("ul")))
+            ts(R("cutE"), R("N0", 0, 256), 32768.0, LT)
+            tt(R("ce2"), R("ce"), R("smk"), MU)
+            mm(R("N1", 0, 256), R("BBf"), R("ce2"), False, True)
+        else:
+            act(R("ce"), IND(R("ef"), R("ul")), AF.Copy)
+            ts(R("cutE"), R("N0", 0, 256), 32768.0, LT)
+        for h in range(2):
+            n = (128 * h, 128 * h + 128)
+            mm(R("Q1", 48 + 8 * h, 56 + 8 * h), R("ce2" if t else "ce", *n), R("B8f" if t else "S8f"))
+        tt(R("w"), R("N2", 0, 256), R("cutE"), MU)
+        tt(R("oh"), R("N0", 0, 256), R("KL"), EQ)
+        if t == 0:
+            onehots(5, 8)
+        mm(R("N2", 0, 256), R("Ib"), R("hb"), True, False)
+        mm(R("N2", 0, 256), R("Ib"), R("tl"), False, False)
+        mm(R("N2", 0, 256), R("Ib"), R("w"), False, True)
+        act(R(zo), R("N2", 0, 256), AF.Copy)
+        if t == 1:
+            newlog("Lo2")
+        tt(Q(3), R("Q1", 48, 64), Q(5), SU)
+        tt(Q(4), Q(3), Q(7), MU)
+        tt(R("vo2"), Q(4), Q(5), AD)
+
+    def turn0():
+        ts(R("m0"), R("Q1", 0, 128), 0.0, GT)
+        for b in range(4):
+            bank = ("G", "N2")[b % 2]
+            for j in range(4):
+                hi = 4 * b + j
+                mm(R(bank, 128 * j, 128 * j + 128), R("BH", 128 * hi, 128 * hi + 128), R("m0"))
+            act(R("MARK", 512 * b, 512 * b + 512), R(bank), AF.Copy)
+        for j in range(16):
+            mm(R("Q1", 0, 128), R("IJ", 128 * j, 128 * j + 128), R("MARK", j, 2048, 16), j == 0, j == 15)
+
+    def turn1():
+        tt(R("dl"), R("elf", 128, 384), R("elf", 0, 256), SU)
+        cp(R("mlf"), R("Q1", 0, 128))
+        for k in range(2):
+            a = (128 * k, 128 * k + 128)
+            tt(R("dm", *a), R("dl", *a), R("mlf"), MU)
+        tt(R("el2"), R("dm"), R("elf", 0, 256), AD)
+
+    def visit(t, vl, v1, v2, xo, lst, z, L16, ini):
+        def s0(ch):
+            if t == 0 and ch == 0:
+                yasum(0)
+            if t == 0 and ch == 1:
+                lists(0)
+            if t == 0 and ch == 3:
+                yasum(1)
+
+        def f0():
+            if t == 0:
+                lists(1)
+                selectors(0)
+                cp(R("Lo0"), R("LA"))
+                send(R("Lo0"), R("LB"), nxt)
+            else:
+                turn1()
+                newlog("Lo1")
+                send(R("Lo1"), R("LC"), nxt)
+            tables(lst, 0)
+            tables(lst, 2)
+
+        def s1(ch):
+            if ch == 0:
+                tables(lst, 1)
+            if ch == 1:
+                tables(lst, 3)
+            if ch == 3:
+                expand("zx1", z, 4)
+
+        def f1():
+            hilo(0)
+            hilo(1)
+            ts(R("Lb"), R(L16), C(13 + t), MU, C(12), AD)
+
+        walk(vl, "zx0", v1, t == 1, s0, f0)
+        send(R(v1), R(ini[0]), nxt)
+        walk(v1, "zx0", v2, t == 1, s1, f1)
+        send(R(v2), R(ini[1]), nxt)
+        act(R(xo), IND(R("xS"), R(v2)), AF.Copy)
+        send(R(xo), R(ini[2]), nxt)
+        gapS(L16, "zx1")
+        gap(t, L16, "zx1", 0)
+        prep(t, z, *ini)
+        gap(t, L16, "zx1", 1)
+        prep2()
+        entries(t, z, ini[0], ini[1])
+        prep3(z)
+        if t == 0:
+            selectors(1)
+
+    visit(0, "vlA", "v1o0", "v2o0", "xo0", "el", "zB", "LB", ("v1i0", "v2i0", "xi0"))
+    decide(0, "zo1")
+    mm(R("Q0", 0, 128, 1, 16), R("vo2"), R("If"))
+    spread("K1")
+    mm(R("N1", 0, 256), R("Sel0f"), R("ce"), False, True)
+    send(R("zo1"), R("zC"), nxt)
+    expand("zx0", "zo1", 4)
+    tolist("K1", "vlB", 0.0)
+    onehots(8, 16)
+    counts("Q1")
+    turn0()
+
+    visit(1, "vlB", "v1o1", "v2o1", "xo1", "el2", "zC", "LC", ("v1i1", "v2i1", "xi1"))
+    decide(1, "zo2")
+    send(R("zo2"), R("zF"), home)
+    send(R("Lo2"), R("LF"), home)
+    send(R("vo2"), R("vF"), home)
+    onehots(2, 16)
+    counts("K0")
+    for k in range(2):
+        ts(R("ya1"), R("e%dr" % k), 16.0, MU)
+        tt(R("dy%d" % k), R("ya1"), R("s01", 128, 256), SU)
+    ts(R("m1"), R("K0", 0, 128), 0.0, GT)
+    tt(R("ya2"), R("m0"), R("m1"), MX)
+    tt(R("ya3"), R("m0"), R("m1"), MU)
+    tt(R("ya4"), R("ya2"), R("dy0"), MU)
+    tt(R("ya5"), R("ya3"), R("dy1"), MU)
+    tt(R("ya1"), R("ya4"), R("ya5"), AD)
+    tt(R("yas"), R("ya1"), R("s01", 0, 128), AD)
+    dma("Y", T.ya[:], ap(R("yas")), [R("yas")], [])
+    act(R("yzs"), R("zF"), AF.Copy)
+    dma("S", T.yz[:], ap(R("yzs")), [R("yzs")], [])
+    cp(R("yls"), R("LF"))
+    dma("Y", T.yl[:], ap(R("yls")), [R("yls")], [])
+    mm(R("Q0", 0, 128, 1, 16), R("vF"), R("If"))
+    cp(R("yvs", 0, 128, 1, 16), R("Q0", 0, 128, 1, 16))
+    nv, at = PLACE["yvs"]
+    s = dma("Y", T.yv[:, 0:128], T[nv][0:8, at:at + 128], [R("yvs")], [])
+    dma("Y", T.yv[:, 128:256], T[nv][8:16, at:at + 128], [R("yvs")], [], s)
+    for s, v in count.items():
+        if known["G"].get(s, 0) < v:
+            g.wait_ge(T.sem[s], v)

@@ -1,38 +1,35 @@
 import numpy as np
-from concourse.mybir import AluOpType as OP, AxisListType, ActivationFunctionType as AF
+from concourse.mybir import AluOpType as OP, ActivationFunctionType as AF
 
-F, B, I, U = "float32", "bfloat16", "int32", "uint16"
+F, B, I, U, H = "float32", "bfloat16", "int32", "uint16", "float16"
 SB = {
-    "eS": (2048, I), "xS": (2048, B), "zA": (256, B), "LA": (256, I), "vA": (16, I), "ef": (2048, F),
-    "t0": (128, I), "t1": (128, I), "t2": (128, I), "tf": (384, F), "elf": (384, F), "el": (256, U), "el2": (256, U),
-    "e0r": (128, I), "e1r": (128, I), "ys": (256, F), "s01": (256, F), "dy0": (128, F), "dy1": (128, F),
-    "iD": (256, I), "iA": (256, I), "iC": (8, I), "iN": (256, I), "zl": (256, U), "col": (32, F), "mg": (128, F),
-    "kk": (256, F), "io128": (128, B), "io16": (16, F), "jm": (16, F), "g16": (16, F), "gp": (16, F), "io2k": (2048, F),
-    "ck": (256, B), "ones": (128, B), "maskJ": (256, F), "Ib": (128, B), "nIb": (128, B), "If": (128, F), "nIf": (128, F),
-    "PHI": (256, B), "P16": (256, B), "W16": (16, B), "B8p": (8, B), "B8n": (8, B), "W8h": (8, B), "BB": (128, B),
-    "BBf": (128, F), "Sel0f": (128, F), "S8f": (8, F), "B8f": (8, F), "BW0": (128, B), "BW1": (128, B), "BD0": (128, F),
-    "BD1": (128, F), "BH": (2048, B), "IJ": (2048, B), "RST": (256, F), "RS01": (256, F), "WY": (16, F),
-    "XA": (2048, B), "XB": (2048, B), "HI": (2048, B), "LO": (2048, B), "MARK": (2048, B),
-    "zx0": (4096, B), "zx1": (4096, B), "df": (4096, B), "ab": (4096, B), "c16": (256, U), "cf": (256, F), "H": (256, B),
-    "mk": (256, B), "R": (512, F), "wi": (32, I), "wa": (32, I), "wb": (32, B), "wT": (128, B), "mj": (256, F),
-    "sc": (256, F), "vlA": (16, U), "v1o0": (16, U), "v2o0": (16, U), "v1o1": (16, U), "v2o1": (16, U), "xo0": (256, B),
-    "xo1": (256, B), "vlB": (16, U),
-    "sh": (1024, B), "sl": (1024, B), "mh": (4096, B), "ml": (4096, B), "eh": (512, B), "en": (512, B), "Lb": (256, F),
-    "r1": (256, F), "r2": (256, F), "v2n": (256, F), "KL": (256, F), "Ln": (256, F), "ab2": (256, B), "hf": (256, I),
-    "hb": (256, B), "like": (256, B), "tl": (256, B), "w": (256, B), "fk": (256, F), "fk2": (256, F), "R2": (256, F),
-    "qs": (160, F), "qi": (64, I), "kT": (128, F), "ui": (32, I), "ul": (16, U), "cutE": (256, B), "oh": (256, F),
-    "ce": (256, F), "ce2": (256, F), "smk": (256, F), "e2": (256, F), "KL2": (256, F), "OH": (4096, B),
-    "m0": (128, B), "m1": (128, B), "mi": (64, I), "mf": (64, F), "dl": (256, F), "dm": (256, F), "mlf": (128, F),
-    "Lo0": (256, U), "zo1": (256, B), "Lo1": (256, U), "zo2": (256, B), "Lo2": (256, U), "vo2": (16, F),
+    "I16": (128, H), "B8h": (8, H), "gm32": (256, F), "zw": (4096, B), "sh": (4096, B), "so": (4096, B), "zT2": (256, B),
+    "eS": (2048, I), "xS": (2048, B), "zA": (256, B), "LA": (256, I), "vA": (16, I), "ef": (2176, F),
+    "t0": (128, I), "t1": (128, I), "tf": (256, H), "el": (256, U), "ys": (384, F),
+    "iC": (8, I), "iN": (32, I), "zl": (32, U), "col": (48, F), "iD": (128, B), "gp": (16, B), "kk": (256, B), "ck": (256, B),
+    "KLc": (128, B), "io": (144, B), "g16": (8, B), "mg": (128, B), "e32": (512, B), "EXP": (512, B), "io2k": (2176, F),
+    "ones": (128, B), "cq": (256, B), "c175": (256, B), "wrow": (256, F), "maskJ": (256, B), "IM": (768, B), "If": (128, F),
+    "RST": (256, B), "RSD": (128, F), "W16": (16, B), "B8": (16, B), "W8": (16, B), "B8f": (16, F), "BB4": (128, B),
+    "SelC": (32, F), "WY": (24, F), "Z2": (144, B),
+    "XB": (2048, B), "HI": (2176, B), "LO": (2176, B), "m0": (128, B), "Sb": (128, B), "m1": (128, B),
+    "zT": (256, B), "xg": (4096, B), "ab": (4096, B), "c16": (256, U), "cf": (256, H), "H": (256, B), "ad": (256, B),
+    "mk": (256, B), "R": (512, F), "wi": (32, I), "wa": (32, I), "wb": (32, B), "wT": (512, B),
+    "vlA": (16, U), "v1o0": (16, U), "v2o0": (16, U), "v1o1": (16, U), "v2o1": (16, U), "vlB": (16, U), "loB": (16, U),
+    "lo1": (16, U), "vi": (32, I), "xo0": (256, B), "xo1": (256, B),
+    "zx0": (4096, B), "zx1": (4096, B), "mh": (4096, B), "ml": (4096, B), "eh": (512, B), "en": (512, B), "Lf": (256, H),
+    "r1": (256, F), "r2": (256, F), "ab2": (256, B), "hb": (256, B), "sl": (256, B), "tl": (256, B), "sc": (256, B),
+    "w": (256, B), "fk": (256, B), "R2": (256, F), "flag": (256, B), "e2": (256, H), "NP": (128, H), "ce": (256, F),
+    "qs": (256, F), "qi": (128, I), "qb": (96, B), "ul": (16, U), "ulo": (16, U), "OH": (4096, B), "gm": (768, H),
+    "adu": (256, B), "ad2": (256, B), "mn": (256, B), "e12": (32, U), "u2": (16, U), "nB": (256, B), "nH": (256, B),
+    "nL": (256, B), "Lo0": (256, U), "zo1": (256, B), "Lo1": (256, U), "fo0": (264, F), "fo1": (264, F),
     "zB": (256, B), "LB": (256, U), "v1i0": (16, U), "v2i0": (16, U), "xi0": (256, B), "zC": (256, B), "LC": (256, U),
-    "v1i1": (16, U), "v2i1": (16, U), "xi1": (256, B), "zF": (256, B), "LF": (256, U), "vF": (16, F),
-    "yzs": (256, F), "yls": (256, F), "yvs": (128, F), "yas": (128, F), "ya1": (128, F), "ya2": (128, F), "ya3": (128, F),
-    "ya4": (128, F), "ya5": (128, F),
+    "v1i1": (16, U), "v2i1": (16, U), "xi1": (256, B), "fi0": (264, F), "fi1": (264, F),
+    "yvs": (256, F), "ya1": (128, F), "ya2": (128, F), "yas": (128, F),
 }
-PS = {"K0": 512, "K1": 512, "G": 512, "N0": 512, "N1": 512, "N2": 512, "Q0": 512, "Q1": 512}
+PS = {"P0": 512, "P1": 512, "K0": 512, "K1": 512, "N0": 512, "N1": 512, "G": 512, "M": 512}
 SCRATCH = {}
 PLACE = {}
-_use = {F: 0, B: 0, I: 0, U: 0}
+_use = {F: 0, B: 0, I: 0, U: 0, H: 0}
 for _n, (_w, _d) in SB.items():
     if _w > 600:
         SCRATCH[_n] = ("sbuf", [128, _w], _d)
@@ -44,7 +41,9 @@ for _d in _use:
     SCRATCH["all_" + _d] = ("sbuf", [128, _use[_d]], _d)
 for _n, _w in PS.items():
     SCRATCH[_n] = ("psum", [128, _w], "float32")
-SEMAPHORES = ["cV", "cS", "cT", "cG"] + ["d%d" % i for i in range(30)] + ["a%d" % i for i in range(16)] + ["l%d" % i for i in range(16)]
+SEMAPHORES = ["cV", "cS", "cT", "cG"] + ["d%d" % i for i in range(30)] + ["a%d" % i for i in range(30)] + ["l%d" % i for i in range(30)]
+OPT = {"tch": 512, "look": 0.5, "ef": "G", "exp": ("SG", "GS"), "load": ("z1Lv", "X0E"),
+       "xg": "S", "sm": "SV", "expw": ("GS", "GS"), "B": "S", "vx": ((1, 1), (0, 0)), "gS": ((0, 0), (0, 1)), "short": 0.0}
 
 
 def rank_program(g, core, T, topo):
@@ -53,74 +52,40 @@ def rank_program(g, core, T, topo):
         return
     nR = len(T.cores)
     HOP = 3
-    SHARE = 32
     TH, TAU = 1020, (1020, 1530)
     nxt, home = T.cores[(rank + HOP) % nR], T.cores[(rank - 2 * HOP) % nR]
+    CY, GA, SCAT, WAKE = 0.83e-3, 1.56, 3.8, 0.06
 
     QS = {"V": g.vector, "S": g.scalar, "T": g.tensor, "G": g, "Y": g.sync}
-    SEMQ = {"V": "cV", "S": "cS", "T": "cT", "G": "cG"}
-    count = {}
-    known = {q: {} for q in QS}
-    toks = []
+    ops = []
     hist = {}
 
     def track(name):
         if name not in hist:
-            hist[name] = {"w": np.full(SB[name][0] if name in SB else 1, -1), "r": {}}
+            hist[name] = {"w": np.full(SB[name][0] if name in SB else PS[name], -1), "r": {}}
         return hist[name]
 
-    def cols(r):
-        return slice(0, 1) if r[0] in PS else slice(r[1], r[2], r[3])
-
-    def need(q, reads, writes):
-        ids = set()
+    def record(q, reads, writes, fn, cost, kind="op", lat=0.0, grp=None, after=(), sem=None, inc=1):
+        me = len(ops)
+        deps = set()
         for r in reads + writes:
-            h = track(r[0])
-            ps = r[0] in PS
-            new = set(int(i) for i in np.unique(h["w"][cols(r)]))
-            if ps or r in writes:
-                for k, arr in h["r"].items():
-                    if not (ps and k == q and r not in writes):
-                        new.update(int(i) for i in np.unique(arr[cols(r)]))
-            if ps and q == "T":
-                new = {i for i in new if i < 0 or toks[i][3] != "T"}
-            ids |= new
-        ids.discard(-1)
-        kn = known[q]
-        want = {}
-        for i in ids:
-            s, v = toks[i][0], toks[i][1]
-            if s[0] == "d":
-                v = count[s]
-            if kn.get(s, 0) < v:
-                want[s] = max(want.get(s, 0), v)
-        for s in list(want):
-            for i in ids:
-                s2 = toks[i][0]
-                if s2 != s and s2 in want and toks[i][2].get(s, 0) >= want[s] and toks[i][1] <= want[s2]:
-                    want.pop(s, None)
-                    break
-        for s, v in want.items():
-            QS[q].wait_ge(T.sem[s], v)
-            kn[s] = max(kn.get(s, 0), v)
-        for i in ids:
-            for s, v in toks[i][2].items():
-                kn[s] = max(kn.get(s, 0), v)
-            if toks[i][0][0] != "d":
-                kn[toks[i][0]] = max(kn.get(toks[i][0], 0), toks[i][1])
-
-    def done(q, sem, inc, reads, writes, snap=None):
-        count[sem] = count.get(sem, 0) + inc
-        toks.append((sem, count[sem], dict(known[q]) if snap is None else snap, q))
-        t = len(toks) - 1
+            deps.update(int(i) for i in np.unique(track(r[0])["w"][r[1]:r[2]:r[3]]))
+        deps.discard(-1)
         for r in writes:
-            track(r[0])["w"][cols(r)] = t
+            h = track(r[0])
+            h["w"][r[1]:r[2]:r[3]] = me
+            for j, cols in list(h["r"].items()):
+                if cols[r[1]:r[2]:r[3]].any():
+                    deps.add(j)
+                    cols[r[1]:r[2]:r[3]] = False
+                    if not cols.any():
+                        del h["r"][j]
         for r in reads:
             h = track(r[0])
-            key = q if sem in SEMQ.values() else sem
-            if key not in h["r"]:
-                h["r"][key] = np.full(len(h["w"]), -1)
-            h["r"][key][cols(r)] = t
+            h["r"].setdefault(me, np.zeros(len(h["w"]), bool))[r[1]:r[2]:r[3]] = True
+        ops.append({"q": q, "fn": fn, "cost": cost, "kind": kind, "lat": lat, "deps": deps, "order": set(after), "grp": grp,
+                    "banks": set(r[0] for r in reads + writes if r[0] in PS), "sem": sem, "inc": inc, "soft": set()})
+        return me
 
     def R(name, a=0, b=None, st=1, p=None):
         if b is None:
@@ -138,41 +103,55 @@ def rank_program(g, core, T, topo):
             n, at = PLACE[n]
             a, b = a + at, b + at
         c = slice(a, b) if st == 1 else slice(a, b, st)
-        return T[n][:, c] if p is None else T[n][0:p, c]
+        return T[n][:, c] if p is None else T[n][p[0]:p[1], c]
 
-    def flat(rs):
-        out = []
-        for r in rs:
-            if isinstance(r, tuple):
-                if r[0] == "ind":
-                    out += [r[1], r[2]]
-                else:
-                    out.append(r)
-        return out
+    def size(r):
+        return 16 * size(r[2]) if r[0] == "ind" else len(range(r[1], r[2], r[3]))
+
+    def narrow(r):
+        return r[0] in SB and SB[r[0]][1] in (B, U, H)
 
     def val(s):
         return ap(s) if isinstance(s, tuple) else s
 
-    def do(q, reads, writes, fn):
-        reads, writes = flat(reads), flat(writes)
-        need(q, reads, writes)
-        fn().then_inc(T.sem[SEMQ[q]], 1)
-        done(q, SEMQ[q], 1, reads, writes)
+    def do(q, ins, out, fn, cyc, **kw):
+        reads, writes = [], []
+        n = size(out)
+        cost = max(64, n * cyc) * CY
+        for r in ins:
+            if isinstance(r, tuple):
+                if r[0] == "ind":
+                    reads += [r[1], r[2]]
+                    cost = 0.06 + n * GA * CY
+                else:
+                    reads.append(r)
+        if out[0] == "ind":
+            reads.append(out[2])
+            writes.append(out[1])
+            cost = 0.05 + n * SCAT * CY
+        else:
+            writes.append(out)
+        return record(q, reads, writes, fn, kw.pop("cost", cost), **kw)
+
+    def half(*rs):
+        return 0.5 if all(narrow(r) for r in rs) else 1
 
     def tt(out, a, b, op):
-        do("V", [a, b], [out], lambda: g.vector.tensor_tensor(ap(out), ap(a), ap(b), op))
+        return do("V", [a, b], out, lambda: g.vector.tensor_tensor(ap(out), ap(a), ap(b), op), 1 if a[0] in PS or b[0] in PS else 2)
 
     def ts(out, a, s1, op0, s2=None, op1=None):
         if op1 is None:
-            do("V", [a, s1], [out], lambda: g.vector.tensor_scalar(ap(out), ap(a), val(s1), None, op0))
-        else:
-            do("V", [a, s1, s2], [out], lambda: g.vector.tensor_scalar(ap(out), ap(a), val(s1), val(s2), op0, op1))
+            return do("V", [a, s1], out, lambda: g.vector.tensor_scalar(ap(out), ap(a), val(s1), None, op0), half(out, a))
+        return do("V", [a, s1, s2], out, lambda: g.vector.tensor_scalar(ap(out), ap(a), val(s1), val(s2), op0, op1), half(out, a))
 
     def cp(out, a):
-        do("V", [a], [out], lambda: g.vector.tensor_copy(ap(out), ap(a)))
+        return do("V", [a], out, lambda: g.vector.tensor_copy(ap(out), ap(a)), half(out, a))
+
+    def fill(out, c):
+        return do("V", [], out, lambda: g.vector.memset(ap(out), c), half(out))
 
     def scan(out, d0, d1, init, op0, op1):
-        do("V", [d0, d1], [out], lambda: g.vector.tensor_tensor_scan(ap(out), ap(d0), ap(d1), init, op0, op1))
+        return do("V", [d0, d1], out, lambda: g.vector.tensor_tensor_scan(ap(out), ap(d0), ap(d1), init, op0, op1), 1)
 
     def act(out, a, f, bias=None, scale=None):
         def fn():
@@ -181,468 +160,587 @@ def rank_program(g, core, T, topo):
             if bias is None:
                 return g.scalar.activation(ap(out), ap(a), f, scale=val(scale))
             return g.scalar.activation(ap(out), ap(a), f, bias=val(bias), scale=val(scale))
-        do("S", [a, bias, scale], [out], fn)
+        return do("S", [a, bias, scale], out, fn, 1)
 
-    def mm(out, l, r, start=True, stop=True):
-        do("T", [l, r], [out], lambda: g.tensor.matmul(ap(out), ap(l), ap(r), start, stop))
+    group = {}
+
+    def mm(out, l, r, start=True, stop=True, after=()):
+        bank = out[0]
+        prev = list(after) if start else [group[bank]]
+        cost = max(min(64, size(l)), size(r)) * (4 if SB[l[0]][1] == F else 1) * CY / 2 + 0.004
+        group[bank] = do("T", [l, r], out, lambda: g.tensor.matmul(ap(out), ap(l), ap(r), start, stop), 1, cost=cost,
+                         grp=(bank, start, stop), after=prev)
+        return group[bank]
 
     def iota(out, pat, base, cm):
+        cost = 0.13 + 2 * size(out) * CY
         if SB[out[0]][1] != I:
-            do("G", [], [out], lambda: g.iota(ap(out), pat, base, cm, allow_small_or_imprecise_dtypes=True))
-        else:
-            do("G", [], [out], lambda: g.iota(ap(out), pat, base, cm))
+            return do("G", [], out, lambda: g.iota(ap(out), pat, base, cm, allow_small_or_imprecise_dtypes=True), 1, cost=cost)
+        return do("G", [], out, lambda: g.iota(ap(out), pat, base, cm), 1, cost=cost)
 
-    nd, nm = [0], [0]
+    def gcopy(out, a):
+        n = size(out)
+        return do("G", [a], out, lambda: g.affine_select(ap(out), ap(a), [[0, n]], OP.is_ge, 0.0, 0, 0), 1, cost=0.17 + 2 * n * CY)
+
+    def copy(out, a, qs, scale=None):
+        first = len(ops)
+        alt = {}
+        for q in qs:
+            if q == "G":
+                gcopy(out, a)
+            elif q == "S":
+                act(out, a, AF.Copy, None, scale)
+            elif scale is None:
+                cp(out, a)
+            else:
+                ts(out, a, scale, OP.mult)
+            alt[q] = (ops[-1]["fn"], ops[-1]["cost"])
+            if len(ops) > first + 1:
+                for h in hist.values():
+                    h["w"][h["w"] == first + 1] = first
+                    h["r"].pop(first + 1, None)
+                ops.pop()
+        ops[first]["alt"] = alt
+        return first
+
+    nd, nm, lastdma = [0], [0], {}
 
     def newsem():
         nd[0] += 1
         return "d%d" % (nd[0] - 1)
 
-    def dma(q, out, in_, reads, writes, sem=None):
-        sem = sem or newsem()
-        need(q, reads, writes)
-        QS[q].dma_start(out, in_).then_inc(T.sem[sem], 16)
-        done(q, sem, 16, reads, writes)
-        return sem
+    def dma(q, out, in_, reads, writes, nbytes, sem=None, chain=True):
+        i = record(q, reads, writes, lambda: QS[q].dma_start(out, in_), 0.1, kind="dma", lat=nbytes / 180e3, sem=sem or newsem(),
+                   inc=16, after=[lastdma[q]] if chain and q in lastdma else [])
+        lastdma[q] = i
+        return i
 
     def send(src, dst, to):
         k = nm[0]
         nm[0] += 1
         engs = topo.engines(core, to)[:8]
         rid, pid, _s = topo.addr(to)
-        need("G", [src], [])
-        g.remote_dma(out_ap=ap(dst), in_ap=ap(src), remote_sem=T.sem["a%d" % k], local_sem=T.sem["l%d" % k], pid=pid,
-                     routing_id=rid, dma_engine_mask=sum(1 << e for e in engs))
-        done("G", "l%d" % k, len(engs), [src], [])
-        done("G", "a%d" % k, len(engs), [], [dst], {})
+        nb = 128 * size(src) * (2 if narrow(src) else 4)
+
+        def fn():
+            return g.remote_dma(out_ap=ap(dst), in_ap=ap(src), remote_sem=T.sem["a%d" % k], local_sem=T.sem["l%d" % k], pid=pid,
+                                routing_id=rid, dma_engine_mask=sum(1 << e for e in engs))
+        i = record("G", [src], [], fn, 0.4 if k else 2.4, kind="send", lat=0.5 + nb / 40e3, sem="l%d" % k, inc=len(engs))
+        record("A", [], [dst], None, 0.0, kind="land", lat=1.5, sem="a%d" % k, inc=len(engs), after=[i])
+        return i
+
+    def chain(ids):
+        for a, b in zip(ids, ids[1:]):
+            ops[b]["soft"].add(a)
 
     def C(i):
         return R("col", i, i + 1)
 
     SH, AN = OP.arith_shift_right, OP.bitwise_and
     EQ, MU, AD, SU, MX, MN, LE, GT, LT = OP.is_equal, OP.mult, OP.add, OP.subtract, OP.max, OP.min, OP.is_le, OP.is_gt, OP.is_lt
+    ROW = (0, 1)
 
-    def expand(zx, z, pieces):
-        w = 256 // pieces
-        for c in range(pieces):
-            act(R(zx, 16 * w * c, 16 * w * c + 16 * w), IND(R(z), R("zl", w * c, w * c + w)), AF.Copy)
+    def hn(h):
+        return (128 * h, 128 * h + 128)
 
-    dma("Y", ap(R("vA")), T.v0[:], [], [R("vA")])
-    dma("S", ap(R("zA")), T.z0[:], [], [R("zA")])
-    dma("Y", ap(R("eS")), T.E[:], [], [R("eS")])
-    dma("Y", ap(R("xS")), T.X[:], [], [R("xS")])
-    for k in range(3):
+    def hm(h):
+        return (8 * h, 8 * h + 8)
+
+    def edges(k, q):
         s = newsem()
         for gg in range(8):
             c = R("t%d" % k, 16 * gg, 16 * gg + 16)
-            dma("Y", ap(c), T.E[16 * gg + k, :], [], [c], s)
-    dma("Y", ap(R("LA")), T.L0[:], [], [R("LA")])
-    dma("Y", ap(R("e0r")), T.E[0::16, :], [], [R("e0r")])
-    dma("Y", ap(R("e1r")), T.E[1::16, :], [], [R("e1r")])
+            dma(q, ap(c), T.E[16 * gg + k, :], [], [c], 50000, s)
+    whole = {"z": ("zA", T.z0, 100000), "L": ("LA", T.L0, 170000), "v": ("vA", T.v0, 50000), "X": ("xS", T.X, 560000), "E": ("eS", T.E, 1090000)}
+    for q, names in zip("SY", OPT["load"]):
+        for c in names:
+            if c in whole:
+                dma(q, ap(R(whole[c][0])), whole[c][1][:], [], [R(whole[c][0])], whole[c][2])
+            else:
+                edges(int(c), q)
 
     iota(R("iC", 0, 1), [[0, 1]], 0, 1)
-    iota(R("iN"), [[1, 256]], 0, 0)
-    iota(R("iD"), [[1, 256]], 128, -1)
-    iota(R("mg"), [[1, 8], [0, 16]], 0, 0)
+    iota(R("iD"), [[1, 128]], 0, -1)
+    iota(R("iN"), [[1, 32]], 0, 0)
     iota(R("gp"), [[0, 2], [1, 8]], 0, 0)
     iota(R("kk"), [[0, 16], [1, 16]], 0, 0)
-    iota(R("ck"), [[144, 2], [0, 8], [256, 16]], 0, 0)
+    iota(R("e32"), [[1, 32], [0, 16]], 0, 0)
+    iota(R("ck", p=ROW), [[16640, 2], [0, 8], [256, 16]], 0, 0)
+    iota(R("io"), [[1, 144]], 0, 0)
+    iota(R("KLc", p=ROW), [[0, 8], [4096, 16]], 65536, 0)
+    iota(R("g16"), [[16, 8]], 0, 0)
+    iota(R("mg"), [[1, 8], [0, 16]], 0, 0)
+    iota(R("io2k"), [[1, 2176]], 0, 0)
     cp(R("zl"), R("iN"))
-    expand("zx0", "zA", 4)
-    send(R("zA"), R("zB"), nxt)
-    iota(R("io128"), [[1, 128]], 0, 0)
-    iota(R("g16"), [[0, 2], [16, 8]], 0, 0)
-    iota(R("io16"), [[1, 16]], 0, 0)
-    iota(R("io2k"), [[1, 2048]], 0, 0)
     ts(R("iC", 1, 2), R("iC", 0, 1), 4, SH)
     ts(R("iC", 2, 3), R("iC", 0, 1), 15, AN)
     ts(R("iC", 3, 4), R("iC", 0, 1), 7, AN)
     ts(R("iC", 4, 5), R("iC", 0, 1), 3, SH, 1, AN)
-    ts(R("iC", 5, 6), R("iC", 0, 1), 3, SH)
-    cp(R("col", 1, 6), R("iC", 1, 6))
-    PG, PK, P7, KY, P8 = C(1), C(2), C(3), C(4), C(5)
-    ts(C(6), PK, 2.0, MU, 1.0, AD)
-    for k in range(4):
-        ts(C(8 + k), PK, float(k), EQ)
-    ts(C(7), C(8), 4096.0, MU)
-    ts(C(12), PK, 2048.0, MU)
-    ts(C(13), PK, 2.0, OP.is_ge)
-    tt(C(20), C(10), C(11), AD)
-    ts(C(14), C(20), -1.0, MU, 1.0, AD)
-    ts(C(15), PK, -2048.0, MU)
-    tt(C(16), C(9), C(8), SU)
-    ts(C(17), KY, -15.0, MU, 16.0, AD)
-    for h in range(2):
-        ts(C(18 + h), PG, float(h), EQ, C(17), MU)
-        ts(C(21 + h), P8, float(h), EQ)
-    ts(C(23), PK, 1.0, AD)
-    act(R("ones"), R("mg"), AF.Identity, 1.0, 0.0)
-    ts(R("If"), R("iD", 0, 128), 128.0, EQ)
+    ts(R("iC", 5, 6), R("iC", 0, 1), 31, AN)
+    cp(R("col", 0, 6), R("iC", 0, 6))
+    PP, PG, PK, P7, KY, P32 = C(0), C(1), C(2), C(3), C(4), C(5)
+    ts(R("col", 8, 16), R("gp", 0, 8), PK, EQ)
+    for t in range(2):
+        tt(C(16 + t), C(8 + 2 * t), C(9 + 2 * t), AD)
+    ts(R("col", 18, 20), R("col", 16, 18), -1.0, MU, 1.0, AD)
+    ts(C(20), PK, 1.0, MU, 0.5, AD)
+    ts(C(21), PK, -1.0, MU, -0.5, AD)
+    ts(C(22), PK, -2.0, MU, -63.5 / 64, AD)
+    ts(C(23), P7, 16.0, MU, 16.0, AD)
+    ts(C(24), KY, -127.0, MU, 128.0, AD)
+    ts(C(25), PP, 2048.0, AD)
+    ts(C(26), PP, 65536.0 + 2048.0, AD)
+    ts(C(27), PK, 2048.0, AD)
+    ts(C(28), PK, 1.0, AD)
+    ts(C(29), C(8), 16.0, MU, -1.0, AD)
+    tt(C(31), C(9), C(8), SU)
+    ts(C(30), C(31), 16.0, MU)
+    fill(R("ones"), 1.0)
+    fill(R("cq"), -0.25)
+    fill(R("c175", p=ROW), 1.75)
+    fill(R("NP"), 0.0)
+    for j, c in enumerate((1.0 / 128, -1.0, 1.0, 0.5, -0.5, 0.25)):
+        ts(R("IM", 128 * j, 128 * j + 128), R("iD"), 0.0, EQ, c, MU)
+    PHI, nI, Ib, Ih, nIh, Iq = [R("IM", 0, 256)] + [R("IM", 128 * j, 128 * j + 128) for j in range(1, 6)]
+    If = R("If")
+    ts(If, R("iD"), 0.0, EQ)
+    ts(R("EXP"), R("e32"), P32, EQ)
     ts(R("W16"), R("gp"), PG, EQ, 4096.0, MU)
-    ts(R("PHI", 0, 128), R("If"), 0.125, MU)
-    ts(R("PHI", 128, 256), R("If"), -2.0, MU)
-    ts(R("RS01"), R("kk"), 0.0, GT)
-    ts(R("RST"), R("RS01"), -67108864.0, MU, 33554432.0, AD)
-    cp(R("Ib"), R("If"))
-    ts(R("iA"), R("iD"), 15, AN)
-    ts(R("maskJ"), R("iA"), 0.0, EQ)
+    ts(R("RST"), R("kk"), 0.0, EQ, 33554432.0, MU)
+    ts(R("RSD"), R("kk", 0, 128), 0.0, EQ, C(26), MU)
+    ts(R("maskJ"), R("kk"), PK, EQ)
+    ts(R("Z2"), R("io"), C(23), EQ, C(24), MU)
+    I16 = R("I16")
+    ts(I16, R("iD"), 0.0, EQ)
+    ts(R("B8h"), R("gp", 0, 8), PG, EQ)
+    ts(R("BB4"), R("mg"), PG, EQ, 4096.0, MU)
+    for out, c in ((R("B8", 0, 8), 1.0), (R("B8", 8, 16), -1.0), (R("W8", 0, 8), C(20)), (R("W8", 8, 16), C(21)),
+                   (R("B8f", 0, 8), 1.0), (R("B8f", 8, 16), 0.5), (R("SelC", 0, 8), C(31)), (R("SelC", 8, 16), C(8)),
+                   (R("SelC", 16, 24), C(9)), (R("SelC", 24, 32), C(10)), (R("WY", 0, 8), C(28)), (R("WY", 8, 16), C(29)),
+                   (R("WY", 16, 24), C(30))):
+        ts(out, R("gp", 0, 8), PG, EQ, c, MU)
+    B8p, B8n = R("B8", 0, 8), R("B8", 8, 16)
+    scan(R("wrow", p=ROW), R("c175", p=ROW), R("cq", p=ROW), 2.0 ** -120 / 1.75, MU, MX)
     for h in range(2):
-        ts(R("BW%d" % h), R("mg"), P7, EQ, C(18 + h), MU)
-        ts(R("BD%d" % h), R("mg"), P7, EQ, C(21 + h), MU)
-    ts(R("BBf"), R("mg"), PG, EQ)
-    cp(R("BB"), R("BBf"))
-    ts(R("B8p"), R("gp", 0, 8), PG, EQ)
-    ts(R("B8n"), R("gp", 0, 8), PG, EQ, -1.0, MU)
-    ts(R("W8h"), R("gp", 0, 8), PG, EQ, C(6), MU)
-    ts(R("B8f"), R("gp", 0, 8), PG, EQ)
-    ts(R("S8f"), R("gp", 0, 8), PG, EQ, C(8), MU)
-    ts(R("nIb"), R("If"), -1.0, MU)
-    ts(R("nIf"), R("If"), -1.0, MU)
-    ts(R("Sel0f"), R("BBf"), C(8), MU)
-    ts(R("WY", 0, 8), R("gp", 0, 8), PG, EQ, C(23), MU)
-    ts(R("WY", 8, 16), R("gp", 0, 8), PG, EQ)
-    ts(R("jm"), R("io16"), PK, EQ)
-    for b in range(2):
-        ts(R("P16", 128 * b, 128 * b + 128), R("If"), C(7), MU)
+        mm(R("N1", 256 + h, 257 + h), R("wrow", *hn(h), 1, ROW), R("If", 0, 1, 1, ROW))
+    cp(R("col", 32, 34), R("N1", 256, 258))
+    ts(R("col", 34, 36), R("col", 32, 34), 2.54, MU)
+
     cp(R("vlA"), R("vA"))
+    send(R("zA"), R("zB"), nxt)
+    cp(R("Lo0"), R("LA"))
+    send(R("Lo0"), R("LB"), nxt)
+    for k in (1, 0):
+        cp(R("tf", *hn(k)), R("t%d" % k))
+        mm(R("N0", *hn(k)), R("tf", *hn(k)), I16)
+        cp(R("el", *hn(k)), R("N0", *hn(k)))
+    w = OPT["tch"]
+    ids = []
+    for c in range(0, 2048, w):
+        copy(R("XB", c, c + w), IND(R("xS"), R("el", 128 + c // 16, 128 + (c + w) // 16)), OPT["B"])
+        for tab, op in (("HI", MX), ("LO", MN)):
+            ids.append(tt(R(tab, c, c + w), IND(R("xS"), R("el", c // 16, (c + w) // 16)), R("XB", c, c + w), op))
+    chain(ids)
+    chain([copy(R("ef", c, c + 256), R("eS", c, c + 256), OPT["ef"]) for c in range(0, 2048, 256)])
+    for hi in range(16):
+        mm(R("M", hi, 384, 16), R("ef", 128 * hi, 128 * hi + 128), R("WY"))
+    act(R("ys"), R("M", 0, 384), AF.Copy)
+    for j in range(3):
+        mm(R("M", *hn(j)), R("ys", *hn(j)), If)
 
-    def lists(part):
-        if part == 0:
-            for k in range(3):
-                cp(R("tf", 128 * k, 128 * k + 128), R("t%d" % k))
-                mm(R("Q0", 128 * k, 128 * k + 128), R("tf", 128 * k, 128 * k + 128), R("If"))
-        else:
-            cp(R("elf"), R("Q0", 0, 384))
-            cp(R("el"), R("elf", 0, 256))
+    pb = [0]
 
-    def selectors(part):
+    def minus_zT(z, h, zT="zT"):
+        mm(R("N%d" % h, 0, 128), R(z, *hn(h)), nI)
+        copy(R(zT, *hn(h)), R("N%d" % h, 0, 128), OPT["sm"])
+
+    def expand(t, zx, z, zwalk):
+        ids = []
+        for h in range(2):
+            a, b = 128 * h, 128 * h + 128 - 32 * OPT["gS"][t][h]
+            if a < b:
+                ids += [copy(R(zx, 16 * a + k, 16 * b, 16), R(z, a, b), OPT["exp"][t]) for k in range(16)]
+        chain(ids)
+        for h in range(2):
+            a, b = 128 * h + 128 - 32 * max(OPT["vx"][t]), 128 * h + 128
+            if a < b:
+                chain([copy(R("zw", 16 * a + k, 16 * b, 16), R(zwalk, a, b), OPT["expw"][t]) for k in range(16)])
+
+    def tolist(h, parts, out, add, lo=None):
+        kb = "K%d" % h
+        P16, a, n = (0, 16), 256 * h, 2 if lo else 1
+        mm(R(kb, 384, 512, 1, P16), parts, Ib)
+        copy(R("wT", a, a + 128, 1, P16), R(kb, 384, 512, 1, P16), OPT["sm"])
+        if lo:
+            copy(R("wT", a + 128, a + 256, 1, P16), R(kb, 384, 512, 1, P16), OPT["sm"], R("col", 4, 5, 1, P16))
         for j in range(16):
-            c = (128 * j, 128 * j + 128)
-            if part == 0:
-                ts(R("IJ", *c), R("Ib"), R("jm", j, j + 1), MU)
+            mm(R(kb, 256, 256 + 8 * n), R("Z2", 16 - j, 144 - j, 1, P16), R("wT", a + j, a + 128 * n, 16, P16), j == 0, j == 15)
+        ts(R(out, *hm(h)), R(kb, 256, 264), add, AD)
+        if lo:
+            cp(R(lo, *hm(h)), R(kb, 264, 272))
+
+    def masked(h, win, at, slot, n=1, base=False):
+        kb, gm, one = "K%d" % h, "gm32" if base else "gm", R("B8f" if base else "B8h", 0, 8)
+        tt(R(gm, at, at + 128 * n), IND(win, R("zl", 0, 8 * n)), R("maskJ", 0, 128 * n), MU)
+        for j in range(n):
+            o = R(kb, slot + 8 * j, slot + 8 * j + 8)
+            mm(o, R(gm, at + 128 * j, at + 128 * j + 128), one, True, not base)
+            if base:
+                mm(o, R("ones", p=ROW), R("g16", p=ROW), False, True)
+
+    def minus_z(src, b, zT, f, dst):
+        bank = "P%d" % (pb[0] % 2)
+        pb[0] += 1
+        q, n = 32 * (b // 512 % 4), hn(b // 2048)
+        mm(R(bank), Ib, src, True, False)
+        mm(R(bank), R(zT, *n, 1, (q, q + 32)), R("EXP", p=(q, q + 32)), False, True)
+        act(dst, R(bank), f)
+
+    def apart(out, lst):
+        act(out, IND(R("io2k"), lst), AF.Abs, C(22), 1.0 / 64)
+
+    def walk(t, step, h, vl, lo, out, outlo):
+        n, m, kb = hn(h), hm(h), "K%d" % h
+        cp(R("c16", *n), IND(R("eS"), R(vl, *m)))
+        ts(R("cf", *n), R("c16", *n), 0.0, AD)
+        ts(R("H", *n), R("c16", *n), 16448.5, AD)
+        onV = OPT["vx"][t][step]
+        for j in range(4):
+            b = 2048 * h + 512 * j
+            x = IND(R("xS"), R("c16", b // 16, b // 16 + 32))
+            if j < 4 - onV:
+                copy(R("xg", b, b + 512), x, OPT["xg"])
+                minus_z(R("xg", b, b + 512), b, "zT", AF.Abs, R("ab", b, b + 512))
             else:
-                act(R("BH", *c), R("BB"), AF.Copy, None, R("jm", j, j + 1))
+                tt(R("xg", b, b + 512), x, R("zw", b, b + 512), SU)
+                act(R("ab", b, b + 512), R("xg", b, b + 512), AF.Abs)
+        mm(R(kb, 0, 256), R("H", *n), PHI, True, False)
+        mm(R(kb, 0, 256), R("ones", p=ROW), R("ck", p=ROW), False, False)
+        mm(R(kb, 128, 256), R("cf", *n), I16, False, False)
+        if t:
+            apart(R("ad", *n), R(vl, *m))
+            tt(R("mk", *n), IND(R("m0"), R(lo, *m)), R("ad", *n), GT)
+        for k in range(16):
+            mm(R(kb, k, 256, 16), R("ab", 2048 * h + k, 2048 * h + 2048, 16), R("W16"), False, k == 15 and not t)
+        if t:
+            mm(R(kb, 0, 256, 16), R("mk", *n), R("W16"), False, True)
+        scan(R("R", 256 * h, 256 * h + 256), R("RST"), R(kb, 0, 256), 0.0, MX, MN)
+        a = (16 * h, 16 * h + 16)
+        cp(R("wi", *a), R("R", 256 * h + 15, 256 * h + 256, 16))
+        ts(R("wa", *a), R("wi", *a), 127, AN)
+        cp(R("wb", *a), R("wa", *a))
+        tolist(h, R("wb", *a), out, -128.0, outlo)
 
-    def tables(el, piece):
-        h, k = piece % 2, piece // 2
-        act(R("XB" if k else "XA", 1024 * h, 1024 * h + 1024), IND(R("xS"), R(el, 128 * k + 64 * h, 128 * k + 64 * h + 64)), AF.Copy)
+    gaps = []
 
-    def hilo(h):
-        a = (1024 * h, 1024 * h + 1024)
-        tt(R("HI", *a), R("XA", *a), R("XB", *a), MX)
-        tt(R("LO", *a), R("XA", *a), R("XB", *a), MN)
-
-    def yasum(part):
-        if part == 0:
-            for hi in range(16):
-                mm(R("Q1", hi, 256, 16), R("ef", 128 * hi, 128 * hi + 128), R("WY"))
-        else:
-            for b in range(2):
-                mm(R("Q1", 128 * b, 128 * b + 128), R("ys", 128 * b, 128 * b + 128), R("If"))
-        act(R("s01" if part else "ys"), R("Q1", 0, 256), AF.Copy)
-
-    def tolist(bank, out, add, low=False):
-        tt(R("mj"), R(bank, 0, 256), R("maskJ"), MU)
-        scan(R("sc"), R("RS01"), R("mj"), 0.0, MU, AD)
-        if low:
-            cp(R("ui", 0, 16), R("sc", 15, 256, 16))
-            ts(R("ui", 16, 32), R("ui", 0, 16), 2047, AN)
-            cp(R(out), R("ui", 16, 32))
-        else:
-            ts(R(out), R("sc", 15, 256, 16), add, AD)
-
-    def walk(vl, zx, out, marked, sfill, vfill):
-        cp(R("c16"), IND(R("eS"), R(vl)))
-        if vl == "vlA":
-            cp(R("ef"), R("eS"))
-        act(R("cf"), IND(R("ef"), R(vl)), AF.Copy)
-        act(R("H"), R("cf"), AF.Identity, 1024.0, 0.5)
-        if marked:
-            act(R("mk"), IND(R("MARK"), R(vl)), AF.Copy)
-        for ch in range(4):
-            a = (1024 * ch, 1024 * ch + 1024)
-            tt(R("df", *a), IND(R("xS"), R("c16", 64 * ch, 64 * ch + 64)), R(zx, *a), SU)
-            act(R("ab", *a), R("df", *a), AF.Abs)
-            sfill(ch)
-            if ch % 2 == 1:
-                h = ch // 2
-                kb = "K%d" % h
-                n = (128 * h, 128 * h + 128)
-                mm(R(kb, 0, 256), R("ones", 0, 128, 1, 1), R("ck", 0, 256, 1, 1), True, False)
-                mm(R(kb, 0, 256), R("H", *n), R("PHI"), False, False)
-                mm(R(kb, 128, 256), R("cf", *n), R("If"), False, False)
-                if marked:
-                    mm(R(kb, 0, 256), R("mk", *n), R("P16"), False, False)
-                for k in range(16):
-                    mm(R(kb, k, 256, 16), R("ab", 2048 * h + k, 2048 * h + 2048, 16), R("W16"), False, k == 15)
-        vfill()
-        for h in range(2):
-            scan(R("R", 256 * h, 256 * h + 256), R("RST"), R("K%d" % h, 0, 256), 0.0, MX, MN)
-        ts(R("wi"), R("R", 15, 512, 16), -128.0, AD)
-        ts(R("wa"), R("wi"), 255, AN)
-        cp(R("wb"), R("wa"))
-        mm(R("Q0", 0, 128, 1, 32), R("wb"), R("Ib"))
-        cp(R("wT", 0, 128, 1, 32), R("Q0", 0, 128, 1, 32))
-        for h in range(2):
-            mm(R("N0", 128 * h, 128 * h + 128), R("BW%d" % h, 0, 128, 1, 32), R("wT", 0, 128, 1, 32))
-        tolist("N0", out, -16.0)
-
-    def gapS(L16, zx):
-        e0 = 4096 - 16 * SHARE
-        for tab, sb in (("HI", "sh"), ("LO", "sl")):
-            act(R(sb, 0, 16 * SHARE), IND(R(tab), R(L16, 256 - SHARE, 256)), AF.Copy)
-        i = 0
-        for sb, dst in (("sh", "mh"), ("sl", "ml")):
-            for c in range(0, 16 * SHARE, 512):
-                kb = "K%d" % (i % 2)
-                i += 1
-                w = min(512, 16 * SHARE - c)
-                mm(R(kb, 0, w), R("Ib"), R(sb, c, c + w), True, False)
-                mm(R(kb, 0, w), R("nIb"), R(zx, e0 + c, e0 + c + w), False, True)
-                act(R(dst, e0 + c, e0 + c + w), R(kb, 0, w), AF.Relu)
-
-    def gap(t, L16, zx, h):
-        for c in range(2):
-            n0, n1 = 128 * h + 64 * c, min(128 * h + 64 * c + 64, 256 - SHARE)
-            if n0 < n1:
-                a = (16 * n0, 16 * n1)
-                tt(R("mh", *a), IND(R("HI"), R(L16, n0, n1)), R(zx, *a), MX)
-                tt(R("ml", *a), IND(R("LO"), R(L16, n0, n1)), R(zx, *a), MX)
+    def gap(t, h, z, L16, zx):
+        onS = OPT["gS"][t][h]
+        if onS:
+            minus_zT(z, h, "zT2")
+        for j in range(4):
+            n0 = 128 * h + 32 * j
+            a = (16 * n0, 16 * n0 + 512)
+            for tab, dst, sb in (("HI", "mh", "sh"), ("LO", "ml", "so")):
+                x = IND(R(tab, 0, 2048), R(L16, n0, n0 + 32))
+                if j < 4 - onS:
+                    gaps.append(tt(R(dst, *a), x, R(zx, *a), MX))
+                else:
+                    act(R(sb, *a), x, AF.Copy)
+                    minus_z(R(sb, *a), a[0], "zT2", AF.Relu, R(dst, *a))
         for k in range(16):
             if k // 2 != t:
                 o = R("G", 128 * h + k, 128 * h + 128, 16)
-                mm(o, R("mh", 2048 * h + k, 2048 * h + 2048, 16), R("B8p"), True, False)
-                mm(o, R("ml", 2048 * h + k, 2048 * h + 2048, 16), R("B8n"), False, True)
+                mm(o, R("mh", 2048 * h + k, 2048 * h + 2048, 16), B8p, True, False)
+                mm(o, R("ml", 2048 * h + k, 2048 * h + 2048, 16), B8n, False, True)
 
-    def Q(i):
-        return R("qs", 16 * i, 16 * i + 16)
+    def entry(t, h, e, z, vl):
+        a = (256 * e + 128 * h, 256 * e + 128 * h + 128)
+        tt(R("eh", *a), IND(R("HI", 0, 2048), R(vl, *hm(h))), R(z, *hn(h)), MX)
+        tt(R("en", *a), IND(R("LO", 0, 2048), R(vl, *hm(h))), R(z, *hn(h)), MX)
+        o = R("G", 128 * h + 2 * t + e, 128 * h + 128, 16)
+        mm(o, R("eh", *a), B8p, True, False)
+        mm(o, R("en", *a), B8n, False, True)
+        act(R("r%d" % (e + 1), *hn(h)), IND(R("io2k"), R(vl, *hm(h))), AF.Copy, None, C(8 + 2 * t + e))
 
-    def prep(t, z, v1, v2, xi):
-        act(R("r1"), IND(R("io2k"), R(v1)), AF.Copy, None, C(8 + 2 * t))
-        act(R("v2n"), IND(R("io2k"), R(v2)), AF.Copy)
-        act(R("r2"), R("v2n"), AF.Copy, None, C(9 + 2 * t))
-        mm(R("Q0", 0, 256), R("If"), R("Lb"), True, False)
-        mm(R("Q0", 0, 256), R("If"), R("r1"), False, False)
-        mm(R("Q0", 0, 256), R("If"), R("r2"), False, True)
-        act(R("KL"), R("Q0", 0, 256), AF.Copy)
-        act(R("Ln"), R("Q0", 0, 256), AF.Identity, C(15), 1.0)
-        mm(R("N1", 0, 256), R("Ib"), R(xi), True, False)
-        mm(R("N1", 0, 256), R("nIb"), R(z), False, True)
-        mm(R("N2", 0, 256), R("Ib"), R(xi), True, False)
-        mm(R("N2", 0, 256), R("Ib"), R(z), False, True)
+    def decide(t, h, z, L16, xi, zo, Lo):
+        n, m, kb, nb = hn(h), hm(h), "K%d" % h, "N%d" % h
+        s0, s1, s3 = R(nb, 0, 128), R(nb, 128, 256), R(nb, 384, 512)
 
-    def entries(t, z, v1, v2):
-        for e, vl in enumerate((v1, v2)):
-            a = (256 * e, 256 * e + 256)
-            tt(R("eh", *a), IND(R("HI"), R(vl)), R(z), MX)
-            tt(R("en", *a), IND(R("LO"), R(vl)), R(z), MX)
-            for h in range(2):
-                n = (256 * e + 128 * h, 256 * e + 128 * h + 128)
-                o = R("G", 128 * h + 2 * t + e, 128 * h + 128, 16)
-                mm(o, R("eh", *n), R("B8p"), True, False)
-                mm(o, R("en", *n), R("B8n"), False, True)
+        def Q(i, w=8):
+            return R("qs", 128 * h + 8 * i, 128 * h + 8 * i + w)
 
-    def prep2():
-        act(R("ab2"), R("N1", 0, 256), AF.Abs)
-        ts(R("hf"), R("N2", 0, 256), 0.5, MU, -0.25, AD)
-        cp(R("hb"), R("hf"))
-        for h in range(2):
-            n = (128 * h, 128 * h + 128)
-            mm(R("Q1", 8 * h, 8 * h + 8), R("ab2", *n), R("B8p"))
-            mm(R("Q1", 16 + 8 * h, 24 + 8 * h), R("hb", *n), R("W8h"))
-            mm(R("Q1", 32 + 8 * h, 40 + 8 * h), R("v2n", *n), R("S8f"))
-        mm(R("N1", 0, 256), R("BB"), R("ab2"))
-        mm(R("N2", 0, 256), R("Ib"), R("ab2"), True, False)
-        mm(R("N2", 0, 256), R("nIb"), R("hb"), False, True)
-        for h in range(2):
-            mm(R("K0", 128 * h, 128 * h + 128), R("KL", 128 * h, 128 * h + 128), R("If"))
+        def QI(i, w=8):
+            return R("qi", 64 * h + 8 * i, 64 * h + 8 * i + w)
 
-    def prep3(z):
-        act(Q(0), R("Q1", 0, 16), AF.Relu, 32768.0 * (TH + 1), -32768.0)
-        act(Q(2), Q(0), AF.Sign)
-        cp(R("qi", 0, 16), R("Q1", 16, 32))
-        ts(R("qi", 16, 32), R("qi", 0, 16), 2047, AN)
-        tt(Q(3), R("Q1", 32, 48), R("qi", 16, 32), SU)
-        tt(Q(4), Q(3), Q(2), MU)
-        tt(Q(5), Q(4), R("qi", 16, 32), AD)
-        ts(R("like"), R("N1", 0, 256), float(TH), LE)
-        mm(R("N1", 0, 256), R("nIf"), R("Ln"), True, False)
-        tt(R("tl"), R("N2", 0, 256), R("like"), MU)
-        mm(R("N2", 0, 256), R("Ib"), R(z), True, False)
-        mm(R("N2", 0, 256), R("nIb"), R("hb"), False, False)
-        mm(R("N2", 0, 256), R("nIb"), R("tl"), False, True)
+        def QB(i, w=8):
+            return R("qb", 48 * h + 8 * i, 48 * h + 8 * i + w)
 
-    def onehots(c0, c1):
-        for c in range(c0, c1):
-            ts(R("OH", 256 * c, 256 * c + 128), R("io128"), R("mf", c, c + 1), EQ)
-            ts(R("OH", 256 * c + 128, 256 * c + 256), R("io128"), R("mf", 16 + c, 17 + c), EQ)
-
-    def counts(bank):
-        for c in range(16):
-            mm(R(bank, 0, 128), R("OH", 256 * c, 256 * c + 128), R("OH", 256 * c + 128, 256 * c + 256), c == 0, c == 15)
-
-    def spread(bank):
-        cp(R("kT", 0, 128, 1, 16), R("Q0", 0, 128, 1, 16))
-        for h in range(2):
-            mm(R(bank, 128 * h, 128 * h + 128), R("BD%d" % h, 0, 128, 1, 16), R("kT", 0, 128, 1, 16))
-
-    def newlog(Lo):
-        tt(R("e2"), R("N1", 0, 256), R("oh"), MU)
-        tt(R("KL2"), R("Ln"), R("e2"), AD)
-        cp(R(Lo), R("KL2"))
-
-    def decide(t, zo):
-        ts(R("fk"), R("G", 0, 256), float(TAU[t]), LE, 32768.0, MU)
-        tt(R("fk2"), R("K0", 0, 256), R("fk"), AD)
-        scan(R("R2"), R("RST"), R("fk2"), 0.0, MX, MN)
-        tt(Q(6), R("R2", 15, 256, 16), Q(0), MX)
-        mm(R("Q0", 0, 128, 1, 16), Q(6), R("If"))
-        cp(R("mi", 0, 16), Q(6))
-        ts(R("mi", 16, 32), R("mi", 0, 16), 7, SH, 15, AN)
-        ts(R("mi", 32, 48), R("mi", 0, 16), 127, AN)
-        ts(Q(7), Q(6), 32768.0, LT)
-        spread("N0")
-        ts(Q(8), Q(7), -1000.0, MU, 1000.0, AD)
-        tt(Q(9), R("mi", 16, 32), R("g16"), AD)
-        tt(R("mf", 0, 16), Q(9), Q(8), AD)
-        cp(R("mf", 16, 32), R("mi", 32, 48))
-        onehots(0, 5 if t == 0 else 2)
-        tolist("N0", "ul", 0.0, True)
-        if t == 1:
-            act(R("smk"), IND(R("MARK"), R("ul")), AF.Identity, C(8), C(16))
-            cp(R("ce"), IND(R("eS"), R("ul")))
-            ts(R("cutE"), R("N0", 0, 256), 32768.0, LT)
-            tt(R("ce2"), R("ce"), R("smk"), MU)
-            mm(R("N1", 0, 256), R("BBf"), R("ce2"), False, True)
+        def acc(o, pairs, after=()):
+            for i, (l, r) in enumerate(pairs):
+                last = mm(o, l, r, i == 0, i == len(pairs) - 1, after)
+            return last
+        zz, x, ab, hb, tl, sl = R(z, *n), R(xi, *n), R("ab2", *n), R("hb", *n), R("tl", *n), R("sl", *n)
+        Lf, r1, r2 = R("Lf", *n), R("r1", *n), R("r2", *n)
+        ts(Lf, R(L16, *n), C(18 + t), MU)
+        acc(s0, [(Ib, x), (nI, zz)])
+        acc(s1, [(Ih, x), (R("cq", 0, 128, 1, ROW), R("ones", p=ROW)), (Ih, zz)])
+        act(ab, s0, AF.Abs)
+        ts(hb, s1, 12582912.0, AD, -12582912.0, AD)
+        mm(s0, R("BB4"), ab)
+        act(sl, s0, AF.Sign, TH + 0.5, -1.0 / 4096)
+        mm(R(nb, 256, 264), ab, B8p)
+        acc(R(nb, 264, 272), [(hb, R("W8", 8, 16)), (r2, R("B8f", 8, 16))])
+        acc(R(nb, 272, 280), [(hb, R("W8", 0, 8)), (r2, R("B8f", 8, 16))])
+        act(Q(0), R(nb, 256, 264), AF.Sign, TH + 0.5, -1.0)
+        tt(Q(1), R(nb, 264, 272), Q(0), MU)
+        tt(QI(0), R(nb, 272, 280), Q(1), AD)
+        ts(QI(1), QI(0), 2047, AN)
+        cp(R("NP", 0, 128, 16), QI(1))
+        early = [mm(s3, R("NP"), I16)]
+        act(R("ef", 2048, 2176), s3, AF.Copy)
+        acc(s1, [(Ib, ab), (nI, hb)])
+        tt(tl, s1, sl, MU)
+        early.append(acc(s0, [(nIh, tl), (Ib, zz), (nIh, ab), (nIh, hb)]))
+        act(R("fk", *n), R("G", *n), AF.Relu, 262144.0 * (TAU[t] + 0.5), -262144.0)
+        key = R(kb, 0, 128)
+        acc(key, [(r2, If), (R("ones", p=ROW), R("KLc", p=ROW)), (Lf, I16), (r1, If), (sl, R("BB4")), (Ib, R("fk", *n))])
+        scan(R("R2", *n), R("RSD"), key, 0.0, MX, MN)
+        end = R("R2", 128 * h + 15, 128 * h + 128, 16)
+        cp(QI(2), end)
+        ts(QI(3), QI(2), 7, SH, 31, AN)
+        ts(QI(4), QI(2), 127, AN)
+        cp(QB(0, 16), QI(3, 16))
+        tolist(h, QB(0, 16), "ul", 0.0, "ulo")
+        ul, ce = R("ul", *m), R("ce", *n)
+        act(ce, IND(R("ef"), ul), AF.Copy)
+        act(R("sc", *n), IND(R("io2k"), ul), AF.Sign, 2047.5, -1.0)
+        tt(R("flag", *n), key, R("R2", *n), EQ)
+        apart(R("adu", *n), ul)
+        if t == 0:
+            mm(R(kb, 128, 152), ce, R("SelC", 8, 32))
+            act(Q(2, 24), R(kb, 128, 152), AF.Copy)
+            vo = Q(2)
+            masked(h, vo, 384 * h, 272)
+            ts(R("vlB", *m), R(kb, 272, 280), 0.0, AD)
+            cp(R("vi", 16 * h, 16 * h + 8), R(kb, 272, 280))
+            ts(R("vi", 16 * h + 8, 16 * h + 16), R("vi", 16 * h, 16 * h + 8), 127, AN)
+            cp(R("loB", *m), R("vi", 16 * h + 8, 16 * h + 16))
         else:
-            act(R("ce"), IND(R("ef"), R("ul")), AF.Copy)
-            ts(R("cutE"), R("N0", 0, 256), 32768.0, LT)
+            tt(R("mn", *n), IND(R("m0"), R("ulo", *m)), R("adu", *n), GT)
+            mm(R(kb, 128, 144), ce, R("SelC", 0, 16))
+            mm(R(kb, 152, 160), R("mn", *n), B8p)
+            act(Q(2), R(kb, 152, 160), AF.Copy)
+            tt(Q(3), R(kb, 128, 136), Q(2), MU)
+            vo = R("fo%d" % h, 256, 264)
+            tt(vo, R(kb, 136, 144), Q(3), AD)
+        tt(R("w", *n), s0, R("sc", *n), MU)
+        acc(s1, [(Ih, zz), (Iq, ab), (Iq, hb), (Iq, tl), (Ih, R("w", *n))], early)
+        act(zo, s1, AF.Copy)
+        ts(QI(5), QI(2), 4095, AN)
+        tt(Q(5), vo, QI(5), SU)
+        tt(R("e2", *n), IND(Q(5), R("zl", 0, 8)), R("flag", *n), MU)
+        acc(s3, [(R("e2", *n), I16), (I16, Lf), (If, r1), (If, r2)])
+        cp(Lo, s3)
+        tt(QB(2), QB(0), R("g16"), AD)
+        ts(QB(3), end, 65536.0, LT, C(32 + h) if t == 0 else 1.0, MU)
+        ids = []
+        for c in range(8):
+            a = 2048 * h + 256 * c
+            ids.append(ts(R("OH", a, a + 128), R("io", 0, 128), R("qb", 48 * h + 16 + c, 48 * h + 17 + c), EQ, R("qb", 48 * h + 24 + c, 48 * h + 25 + c), MU))
+            ids.append(ts(R("OH", a + 128, a + 256), R("io", 0, 128), R("qb", 48 * h + 8 + c, 48 * h + 9 + c), EQ))
+            mm(R("M", 384, 512), R("OH", a, a + 128), R("OH", a + 128, a + 256), h == 0 and c == 0, h == 1 and c == 7)
+        chain(ids)
+        if t == 0:
+            masked(h, Q(3, 16), 384 * h + 128, 280, 2)
+            ts(R("e12", 16 * h, 16 * h + 16), R(kb, 280, 296), 0.0, AD)
+            act(R("nB", *n), IND(R("xS"), R("e12", 16 * h + 8, 16 * h + 16)), AF.Copy)
+            tt(R("nH", *n), IND(R("xS"), R("e12", 16 * h, 16 * h + 8)), R("nB", *n), MX)
+            tt(R("nL", *n), IND(R("xS"), R("e12", 16 * h, 16 * h + 8)), R("nB", *n), MN)
+            act(R("ad2", *n), R("adu", *n), AF.Relu, 9e29, -9e29)
+            ts(Q(6), QI(5), C(25), SU)
+
+    def turn(h):
+        n, m, kb = hn(h), hm(h), "K%d" % h
+        tt(R("mn", *n), IND(R("Sb"), R("ulo", *m)), R("ad2", *n), MN)
+        mm(R(kb, 296, 304), R("mn", *n), B8p)
+        a = 128 * h
+        ts(R("qs", a + 56, a + 64), R(kb, 296, 304), C(34 + h), LE)
+        tt(R("qs", a + 64, a + 72), R("qs", a + 56, a + 64), R("qs", a + 48, a + 56), MU)
+        masked(h, R("qs", a + 64, a + 72), 128 * h, 304, 1, True)
+        ts(R("u2", *m), R(kb, 304, 312), C(27), AD)
+        cp(IND(R("HI"), R("u2", *m)), R("nH", *n))
+        cp(IND(R("LO"), R("u2", *m)), R("nL", *n))
+
+    def visit(t, vl, lo, v1, v2, xo, z, L16, zx, ini):
+        expand(t, zx, z, "zo1" if t else "zA")
         for h in range(2):
-            n = (128 * h, 128 * h + 128)
-            mm(R("Q1", 48 + 8 * h, 56 + 8 * h), R("ce2" if t else "ce", *n), R("B8f" if t else "S8f"))
-        tt(R("w"), R("N2", 0, 256), R("cutE"), MU)
-        tt(R("oh"), R("N0", 0, 256), R("KL"), EQ)
-        if t == 0:
-            onehots(5, 8)
-        mm(R("N2", 0, 256), R("Ib"), R("hb"), True, False)
-        mm(R("N2", 0, 256), R("Ib"), R("tl"), False, False)
-        mm(R("N2", 0, 256), R("Ib"), R("w"), False, True)
-        act(R(zo), R("N2", 0, 256), AF.Copy)
-        if t == 1:
-            newlog("Lo2")
-        tt(Q(3), R("Q1", 48, 64), Q(5), SU)
-        tt(Q(4), Q(3), Q(7), MU)
-        tt(R("vo2"), Q(4), Q(5), AD)
-
-    def turn0():
-        ts(R("m0"), R("Q1", 0, 128), 0.0, GT)
-        for b in range(4):
-            bank = ("G", "N2")[b % 2]
-            for j in range(4):
-                hi = 4 * b + j
-                mm(R(bank, 128 * j, 128 * j + 128), R("BH", 128 * hi, 128 * hi + 128), R("m0"))
-            act(R("MARK", 512 * b, 512 * b + 512), R(bank), AF.Copy)
-        for j in range(16):
-            mm(R("Q1", 0, 128), R("IJ", 128 * j, 128 * j + 128), R("MARK", j, 2048, 16), j == 0, j == 15)
-
-    def turn1():
-        tt(R("dl"), R("elf", 128, 384), R("elf", 0, 256), SU)
-        cp(R("mlf"), R("Q1", 0, 128))
-        for k in range(2):
-            a = (128 * k, 128 * k + 128)
-            tt(R("dm", *a), R("dl", *a), R("mlf"), MU)
-        tt(R("el2"), R("dm"), R("elf", 0, 256), AD)
-
-    def visit(t, vl, v1, v2, xo, lst, z, L16, ini):
-        def s0(ch):
-            if t == 0 and ch == 0:
-                yasum(0)
-            if t == 0 and ch == 1:
-                lists(0)
-            if t == 0 and ch == 3:
-                yasum(1)
-
-        def f0():
-            if t == 0:
-                lists(1)
-                selectors(0)
-                cp(R("Lo0"), R("LA"))
-                send(R("Lo0"), R("LB"), nxt)
-            else:
-                turn1()
-                newlog("Lo1")
-                send(R("Lo1"), R("LC"), nxt)
-            tables(lst, 0)
-            tables(lst, 2)
-
-        def s1(ch):
-            if ch == 0:
-                tables(lst, 1)
-            if ch == 1:
-                tables(lst, 3)
-            if ch == 3:
-                expand("zx1", z, 4)
-
-        def f1():
-            hilo(0)
-            hilo(1)
-            ts(R("Lb"), R(L16), C(13 + t), MU, C(12), AD)
-
-        walk(vl, "zx0", v1, t == 1, s0, f0)
+            walk(t, 0, h, vl, lo, v1, "lo1" if t else None)
         send(R(v1), R(ini[0]), nxt)
-        walk(v1, "zx0", v2, t == 1, s1, f1)
-        send(R(v2), R(ini[1]), nxt)
-        act(R(xo), IND(R("xS"), R(v2)), AF.Copy)
-        send(R(xo), R(ini[2]), nxt)
-        gapS(L16, "zx1")
-        gap(t, L16, "zx1", 0)
-        prep(t, z, *ini)
-        gap(t, L16, "zx1", 1)
-        prep2()
-        entries(t, z, ini[0], ini[1])
-        prep3(z)
-        if t == 0:
-            selectors(1)
+        for h in range(2):
+            walk(t, 1, h, v1, "lo1", v2, None)
+            send(R(v2, *hm(h)), R(ini[1], *hm(h)), nxt)
+            act(R(xo, *hn(h)), IND(R("xS"), R(v2, *hm(h))), AF.Copy)
+            send(R(xo, *hn(h)), R(ini[2], *hn(h)), nxt)
+        del gaps[:]
+        for h in range(2):
+            gap(t, h, z, L16, zx)
+        chain(gaps)
+        for h in range(2):
+            entry(t, h, 0, z, ini[0])
+            entry(t, h, 1, z, ini[1])
 
-    visit(0, "vlA", "v1o0", "v2o0", "xo0", "el", "zB", "LB", ("v1i0", "v2i0", "xi0"))
-    decide(0, "zo1")
-    mm(R("Q0", 0, 128, 1, 16), R("vo2"), R("If"))
-    spread("K1")
-    mm(R("N1", 0, 256), R("Sel0f"), R("ce"), False, True)
-    send(R("zo1"), R("zC"), nxt)
-    expand("zx0", "zo1", 4)
-    tolist("K1", "vlB", 0.0)
-    onehots(8, 16)
-    counts("Q1")
-    turn0()
+    for h in range(2):
+        minus_zT("zA", h)
+    visit(0, "vlA", None, "v1o0", "v2o0", "xo0", "zB", "LB", "zx0", ("v1i0", "v2i0", "xi0"))
+    for h in range(2):
+        decide(0, h, "zB", "LB", "xi0", R("zo1", *hn(h)), R("Lo1", *hn(h)))
+        send(R("zo1", *hn(h)), R("zC", *hn(h)), nxt)
+        minus_zT("zo1", h)
+        send(R("Lo1", *hn(h)), R("LC", *hn(h)), nxt)
+    act(R("m0"), R("M", 384, 512), AF.Sign)
+    act(R("Sb"), R("M", 384, 512), AF.Copy)
+    for h in range(2):
+        turn(h)
+    tt(R("ya1"), R("M", 128, 256), R("m0"), MU)
+    tt(R("ya2"), R("M", 256, 384), R("m0"), MU)
+    tt(R("M", 0, 128), R("M", 0, 128), R("ya1"), AD)
+    tt(R("M", 128, 256), R("M", 128, 256), R("ya2"), AD)
 
-    visit(1, "vlB", "v1o1", "v2o1", "xo1", "el2", "zC", "LC", ("v1i1", "v2i1", "xi1"))
-    decide(1, "zo2")
-    send(R("zo2"), R("zF"), home)
-    send(R("Lo2"), R("LF"), home)
-    send(R("vo2"), R("vF"), home)
-    onehots(2, 16)
-    counts("K0")
-    for k in range(2):
-        ts(R("ya1"), R("e%dr" % k), 16.0, MU)
-        tt(R("dy%d" % k), R("ya1"), R("s01", 128, 256), SU)
-    ts(R("m1"), R("K0", 0, 128), 0.0, GT)
-    tt(R("ya2"), R("m0"), R("m1"), MX)
-    tt(R("ya3"), R("m0"), R("m1"), MU)
-    tt(R("ya4"), R("ya2"), R("dy0"), MU)
-    tt(R("ya5"), R("ya3"), R("dy1"), MU)
-    tt(R("ya1"), R("ya4"), R("ya5"), AD)
-    tt(R("yas"), R("ya1"), R("s01", 0, 128), AD)
-    dma("Y", T.ya[:], ap(R("yas")), [R("yas")], [])
-    act(R("yzs"), R("zF"), AF.Copy)
-    dma("S", T.yz[:], ap(R("yzs")), [R("yzs")], [])
-    cp(R("yls"), R("LF"))
-    dma("Y", T.yl[:], ap(R("yls")), [R("yls")], [])
-    mm(R("Q0", 0, 128, 1, 16), R("vF"), R("If"))
-    cp(R("yvs", 0, 128, 1, 16), R("Q0", 0, 128, 1, 16))
-    nv, at = PLACE["yvs"]
-    s = dma("Y", T.yv[:, 0:128], T[nv][0:8, at:at + 128], [R("yvs")], [])
-    dma("Y", T.yv[:, 128:256], T[nv][8:16, at:at + 128], [R("yvs")], [], s)
+    visit(1, "vlB", "loB", "v1o1", "v2o1", "xo1", "zC", "LC", "zx1", ("v1i1", "v2i1", "xi1"))
+    for h in range(2):
+        fo, fi, kb = "fo%d" % h, "fi%d" % h, "K%d" % h
+        decide(1, h, "zC", "LC", "xi1", R(fo, 0, 128), R(fo, 128, 256))
+        send(R(fo), R(fi), home)
+    act(R("m1"), R("M", 384, 512), AF.Sign)
+    tt(R("ya1"), R("M", 128, 256), R("m1"), MU)
+    tt(R("yas"), R("M", 0, 128), R("ya1"), AD)
+    dma("Y", T.ya[:], ap(R("yas")), [R("yas")], [], 1 << 16, chain=False)
+    for h in range(2):
+        fi, kb = "fi%d" % h, "K%d" % h
+        a, b = hn(h)
+        dma("Y", T.yz[:, a:b], ap(R(fi, 0, 128)), [R(fi, 0, 128)], [], 1 << 16, chain=False)
+        dma("S", T.yl[:, a:b], ap(R(fi, 128, 256)), [R(fi, 128, 256)], [], 1 << 16, chain=False)
+        mm(R(kb, 384, 512, 1, (0, 8)), R(fi, 256, 264), If)
+        cp(R("yvs", a, b, 1, (0, 8)), R(kb, 384, 512, 1, (0, 8)))
+        dma("Y", T.yv[:, a:b], ap(R("yvs", a, b, 1, (0, 8))), [R("yvs", a, b)], [], 1 << 12, chain=False)
+
+    nop = len(ops)
+    for o in ops:
+        if o["q"] == "T":
+            same = {d for d in o["deps"] if ops[d]["q"] == "T"}
+            o["deps"] -= same
+            o["order"] |= same
+    prio = [0.0] * nop
+    for i in range(nop - 1, -1, -1):
+        o = ops[i]
+        prio[i] += o["cost"] + o["lat"] + (1.8 if o["kind"] == "dma" else 0)
+        for d in o["deps"] | o["order"] | o["soft"]:
+            prio[d] = max(prio[d], prio[i] + WAKE)
+    for i, o in enumerate(ops):
+        prio[i] -= OPT["short"] * o["cost"]
+    users = [[] for _ in ops]
+    left = [0] * nop
+    for i, o in enumerate(ops):
+        for d in o["deps"] | o["order"]:
+            users[d].append(i)
+            left[i] += 1
+    cand = {q: [] for q in "VSTGYA"}
+    for i in range(nop):
+        ops[i].setdefault("alt", {ops[i]["q"]: (ops[i]["fn"], ops[i]["cost"])})
+        if left[i] == 0:
+            for q in ops[i]["alt"]:
+                cand[q].append(i)
+    free = {q: 0.0 for q in cand}
+    fin, issued, ready = [0.0] * nop, [0.0] * nop, [0.0] * nop
+    lastin = {b: {} for b in PS}
+    opened = {}
+    engines = [0.0]
+    order = []
+    while len(order) < nop:
+        best = None
+        for q, lst in cand.items():
+            at = []
+            for i in lst:
+                o = ops[i]
+                if o["grp"] and o["grp"][1] and opened.get(o["grp"][0]):
+                    continue
+                r = ready[i]
+                for b in o["banks"]:
+                    for q2, j in lastin[b].items():
+                        if q2 != q:
+                            r = max(r, fin[j] + WAKE)
+                at.append((max(r, free[q]) if q != "A" else r, i))
+            if not at:
+                continue
+            t0 = min(at)[0]
+            pick = max((x for x in at if x[0] <= t0 + 1e-9), key=lambda x: prio[x[1]])
+            for x in at:
+                if prio[x[1]] > prio[pick[1]] and x[0] <= t0 + OPT["look"] * ops[pick[1]]["alt"][q][1]:
+                    pick = x
+            if best is None or pick[0] < best[0] - 1e-9 or (pick[1] == best[1] and pick[0] < best[0] + 1e-9 and q == ops[pick[1]]["q"]):
+                best = pick + (q,)
+        start, i, q = best
+        o = ops[i]
+        for q2 in o["alt"]:
+            cand[q2].remove(i)
+        o["q"] = q
+        o["fn"], o["cost"] = o["alt"][q]
+        order.append(i)
+        free[q] = issued[i] = start + o["cost"]
+        if o["kind"] == "dma":
+            engines[0] = fin[i] = max(free[q] + 1.8, engines[0]) + o["lat"]
+        else:
+            fin[i] = free[q] + o["lat"]
+        for b in o["banks"]:
+            o["deps"] |= {j for q2, j in lastin[b].items() if q2 != q}
+            lastin[b][q] = i
+        if o["grp"]:
+            opened[o["grp"][0]] = not o["grp"][2]
+        for u in users[i]:
+            if i in ops[u]["deps"] or ops[u]["kind"] == "land":
+                ready[u] = max(ready[u], fin[i] + WAKE)
+            else:
+                ready[u] = max(ready[u], issued[i])
+            left[u] -= 1
+            if left[u] == 0:
+                for q2 in ops[u]["alt"]:
+                    cand[q2].append(u)
+
+    total = {}
+    for o in ops:
+        if o["kind"] == "dma":
+            total[o["sem"]] = total.get(o["sem"], 0) + 16
+    count, tok = {}, {}
+    known = {q: {} for q in QS}
+    for i in order:
+        o = ops[i]
+        q = o["q"]
+        s = o["sem"] or "c" + q
+        count[s] = count.get(s, 0) + o["inc"]
+        v = total[s] if o["kind"] == "dma" else count[s]
+        if o["kind"] == "land":
+            tok[i] = (s, v, {})
+            continue
+        kn = known[q]
+        want = {}
+        for d in o["deps"]:
+            if kn.get(tok[d][0], 0) < tok[d][1]:
+                want[tok[d][0]] = max(want.get(tok[d][0], 0), tok[d][1])
+        for s1 in list(want):
+            for d in o["deps"]:
+                s2 = tok[d][0]
+                if s2 != s1 and s2 in want and tok[d][2].get(s1, 0) >= want[s1]:
+                    want.pop(s1)
+                    break
+        for s1, v1 in want.items():
+            QS[q].wait_ge(T.sem[s1], v1)
+        for d in o["deps"]:
+            for s1, v1 in list(tok[d][2].items()) + [tok[d][:2]]:
+                kn[s1] = max(kn.get(s1, 0), v1)
+        call = o["fn"]()
+        if o["kind"] != "send":
+            call.then_inc(T.sem[s], o["inc"])
+        tok[i] = (s, v, dict(kn))
     for s, v in count.items():
         if known["G"].get(s, 0) < v:
             g.wait_ge(T.sem[s], v)

@@ -4,26 +4,26 @@ from concourse.mybir import AluOpType as OP, ActivationFunctionType as AF
 F, B, I, U, H = "float32", "bfloat16", "int32", "uint16", "float16"
 SB = {
     "I16": (128, H), "B8h": (8, H), "gm32": (256, F), "zw": (4096, B), "sh": (4096, B), "so": (4096, B), "zT2": (256, B),
-    "eS": (2048, I), "xS": (2048, B), "zA": (256, B), "LA": (256, I), "vA": (16, I), "ef": (2176, F),
-    "t0": (128, I), "t1": (128, I), "tf": (256, H), "el": (256, U), "ys": (384, F),
+    "eS": (2176, I), "xS": (2048, B), "zA": (256, B), "LA": (256, I), "vA": (16, I), "ef": (2048, H),
+    "t0": (512, I), "tf": (512, H), "el": (256, U), "ys": (384, F),
     "iC": (8, I), "iN": (32, I), "zl": (32, U), "col": (48, F), "iD": (128, B), "gp": (16, B), "kk": (256, B), "ck": (256, B),
     "KLc": (128, B), "io": (144, B), "g16": (8, B), "mg": (128, B), "e32": (512, B), "EXP": (512, B), "io2k": (2176, F),
     "ones": (128, B), "cq": (256, B), "c175": (256, B), "wrow": (256, F), "maskJ": (256, B), "IM": (768, B), "If": (128, F),
     "RST": (256, B), "RSD": (128, F), "W16": (16, B), "B8": (16, B), "W8": (16, B), "B8f": (16, F), "BB4": (128, B),
-    "SelC": (32, F), "WY": (24, F), "Z2": (144, B),
+    "SelC": (32, H), "WY": (24, H), "B128": (8, B), "B8i": (8, H),
     "XB": (2048, B), "HI": (2176, B), "LO": (2176, B), "m0": (128, B), "Sb": (128, B), "m1": (128, B),
     "zT": (256, B), "xg": (4096, B), "ab": (4096, B), "c16": (256, U), "cf": (256, H), "H": (256, B), "ad": (256, B),
     "mk": (256, B), "R": (512, F), "wi": (32, I), "wa": (32, I), "wb": (32, B), "wT": (512, B),
     "vlA": (16, U), "v1o0": (16, U), "v2o0": (16, U), "v1o1": (16, U), "v2o1": (16, U), "vlB": (16, U), "loB": (16, U),
     "lo1": (16, U), "vi": (32, I), "xo0": (256, B), "xo1": (256, B),
     "zx0": (4096, B), "zx1": (4096, B), "mh": (4096, B), "ml": (4096, B), "eh": (512, B), "en": (512, B), "Lf": (256, H),
-    "r1": (256, F), "r2": (256, F), "ab2": (256, B), "hb": (256, B), "sl": (256, B), "tl": (256, B), "sc": (256, B),
-    "w": (256, B), "fk": (256, B), "R2": (256, F), "flag": (256, B), "e2": (256, H), "NP": (128, H), "ce": (256, F),
+    "r1": (256, H), "r2": (256, H), "ab2": (256, B), "hb": (256, B), "sl": (256, B), "tl": (256, B), "sc": (256, B),
+    "w": (256, B), "fk": (256, B), "R2": (256, F), "flag": (256, B), "e2": (256, H), "NP": (128, H), "ce": (256, H),
     "qs": (256, F), "qi": (128, I), "qb": (96, B), "ul": (16, U), "ulo": (16, U), "OH": (4096, B), "gm": (768, H),
     "adu": (256, B), "ad2": (256, B), "mn": (256, B), "e12": (32, U), "u2": (16, U), "nB": (256, B), "nH": (256, B),
-    "nL": (256, B), "Lo0": (256, U), "zo1": (256, B), "Lo1": (256, U), "fo0": (264, F), "fo1": (264, F),
+    "nL": (256, B), "Lo0": (256, U), "zo1": (256, B), "Lo1": (256, U), "fo0": (264, H), "fo1": (264, H), "out": (512, F),
     "zB": (256, B), "LB": (256, U), "v1i0": (16, U), "v2i0": (16, U), "xi0": (256, B), "zC": (256, B), "LC": (256, U),
-    "v1i1": (16, U), "v2i1": (16, U), "xi1": (256, B), "fi0": (264, F), "fi1": (264, F),
+    "v1i1": (16, U), "v2i1": (16, U), "xi1": (256, B), "fi0": (264, H), "fi1": (264, H),
     "yvs": (256, F), "ya1": (128, F), "ya2": (128, F), "yas": (128, F),
 }
 PS = {"P0": 512, "P1": 512, "K0": 512, "K1": 512, "N0": 512, "N1": 512, "G": 512, "M": 512}
@@ -42,8 +42,9 @@ for _d in _use:
 for _n, _w in PS.items():
     SCRATCH[_n] = ("psum", [128, _w], "float32")
 SEMAPHORES = ["cV", "cS", "cT", "cG"] + ["d%d" % i for i in range(30)] + ["a%d" % i for i in range(30)] + ["l%d" % i for i in range(30)]
-OPT = {"tch": 512, "look": 0.5, "ef": "G", "exp": ("SG", "GS"), "load": ("z1Lv", "X0E"),
-       "xg": "S", "sm": "SV", "expw": ("GS", "GS"), "B": "S", "vx": ((1, 1), (0, 0)), "gS": ((0, 0), (0, 1)), "short": 0.0}
+OPT = {"tch": 512, "look": 0.5, "ef": "G", "exp": ("SG", "GS"), "load": ("0zv", "1XLE"), "ahead": 2, "short": 0, "cyT": 0.56e-3,
+       "xg": (("S", "S"), ("S", "S")), "sm": "SV", "expw": ("GS", "GS"), "B": "S", "vx": ((1, 1), (0, 1)), "gS": ((0, 1), (1, 2)), "rounds": 8, "mix": 1.0}
+PLAN = {}
 
 
 def rank_program(g, core, T, topo):
@@ -62,7 +63,7 @@ def rank_program(g, core, T, topo):
 
     def track(name):
         if name not in hist:
-            hist[name] = {"w": np.full(SB[name][0] if name in SB else PS[name], -1), "r": {}}
+            hist[name] = {"w": np.full(SB[name][0] if name in SB else 512, -1), "r": {}}
         return hist[name]
 
     def record(q, reads, writes, fn, cost, kind="op", lat=0.0, grp=None, after=(), sem=None, inc=1):
@@ -84,12 +85,13 @@ def rank_program(g, core, T, topo):
             h = track(r[0])
             h["r"].setdefault(me, np.zeros(len(h["w"]), bool))[r[1]:r[2]:r[3]] = True
         ops.append({"q": q, "fn": fn, "cost": cost, "kind": kind, "lat": lat, "deps": deps, "order": set(after), "grp": grp,
-                    "banks": set(r[0] for r in reads + writes if r[0] in PS), "sem": sem, "inc": inc, "soft": set()})
+                    "banks": set(r[0] for r in reads + writes if r[0] in PS), "sem": sem, "inc": inc, "soft": set(),
+                    "name": (writes + reads)[0][:2]})
         return me
 
     def R(name, a=0, b=None, st=1, p=None):
         if b is None:
-            b = SB[name][0] if name in SB else PS[name]
+            b = SB[name][0] if name in SB else 512
         return (name, a, b, st, p)
 
     def IND(win, off):
@@ -99,6 +101,8 @@ def rank_program(g, core, T, topo):
         if r[0] == "ind":
             return ap(r[1]).indirect(ap(r[2]))
         n, a, b, st, p = r
+        if "#" in n:
+            n = PLAN["plan"][5][n]
         if n in PLACE:
             n, at = PLACE[n]
             a, b = a + at, b + at
@@ -167,7 +171,7 @@ def rank_program(g, core, T, topo):
     def mm(out, l, r, start=True, stop=True, after=()):
         bank = out[0]
         prev = list(after) if start else [group[bank]]
-        cost = max(min(64, size(l)), size(r)) * (4 if SB[l[0]][1] == F else 1) * CY / 2 + 0.004
+        cost = max(min(64, size(l)), size(r)) * (4 if SB[l[0]][1] == F else 1) * OPT["cyT"]
         group[bank] = do("T", [l, r], out, lambda: g.tensor.matmul(ap(out), ap(l), ap(r), start, stop), 1, cost=cost,
                          grp=(bank, start, stop), after=prev)
         return group[bank]
@@ -183,18 +187,16 @@ def rank_program(g, core, T, topo):
         return do("G", [a], out, lambda: g.affine_select(ap(out), ap(a), [[0, n]], OP.is_ge, 0.0, 0, 0), 1, cost=0.17 + 2 * n * CY)
 
     def copy(out, a, qs, scale=None):
+        ways = {"G": lambda: gcopy(out, a), "S": lambda: act(out, a, AF.Copy, None, scale),
+                "V": lambda: cp(out, a) if scale is None else ts(out, a, scale, OP.mult)}
+        return either(*[ways[q] for q in qs])
+
+    def either(*ways):
         first = len(ops)
         alt = {}
-        for q in qs:
-            if q == "G":
-                gcopy(out, a)
-            elif q == "S":
-                act(out, a, AF.Copy, None, scale)
-            elif scale is None:
-                cp(out, a)
-            else:
-                ts(out, a, scale, OP.mult)
-            alt[q] = (ops[-1]["fn"], ops[-1]["cost"])
+        for way in ways:
+            way()
+            alt[ops[-1]["q"]] = (ops[-1]["fn"], ops[-1]["cost"])
             if len(ops) > first + 1:
                 for h in hist.values():
                     h["w"][h["w"] == first + 1] = first
@@ -248,14 +250,15 @@ def rank_program(g, core, T, topo):
 
     def edges(k, q):
         s = newsem()
-        for gg in range(8):
-            c = R("t%d" % k, 16 * gg, 16 * gg + 16)
-            dma(q, ap(c), T.E[16 * gg + k, :], [], [c], 50000, s)
+        for gg in range(4 * k, 4 * k + 4):
+            c = R("t0", 64 * gg, 64 * gg + 64, 1, (0, 64))
+            dma(q, ap(c), T.E[16 * gg:16 * gg + 2, :], [], [c], 38000, s)
     whole = {"z": ("zA", T.z0, 100000), "L": ("LA", T.L0, 170000), "v": ("vA", T.v0, 50000), "X": ("xS", T.X, 560000), "E": ("eS", T.E, 1090000)}
     for q, names in zip("SY", OPT["load"]):
         for c in names:
             if c in whole:
-                dma(q, ap(R(whole[c][0])), whole[c][1][:], [], [R(whole[c][0])], whole[c][2])
+                to = R(whole[c][0], 0, whole[c][1].shape[1])
+                dma(q, ap(to), whole[c][1][:], [], [to], whole[c][2])
             else:
                 edges(int(c), q)
 
@@ -286,8 +289,6 @@ def rank_program(g, core, T, topo):
     ts(C(20), PK, 1.0, MU, 0.5, AD)
     ts(C(21), PK, -1.0, MU, -0.5, AD)
     ts(C(22), PK, -2.0, MU, -63.5 / 64, AD)
-    ts(C(23), P7, 16.0, MU, 16.0, AD)
-    ts(C(24), KY, -127.0, MU, 128.0, AD)
     ts(C(25), PP, 2048.0, AD)
     ts(C(26), PP, 65536.0 + 2048.0, AD)
     ts(C(27), PK, 2048.0, AD)
@@ -309,13 +310,13 @@ def rank_program(g, core, T, topo):
     ts(R("RST"), R("kk"), 0.0, EQ, 33554432.0, MU)
     ts(R("RSD"), R("kk", 0, 128), 0.0, EQ, C(26), MU)
     ts(R("maskJ"), R("kk"), PK, EQ)
-    ts(R("Z2"), R("io"), C(23), EQ, C(24), MU)
+    ts(R("B128"), R("gp", 0, 8), PG, EQ, 128.0, MU)
     I16 = R("I16")
     ts(I16, R("iD"), 0.0, EQ)
     ts(R("B8h"), R("gp", 0, 8), PG, EQ)
     ts(R("BB4"), R("mg"), PG, EQ, 4096.0, MU)
     for out, c in ((R("B8", 0, 8), 1.0), (R("B8", 8, 16), -1.0), (R("W8", 0, 8), C(20)), (R("W8", 8, 16), C(21)),
-                   (R("B8f", 0, 8), 1.0), (R("B8f", 8, 16), 0.5), (R("SelC", 0, 8), C(31)), (R("SelC", 8, 16), C(8)),
+                   (R("B8f", 0, 8), 1.0), (R("B8i"), 0.5), (R("SelC", 0, 8), C(31)), (R("SelC", 8, 16), C(8)),
                    (R("SelC", 16, 24), C(9)), (R("SelC", 24, 32), C(10)), (R("WY", 0, 8), C(28)), (R("WY", 8, 16), C(29)),
                    (R("WY", 16, 24), C(30))):
         ts(out, R("gp", 0, 8), PG, EQ, c, MU)
@@ -330,21 +331,22 @@ def rank_program(g, core, T, topo):
     send(R("zA"), R("zB"), nxt)
     cp(R("Lo0"), R("LA"))
     send(R("Lo0"), R("LB"), nxt)
-    for k in (1, 0):
-        cp(R("tf", *hn(k)), R("t%d" % k))
-        mm(R("N0", *hn(k)), R("tf", *hn(k)), I16)
-        cp(R("el", *hn(k)), R("N0", *hn(k)))
-    w = OPT["tch"]
+    for k in range(2):
+        cp(R("tf", 256 * k, 256 * k + 256, 1, (0, 64)), R("t0", 256 * k, 256 * k + 256, 1, (0, 64)))
     ids = []
-    for c in range(0, 2048, w):
-        copy(R("XB", c, c + w), IND(R("xS"), R("el", 128 + c // 16, 128 + (c + w) // 16)), OPT["B"])
+    for b in range(4):
+        mm(R("N0", 64 * b, 64 * b + 64), R("tf", b, 512, 4, (0, 64)), R("I16", 0, 64, 1, (0, 64)))
+    cp(R("el"), R("N0", 0, 256))
+    for b in range(4):
+        c = R("XB", 512 * b, 512 * b + 512)
+        copy(c, IND(R("xS"), R("el", 64 * b + 32, 64 * b + 64)), OPT["B"])
         for tab, op in (("HI", MX), ("LO", MN)):
-            ids.append(tt(R(tab, c, c + w), IND(R("xS"), R("el", c // 16, (c + w) // 16)), R("XB", c, c + w), op))
+            ids.append(tt(R(tab, b, 2048, 4), IND(R("xS"), R("el", 64 * b, 64 * b + 32)), c, op))
     chain(ids)
     chain([copy(R("ef", c, c + 256), R("eS", c, c + 256), OPT["ef"]) for c in range(0, 2048, 256)])
     for hi in range(16):
         mm(R("M", hi, 384, 16), R("ef", 128 * hi, 128 * hi + 128), R("WY"))
-    act(R("ys"), R("M", 0, 384), AF.Copy)
+    copy(R("ys"), R("M", 0, 384), "SV")
     for j in range(3):
         mm(R("M", *hn(j)), R("ys", *hn(j)), If)
 
@@ -368,15 +370,13 @@ def rank_program(g, core, T, topo):
 
     def tolist(h, parts, out, add, lo=None):
         kb = "K%d" % h
-        P16, a, n = (0, 16), 256 * h, 2 if lo else 1
-        mm(R(kb, 384, 512, 1, P16), parts, Ib)
-        copy(R("wT", a, a + 128, 1, P16), R(kb, 384, 512, 1, P16), OPT["sm"])
-        if lo:
-            copy(R("wT", a + 128, a + 256, 1, P16), R(kb, 384, 512, 1, P16), OPT["sm"], R("col", 4, 5, 1, P16))
-        for j in range(16):
-            mm(R(kb, 256, 256 + 8 * n), R("Z2", 16 - j, 144 - j, 1, P16), R("wT", a + j, a + 128 * n, 16, P16), j == 0, j == 15)
+        a = 256 * h
+        tt(R("wT", a, a + 256), IND(parts, R("zl", 0, 16)), R("maskJ"), MU)
+        mm(R(kb, 256, 264), R("wT", a, a + 128), R("B128"), True, False)
+        mm(R(kb, 256, 264), R("wT", a + 128, a + 256), B8p, False, True)
         ts(R(out, *hm(h)), R(kb, 256, 264), add, AD)
         if lo:
+            mm(R(kb, 264, 272), R("wT", a + 128, a + 256), B8p)
             cp(R(lo, *hm(h)), R(kb, 264, 272))
 
     def masked(h, win, at, slot, n=1, base=False):
@@ -389,19 +389,27 @@ def rank_program(g, core, T, topo):
                 mm(o, R("ones", p=ROW), R("g16", p=ROW), False, True)
 
     def minus_z(src, b, zT, f, dst):
-        bank = "P%d" % (pb[0] % 2)
+        bank = "P#%d" % pb[0]
         pb[0] += 1
         q, n = 32 * (b // 512 % 4), hn(b // 2048)
-        mm(R(bank), Ib, src, True, False)
-        mm(R(bank), R(zT, *n, 1, (q, q + 32)), R("EXP", p=(q, q + 32)), False, True)
-        act(dst, R(bank), f)
+        first = mm(R(bank), Ib, src, True, False, pb[1:] if zT == "zT" else ())
+        ops[first]["take"] = bank
+        if zT == "zT":
+            pb[1:] = [first]
+        second = mm(R(bank), R(zT, *n, 1, (q, q + 32)), R("EXP", p=(q, q + 32)), False, True)
+        ops[first]["deps"] |= ops[second]["deps"] - {first}
+        last = act(dst, R(bank), f)
+        ops[last]["give"] = bank
+        return last
 
     def apart(out, lst):
         act(out, IND(R("io2k"), lst), AF.Abs, C(22), 1.0 / 64)
 
+    behind = []
+
     def walk(t, step, h, vl, lo, out, outlo):
         n, m, kb = hn(h), hm(h), "K%d" % h
-        cp(R("c16", *n), IND(R("eS"), R(vl, *m)))
+        cp(R("c16", *n), IND(R("eS", 0, 2048), R(vl, *m)))
         ts(R("cf", *n), R("c16", *n), 0.0, AD)
         ts(R("H", *n), R("c16", *n), 16448.5, AD)
         onV = OPT["vx"][t][step]
@@ -409,8 +417,9 @@ def rank_program(g, core, T, topo):
             b = 2048 * h + 512 * j
             x = IND(R("xS"), R("c16", b // 16, b // 16 + 32))
             if j < 4 - onV:
-                copy(R("xg", b, b + 512), x, OPT["xg"])
-                minus_z(R("xg", b, b + 512), b, "zT", AF.Abs, R("ab", b, b + 512))
+                i = copy(R("xg", b, b + 512), x, OPT["xg"][t][step])
+                ops[i]["order" if OPT["xg"][t][step] == "S" else "deps"].update(behind[-OPT["ahead"]:][:1])
+                behind.append(minus_z(R("xg", b, b + 512), b, "zT", AF.Abs, R("ab", b, b + 512)))
             else:
                 tt(R("xg", b, b + 512), x, R("zw", b, b + 512), SU)
                 act(R("ab", b, b + 512), R("xg", b, b + 512), AF.Abs)
@@ -428,8 +437,7 @@ def rank_program(g, core, T, topo):
         a = (16 * h, 16 * h + 16)
         cp(R("wi", *a), R("R", 256 * h + 15, 256 * h + 256, 16))
         ts(R("wa", *a), R("wi", *a), 127, AN)
-        cp(R("wb", *a), R("wa", *a))
-        tolist(h, R("wb", *a), out, -128.0, outlo)
+        tolist(h, R("wa", *a), out, -128.0, outlo)
 
     gaps = []
 
@@ -460,7 +468,7 @@ def rank_program(g, core, T, topo):
         o = R("G", 128 * h + 2 * t + e, 128 * h + 128, 16)
         mm(o, R("eh", *a), B8p, True, False)
         mm(o, R("en", *a), B8n, False, True)
-        act(R("r%d" % (e + 1), *hn(h)), IND(R("io2k"), R(vl, *hm(h))), AF.Copy, None, C(8 + 2 * t + e))
+        copy(R("r%d" % (e + 1), *hn(h)), IND(R("io2k"), R(vl, *hm(h))), "V", C(8 + 2 * t + e))
 
     def decide(t, h, z, L16, xi, zo, Lo):
         n, m, kb, nb = hn(h), hm(h), "K%d" % h, "N%d" % h
@@ -489,36 +497,37 @@ def rank_program(g, core, T, topo):
         mm(s0, R("BB4"), ab)
         act(sl, s0, AF.Sign, TH + 0.5, -1.0 / 4096)
         mm(R(nb, 256, 264), ab, B8p)
-        acc(R(nb, 264, 272), [(hb, R("W8", 8, 16)), (r2, R("B8f", 8, 16))])
-        acc(R(nb, 272, 280), [(hb, R("W8", 0, 8)), (r2, R("B8f", 8, 16))])
+        acc(R(nb, 264, 272), [(hb, R("W8", 8, 16)), (r2, R("B8i"))])
+        acc(R(nb, 272, 280), [(hb, R("W8", 0, 8)), (r2, R("B8i"))])
         act(Q(0), R(nb, 256, 264), AF.Sign, TH + 0.5, -1.0)
         tt(Q(1), R(nb, 264, 272), Q(0), MU)
         tt(QI(0), R(nb, 272, 280), Q(1), AD)
         ts(QI(1), QI(0), 2047, AN)
         cp(R("NP", 0, 128, 16), QI(1))
         early = [mm(s3, R("NP"), I16)]
-        act(R("ef", 2048, 2176), s3, AF.Copy)
+        cp(R("eS", 2048, 2176), s3)
         acc(s1, [(Ib, ab), (nI, hb)])
         tt(tl, s1, sl, MU)
         early.append(acc(s0, [(nIh, tl), (Ib, zz), (nIh, ab), (nIh, hb)]))
-        act(R("fk", *n), R("G", *n), AF.Relu, 262144.0 * (TAU[t] + 0.5), -262144.0)
+        either(lambda: act(R("fk", *n), R("G", *n), AF.Relu, 262144.0 * (TAU[t] + 0.5), -262144.0),
+               lambda: ts(R("fk", *n), R("G", *n), float(TAU[t]), LE, 131072.0, MU))
         key = R(kb, 0, 128)
-        acc(key, [(r2, If), (R("ones", p=ROW), R("KLc", p=ROW)), (Lf, I16), (r1, If), (sl, R("BB4")), (Ib, R("fk", *n))])
+        acc(key, [(r2, I16), (R("ones", p=ROW), R("KLc", p=ROW)), (Lf, I16), (r1, I16), (sl, R("BB4")), (Ib, R("fk", *n))])
         scan(R("R2", *n), R("RSD"), key, 0.0, MX, MN)
         end = R("R2", 128 * h + 15, 128 * h + 128, 16)
         cp(QI(2), end)
         ts(QI(3), QI(2), 7, SH, 31, AN)
         ts(QI(4), QI(2), 127, AN)
         cp(QB(0, 16), QI(3, 16))
-        tolist(h, QB(0, 16), "ul", 0.0, "ulo")
+        tolist(h, QI(3, 16), "ul", 0.0, "ulo")
         ul, ce = R("ul", *m), R("ce", *n)
-        act(ce, IND(R("ef"), ul), AF.Copy)
+        cp(ce, IND(R("eS"), ul))
         act(R("sc", *n), IND(R("io2k"), ul), AF.Sign, 2047.5, -1.0)
         tt(R("flag", *n), key, R("R2", *n), EQ)
         apart(R("adu", *n), ul)
         if t == 0:
             mm(R(kb, 128, 152), ce, R("SelC", 8, 32))
-            act(Q(2, 24), R(kb, 128, 152), AF.Copy)
+            copy(Q(2, 24), R(kb, 128, 152), "SV")
             vo = Q(2)
             masked(h, vo, 384 * h, 272)
             ts(R("vlB", *m), R(kb, 272, 280), 0.0, AD)
@@ -529,17 +538,17 @@ def rank_program(g, core, T, topo):
             tt(R("mn", *n), IND(R("m0"), R("ulo", *m)), R("adu", *n), GT)
             mm(R(kb, 128, 144), ce, R("SelC", 0, 16))
             mm(R(kb, 152, 160), R("mn", *n), B8p)
-            act(Q(2), R(kb, 152, 160), AF.Copy)
+            copy(Q(2), R(kb, 152, 160), "SV")
             tt(Q(3), R(kb, 128, 136), Q(2), MU)
             vo = R("fo%d" % h, 256, 264)
             tt(vo, R(kb, 136, 144), Q(3), AD)
         tt(R("w", *n), s0, R("sc", *n), MU)
         acc(s1, [(Ih, zz), (Iq, ab), (Iq, hb), (Iq, tl), (Ih, R("w", *n))], early)
-        act(zo, s1, AF.Copy)
+        copy(zo, s1, "V" if t else "SV")
         ts(QI(5), QI(2), 4095, AN)
         tt(Q(5), vo, QI(5), SU)
         tt(R("e2", *n), IND(Q(5), R("zl", 0, 8)), R("flag", *n), MU)
-        acc(s3, [(R("e2", *n), I16), (I16, Lf), (If, r1), (If, r2)])
+        acc(s3, [(R("e2", *n), I16), (I16, Lf), (I16, r1), (I16, r2)])
         cp(Lo, s3)
         tt(QB(2), QB(0), R("g16"), AD)
         ts(QB(3), end, 65536.0, LT, C(32 + h) if t == 0 else 1.0, MU)
@@ -553,10 +562,11 @@ def rank_program(g, core, T, topo):
         if t == 0:
             masked(h, Q(3, 16), 384 * h + 128, 280, 2)
             ts(R("e12", 16 * h, 16 * h + 16), R(kb, 280, 296), 0.0, AD)
-            act(R("nB", *n), IND(R("xS"), R("e12", 16 * h + 8, 16 * h + 16)), AF.Copy)
+            copy(R("nB", *n), IND(R("xS"), R("e12", 16 * h + 8, 16 * h + 16)), "SV")
             tt(R("nH", *n), IND(R("xS"), R("e12", 16 * h, 16 * h + 8)), R("nB", *n), MX)
             tt(R("nL", *n), IND(R("xS"), R("e12", 16 * h, 16 * h + 8)), R("nB", *n), MN)
-            act(R("ad2", *n), R("adu", *n), AF.Relu, 9e29, -9e29)
+            either(lambda: act(R("ad2", *n), R("adu", *n), AF.Relu, 9e29, -9e29),
+                   lambda: ts(R("ad2", *n), R("adu", *n), 1.0, LT, 9e29, MU))
             ts(Q(6), QI(5), C(25), SU)
 
     def turn(h):
@@ -579,7 +589,7 @@ def rank_program(g, core, T, topo):
         for h in range(2):
             walk(t, 1, h, v1, "lo1", v2, None)
             send(R(v2, *hm(h)), R(ini[1], *hm(h)), nxt)
-            act(R(xo, *hn(h)), IND(R("xS"), R(v2, *hm(h))), AF.Copy)
+            copy(R(xo, *hn(h)), IND(R("xS"), R(v2, *hm(h))), "SV")
             send(R(xo, *hn(h)), R(ini[2], *hn(h)), nxt)
         del gaps[:]
         for h in range(2):
@@ -597,8 +607,10 @@ def rank_program(g, core, T, topo):
         send(R("zo1", *hn(h)), R("zC", *hn(h)), nxt)
         minus_zT("zo1", h)
         send(R("Lo1", *hn(h)), R("LC", *hn(h)), nxt)
-    act(R("m0"), R("M", 384, 512), AF.Sign)
-    act(R("Sb"), R("M", 384, 512), AF.Copy)
+    def counted(out):
+        either(lambda: act(R(out), R("M", 384, 512), AF.Sign), lambda: ts(R(out), R("M", 384, 512), 0.0, GT))
+    counted("m0")
+    copy(R("Sb"), R("M", 384, 512), "SV")
     for h in range(2):
         turn(h)
     tt(R("ya1"), R("M", 128, 256), R("m0"), MU)
@@ -611,17 +623,19 @@ def rank_program(g, core, T, topo):
         fo, fi, kb = "fo%d" % h, "fi%d" % h, "K%d" % h
         decide(1, h, "zC", "LC", "xi1", R(fo, 0, 128), R(fo, 128, 256))
         send(R(fo), R(fi), home)
-    act(R("m1"), R("M", 384, 512), AF.Sign)
+    counted("m1")
     tt(R("ya1"), R("M", 128, 256), R("m1"), MU)
     tt(R("yas"), R("M", 0, 128), R("ya1"), AD)
     dma("Y", T.ya[:], ap(R("yas")), [R("yas")], [], 1 << 16, chain=False)
     for h in range(2):
         fi, kb = "fi%d" % h, "K%d" % h
         a, b = hn(h)
-        dma("Y", T.yz[:, a:b], ap(R(fi, 0, 128)), [R(fi, 0, 128)], [], 1 << 16, chain=False)
-        dma("S", T.yl[:, a:b], ap(R(fi, 128, 256)), [R(fi, 128, 256)], [], 1 << 16, chain=False)
-        mm(R(kb, 384, 512, 1, (0, 8)), R(fi, 256, 264), If)
-        cp(R("yvs", a, b, 1, (0, 8)), R(kb, 384, 512, 1, (0, 8)))
+        oz, ol = R("out", 2 * a, 2 * a + 128), R("out", 2 * a + 128, 2 * b)
+        cp(R("out", 2 * a, 2 * b), R(fi, 0, 256))
+        dma("Y", T.yz[:, a:b], ap(oz), [oz], [], 1 << 16, chain=False)
+        dma("S", T.yl[:, a:b], ap(ol), [ol], [], 1 << 16, chain=False)
+        mm(R(kb, 384, 512, 1, (0, 8)), R(fi, 256, 264), I16)
+        copy(R("yvs", a, b, 1, (0, 8)), R(kb, 384, 512, 1, (0, 8)), "SV")
         dma("Y", T.yv[:, a:b], ap(R("yvs", a, b, 1, (0, 8))), [R("yvs", a, b)], [], 1 << 12, chain=False)
 
     nop = len(ops)
@@ -636,75 +650,121 @@ def rank_program(g, core, T, topo):
         prio[i] += o["cost"] + o["lat"] + (1.8 if o["kind"] == "dma" else 0)
         for d in o["deps"] | o["order"] | o["soft"]:
             prio[d] = max(prio[d], prio[i] + WAKE)
-    for i, o in enumerate(ops):
-        prio[i] -= OPT["short"] * o["cost"]
     users = [[] for _ in ops]
-    left = [0] * nop
     for i, o in enumerate(ops):
+        o.setdefault("alt", {o["q"]: (o["fn"], o["cost"])})
         for d in o["deps"] | o["order"]:
             users[d].append(i)
-            left[i] += 1
-    cand = {q: [] for q in "VSTGYA"}
-    for i in range(nop):
-        ops[i].setdefault("alt", {ops[i]["q"]: (ops[i]["fn"], ops[i]["cost"])})
-        if left[i] == 0:
-            for q in ops[i]["alt"]:
-                cand[q].append(i)
-    free = {q: 0.0 for q in cand}
-    fin, issued, ready = [0.0] * nop, [0.0] * nop, [0.0] * nop
-    lastin = {b: {} for b in PS}
-    opened = {}
-    engines = [0.0]
-    order = []
-    while len(order) < nop:
-        best = None
-        for q, lst in cand.items():
-            at = []
-            for i in lst:
-                o = ops[i]
-                if o["grp"] and o["grp"][1] and opened.get(o["grp"][0]):
+
+    def forward(prio):
+        left = [len(o["deps"] | o["order"]) for o in ops]
+        cand = {q: [i for i in range(nop) if left[i] == 0 and q in ops[i]["alt"]] for q in "VSTGYA"}
+        free = {q: 0.0 for q in cand}
+        fin, ready = [0.0] * nop, [0.0] * nop
+        lastin = {b: {} for b in PS}
+        opened, engines, order, queue, more = {}, 0.0, [], [None] * nop, [None] * nop
+        pool, held = [(0.0, "P0", -1), (0.0, "P1", -1)], {}
+        while len(order) < nop:
+            best = None
+            for q, lst in cand.items():
+                at = []
+                for i in lst:
+                    o = ops[i]
+                    if o["grp"] and o["grp"][1] and opened.get(o["grp"][0]):
+                        continue
+                    r = ready[i]
+                    if "take" in o:
+                        if not pool:
+                            continue
+                        r = max(r, min(pool)[0])
+                    for b in o["banks"]:
+                        for q2, j in lastin[b].items():
+                            if q2 != q:
+                                r = max(r, fin[j] + WAKE)
+                    at.append((max(r, free[q]) if q != "A" else r, i))
+                if not at:
                     continue
-                r = ready[i]
-                for b in o["banks"]:
-                    for q2, j in lastin[b].items():
-                        if q2 != q:
-                            r = max(r, fin[j] + WAKE)
-                at.append((max(r, free[q]) if q != "A" else r, i))
-            if not at:
-                continue
-            t0 = min(at)[0]
-            pick = max((x for x in at if x[0] <= t0 + 1e-9), key=lambda x: prio[x[1]])
-            for x in at:
-                if prio[x[1]] > prio[pick[1]] and x[0] <= t0 + OPT["look"] * ops[pick[1]]["alt"][q][1]:
-                    pick = x
-            if best is None or pick[0] < best[0] - 1e-9 or (pick[1] == best[1] and pick[0] < best[0] + 1e-9 and q == ops[pick[1]]["q"]):
-                best = pick + (q,)
-        start, i, q = best
-        o = ops[i]
-        for q2 in o["alt"]:
-            cand[q2].remove(i)
-        o["q"] = q
-        o["fn"], o["cost"] = o["alt"][q]
-        order.append(i)
-        free[q] = issued[i] = start + o["cost"]
-        if o["kind"] == "dma":
-            engines[0] = fin[i] = max(free[q] + 1.8, engines[0]) + o["lat"]
-        else:
-            fin[i] = free[q] + o["lat"]
-        for b in o["banks"]:
-            o["deps"] |= {j for q2, j in lastin[b].items() if q2 != q}
-            lastin[b][q] = i
-        if o["grp"]:
-            opened[o["grp"][0]] = not o["grp"][2]
-        for u in users[i]:
-            if i in ops[u]["deps"] or ops[u]["kind"] == "land":
-                ready[u] = max(ready[u], fin[i] + WAKE)
+                t0 = min(at)[0]
+                pick = max((x for x in at if x[0] <= t0 + 1e-9), key=lambda x: prio[x[1]])
+                for x in at:
+                    if prio[x[1]] > prio[pick[1]] and x[0] <= t0 + OPT["look"] * ops[pick[1]]["alt"][q][1]:
+                        pick = x
+                if best is None or pick[0] < best[0] - 1e-9 or (pick[1] == best[1] and pick[0] < best[0] + 1e-9 and q == ops[pick[1]]["q"]):
+                    best = pick + (q,)
+            start, i, q = best
+            o = ops[i]
+            for q2 in o["alt"]:
+                cand[q2].remove(i)
+            queue[i] = q
+            order.append(i)
+            free[q] = start + o["alt"][q][1]
+            if o["kind"] == "dma":
+                engines = fin[i] = max(free[q] + 1.8, engines) + o["lat"]
             else:
-                ready[u] = max(ready[u], issued[i])
-            left[u] -= 1
-            if left[u] == 0:
-                for q2 in ops[u]["alt"]:
-                    cand[q2].append(u)
+                fin[i] = free[q] + o["lat"]
+            more[i] = set()
+            if "take" in o:
+                _t, held[o["take"]], last = min(pool)
+                pool.remove(min(pool))
+                more[i] = {last} - {-1}
+            if "give" in o:
+                pool.append((fin[i] + WAKE, held[o["give"]], i))
+            for b in o["banks"]:
+                more[i] |= {j for q2, j in lastin[b].items() if q2 != q}
+                lastin[b][q] = i
+            if o["grp"]:
+                opened[o["grp"][0]] = not o["grp"][2]
+            for u in users[i]:
+                waits = i in ops[u]["deps"] or ops[u]["kind"] == "land"
+                ready[u] = max(ready[u], fin[i] + WAKE if waits else free[q])
+                left[u] -= 1
+                if left[u] == 0:
+                    for q2 in ops[u]["alt"]:
+                        cand[q2].append(u)
+        return max(fin), order, queue, more, fin, held
+
+    def backward(queue, fin):
+        left = [len(u) for u in users]
+        cand = {q: [i for i in range(nop) if left[i] == 0 and queue[i] == q] for q in "VSTGYA"}
+        free = {q: 0.0 for q in cand}
+        back, ready = [0.0] * nop, [o["lat"] + (1.8 if o["kind"] == "dma" else 0) for o in ops]
+        for _ in range(nop):
+            best = None
+            for q, lst in cand.items():
+                if lst:
+                    t0 = max(min(ready[i] for i in lst), free[q] if q != "A" else 0.0)
+                    pick = max((i for i in lst if ready[i] <= t0 + 1e-9), key=lambda i: fin[i])
+                    if best is None or t0 < best[0]:
+                        best = (t0, pick, q)
+            start, i, q = best
+            o = ops[i]
+            cand[q].remove(i)
+            free[q] = back[i] = start + o["alt"][q][1]
+            for d in o["deps"] | o["order"]:
+                p = ops[d]
+                waits = d in o["deps"] or o["kind"] == "land"
+                ready[d] = max(ready[d], back[i] + (WAKE + p["lat"] + (1.8 if p["kind"] == "dma" else 0) if waits else 0))
+                left[d] -= 1
+                if left[d] == 0:
+                    cand[queue[d]].append(d)
+        return back
+
+    if PLAN.get("opt") != repr(OPT):
+        PLAN.clear()
+        PLAN["opt"] = repr(OPT)
+        PLAN["ops"] = ops
+        for _ in range(OPT["rounds"]):
+            plan = forward([p + (OPT["short"] if o["cost"] < 0.3 and o["q"] in "VS" and not o["soft"] else 0) for p, o in zip(prio, ops)])
+            PLAN.setdefault("ends", []).append(round(plan[0], 1))
+            if "plan" not in PLAN or plan[0] < PLAN["plan"][0]:
+                PLAN["plan"] = plan
+            back = backward(plan[2], plan[4])
+            prio = [OPT["mix"] * b + (1 - OPT["mix"]) * p for b, p in zip(back, prio)]
+    order, queue, more = PLAN["plan"][1:4]
+    for i, o in enumerate(ops):
+        o["q"] = queue[i]
+        o["fn"] = o["alt"][queue[i]][0]
+        o["deps"] |= more[i]
 
     total = {}
     for o in ops:

@@ -3,7 +3,8 @@ from concourse.mybir import AluOpType as OP, ActivationFunctionType as AF
 
 F, B, I, U, H = "float32", "bfloat16", "int32", "uint16", "float16"
 SB = {
-    "I16": (128, H), "B8h": (8, H), "gm32": (256, F), "zw": (4096, B), "sh": (4096, B), "so": (4096, B), "zT2": (256, B),
+    "I16": (128, H), "B8h": (8, H), "gm32": (256, F), "zw": (4096, B), "sh": (4096, B), "so": (4096, B), "zT2": (256, B), "es": (1024, B),
+    "Lp": (256, U), "Lq": (256, H),
     "eS": (2176, I), "xS": (2048, B), "zA": (256, B), "LA": (256, I), "vA": (16, I), "ef": (2048, H),
     "t0": (512, I), "tf": (512, H), "el": (256, U), "ys": (384, F),
     "iC": (8, I), "iN": (32, I), "zl": (32, U), "col": (48, F), "iD": (128, B), "gp": (16, B), "kk": (256, B), "ck": (256, B),
@@ -42,8 +43,8 @@ for _d in _use:
 for _n, _w in PS.items():
     SCRATCH[_n] = ("psum", [128, _w], "float32")
 SEMAPHORES = ["cV", "cS", "cT", "cG"] + ["d%d" % i for i in range(30)] + ["a%d" % i for i in range(30)] + ["l%d" % i for i in range(30)]
-OPT = {"tch": 512, "look": 0.5, "ef": "G", "exp": ("SG", "GS"), "load": ("0zv", "1XLE"), "ahead": 2, "short": 0, "cyT": 0.56e-3,
-       "xg": (("S", "S"), ("S", "S")), "sm": "SV", "expw": ("GS", "GS"), "B": "S", "vx": ((1, 1), (0, 1)), "gS": ((0, 1), (1, 2)), "rounds": 8, "mix": 1.0}
+OPT = {"tch": 512, "look": 0.35, "ef": "G", "exp": ("SG", "GS"), "load": ("0zv", "1XLE"), "ahead": 2, "short": 0, "cyT": 0.6e-3, "f": 1.15, "ga": 1.56, "wake": 0.13, "rate": 230e3, "land": 1.7, "s16": "V", "lead": (0.0, 5.0), "enS": ((1, 0), (1, 0)), "patch": ((0, 0), (0, 0)),
+       "xg": (("S", "S"), ("S", "S")), "sm": "SV", "expw": ("GS", "GS"), "B": "S", "vx": ((1, 1), (0, 1)), "gS": ((0, 2), (1, 2)), "rounds": 4, "tries": 120, "swap": 10, "tol": 0.2, "seed": 0}
 PLAN = {}
 
 
@@ -55,7 +56,7 @@ def rank_program(g, core, T, topo):
     HOP = 3
     TH, TAU = 1020, (1020, 1530)
     nxt, home = T.cores[(rank + HOP) % nR], T.cores[(rank - 2 * HOP) % nR]
-    CY, GA, SCAT, WAKE = 0.83e-3, 1.56, 3.8, 0.06
+    CY, GA, SCAT, WAKE = 0.83e-3 * OPT["f"], OPT["ga"], 3.8, OPT["wake"]
 
     QS = {"V": g.vector, "S": g.scalar, "T": g.tensor, "G": g, "Y": g.sync}
     ops = []
@@ -171,7 +172,7 @@ def rank_program(g, core, T, topo):
     def mm(out, l, r, start=True, stop=True, after=()):
         bank = out[0]
         prev = list(after) if start else [group[bank]]
-        cost = max(min(64, size(l)), size(r)) * (4 if SB[l[0]][1] == F else 1) * OPT["cyT"]
+        cost = max(min(64, size(l)), size(r)) * (4 if SB[l[0]][1] == F else 1) * OPT["cyT"] * OPT["f"]
         group[bank] = do("T", [l, r], out, lambda: g.tensor.matmul(ap(out), ap(l), ap(r), start, stop), 1, cost=cost,
                          grp=(bank, start, stop), after=prev)
         return group[bank]
@@ -212,7 +213,7 @@ def rank_program(g, core, T, topo):
         return "d%d" % (nd[0] - 1)
 
     def dma(q, out, in_, reads, writes, nbytes, sem=None, chain=True):
-        i = record(q, reads, writes, lambda: QS[q].dma_start(out, in_), 0.1, kind="dma", lat=nbytes / 180e3, sem=sem or newsem(),
+        i = record(q, reads, writes, lambda: QS[q].dma_start(out, in_), 0.1, kind="dma", lat=nbytes / OPT["rate"], sem=sem or newsem(),
                    inc=16, after=[lastdma[q]] if chain and q in lastdma else [])
         lastdma[q] = i
         return i
@@ -228,7 +229,7 @@ def rank_program(g, core, T, topo):
             return g.remote_dma(out_ap=ap(dst), in_ap=ap(src), remote_sem=T.sem["a%d" % k], local_sem=T.sem["l%d" % k], pid=pid,
                                 routing_id=rid, dma_engine_mask=sum(1 << e for e in engs))
         i = record("G", [src], [], fn, 0.4 if k else 2.4, kind="send", lat=0.5 + nb / 40e3, sem="l%d" % k, inc=len(engs))
-        record("A", [], [dst], None, 0.0, kind="land", lat=1.5, sem="a%d" % k, inc=len(engs), after=[i])
+        record("A", [], [dst], None, 0.0, kind="land", lat=OPT["land"], sem="a%d" % k, inc=len(engs), after=[i])
         return i
 
     def chain(ids):
@@ -441,8 +442,18 @@ def rank_program(g, core, T, topo):
 
     gaps = []
 
-    def gap(t, h, z, L16, zx):
-        onS = OPT["gS"][t][h]
+    def gap(t, h, z, L16, zx, ini):
+        onS, known, n = OPT["gS"][t][h], OPT["patch"][t][h], hn(h)
+        ts(R("Lf", *n), R(L16, *n), C(18 + t), MU)
+        for e in range(2):
+            copy(R("r%d" % (e + 1), *n), IND(R("io2k"), R(ini[e], *hm(h))), OPT["s16"], C(8 + 2 * t + e))
+        if known:
+            s3, rows = R("N%d" % h, 384, 512), ["r2", "r1", "Lf"][2 - known:]
+            for i, r in enumerate(rows):
+                mm(s3, I16, R(r, *n), i == 0, i == known)
+            L16 = "Lp"
+            cp(R(L16, *n), s3)
+            ts(R("Lq", *n), R(L16, *n), 0.0, AD)
         if onS:
             minus_zT(z, h, "zT2")
         for j in range(4):
@@ -456,19 +467,30 @@ def rank_program(g, core, T, topo):
                     act(R(sb, *a), x, AF.Copy)
                     minus_z(R(sb, *a), a[0], "zT2", AF.Relu, R(dst, *a))
         for k in range(16):
-            if k // 2 != t:
+            if k // 2 != t or k % 2 < known:
                 o = R("G", 128 * h + k, 128 * h + 128, 16)
                 mm(o, R("mh", 2048 * h + k, 2048 * h + 2048, 16), B8p, True, False)
                 mm(o, R("ml", 2048 * h + k, 2048 * h + 2048, 16), B8n, False, True)
 
     def entry(t, h, e, z, vl):
         a = (256 * e + 128 * h, 256 * e + 128 * h + 128)
-        tt(R("eh", *a), IND(R("HI", 0, 2048), R(vl, *hm(h))), R(z, *hn(h)), MX)
-        tt(R("en", *a), IND(R("LO", 0, 2048), R(vl, *hm(h))), R(z, *hn(h)), MX)
+        if OPT["enS"][t][e]:
+            bank = "P#%d" % pb[0]
+            pb[0] += 1
+            for j, tab in enumerate(("HI", "LO")):
+                act(R("es", 2 * a[0] + 128 * j, 2 * a[0] + 128 * j + 128), IND(R(tab, 0, 2048), R(vl, *hm(h))), AF.Copy)
+            ops[mm(R(bank, 0, 256), Ib, R("es", 2 * a[0], 2 * a[1]), True, False)]["take"] = bank
+            for j in range(2):
+                last = mm(R(bank, 128 * j, 128 * j + 128), nI, R(z, *hn(h)), False, j == 1)
+            ops[act(R("eh", *a), R(bank, 0, 128), AF.Relu)]["deps"].add(last)
+            ops[act(R("en", *a), R(bank, 128, 256), AF.Relu)]["give"] = bank
+            ops[-1]["order"].add(len(ops) - 2)
+        else:
+            tt(R("eh", *a), IND(R("HI", 0, 2048), R(vl, *hm(h))), R(z, *hn(h)), MX)
+            tt(R("en", *a), IND(R("LO", 0, 2048), R(vl, *hm(h))), R(z, *hn(h)), MX)
         o = R("G", 128 * h + 2 * t + e, 128 * h + 128, 16)
         mm(o, R("eh", *a), B8p, True, False)
         mm(o, R("en", *a), B8n, False, True)
-        copy(R("r%d" % (e + 1), *hn(h)), IND(R("io2k"), R(vl, *hm(h))), "V", C(8 + 2 * t + e))
 
     def decide(t, h, z, L16, xi, zo, Lo):
         n, m, kb, nb = hn(h), hm(h), "K%d" % h, "N%d" % h
@@ -488,8 +510,8 @@ def rank_program(g, core, T, topo):
                 last = mm(o, l, r, i == 0, i == len(pairs) - 1, after)
             return last
         zz, x, ab, hb, tl, sl = R(z, *n), R(xi, *n), R("ab2", *n), R("hb", *n), R("tl", *n), R("sl", *n)
-        Lf, r1, r2 = R("Lf", *n), R("r1", *n), R("r2", *n)
-        ts(Lf, R(L16, *n), C(18 + t), MU)
+        r2 = R("r2", *n)
+        log = [R(r, *n) for r in (("r2", "r1", "Lf"), ("r2", "Lq"), ("Lq",))[OPT["patch"][t][h]]]
         acc(s0, [(Ib, x), (nI, zz)])
         acc(s1, [(Ih, x), (R("cq", 0, 128, 1, ROW), R("ones", p=ROW)), (Ih, zz)])
         act(ab, s0, AF.Abs)
@@ -512,7 +534,7 @@ def rank_program(g, core, T, topo):
         either(lambda: act(R("fk", *n), R("G", *n), AF.Relu, 262144.0 * (TAU[t] + 0.5), -262144.0),
                lambda: ts(R("fk", *n), R("G", *n), float(TAU[t]), LE, 131072.0, MU))
         key = R(kb, 0, 128)
-        acc(key, [(r2, I16), (R("ones", p=ROW), R("KLc", p=ROW)), (Lf, I16), (r1, I16), (sl, R("BB4")), (Ib, R("fk", *n))])
+        acc(key, [(r, I16) for r in log] + [(R("ones", p=ROW), R("KLc", p=ROW)), (sl, R("BB4")), (Ib, R("fk", *n))])
         scan(R("R2", *n), R("RSD"), key, 0.0, MX, MN)
         end = R("R2", 128 * h + 15, 128 * h + 128, 16)
         cp(QI(2), end)
@@ -544,12 +566,12 @@ def rank_program(g, core, T, topo):
             tt(vo, R(kb, 136, 144), Q(3), AD)
         tt(R("w", *n), s0, R("sc", *n), MU)
         acc(s1, [(Ih, zz), (Iq, ab), (Iq, hb), (Iq, tl), (Ih, R("w", *n))], early)
-        copy(zo, s1, "V" if t else "SV")
+        copy(zo, s1, OPT["s16"] if t else "SV")
         ts(QI(5), QI(2), 4095, AN)
         tt(Q(5), vo, QI(5), SU)
         tt(R("e2", *n), IND(Q(5), R("zl", 0, 8)), R("flag", *n), MU)
-        acc(s3, [(R("e2", *n), I16), (I16, Lf), (I16, r1), (I16, r2)])
-        cp(Lo, s3)
+        acc(s3, [(R("e2", *n), I16)] + [(I16, r) for r in log])
+        copy(Lo, s3, OPT["s16"] if t else "V")
         tt(QB(2), QB(0), R("g16"), AD)
         ts(QB(3), end, 65536.0, LT, C(32 + h) if t == 0 else 1.0, MU)
         ids = []
@@ -593,11 +615,11 @@ def rank_program(g, core, T, topo):
             send(R(xo, *hn(h)), R(ini[2], *hn(h)), nxt)
         del gaps[:]
         for h in range(2):
-            gap(t, h, z, L16, zx)
+            gap(t, h, z, L16, zx, ini)
         chain(gaps)
         for h in range(2):
-            entry(t, h, 0, z, ini[0])
-            entry(t, h, 1, z, ini[1])
+            for e in range(OPT["patch"][t][h], 2):
+                entry(t, h, e, z, ini[e])
 
     for h in range(2):
         minus_zT("zA", h)
@@ -622,7 +644,7 @@ def rank_program(g, core, T, topo):
     for h in range(2):
         fo, fi, kb = "fo%d" % h, "fi%d" % h, "K%d" % h
         decide(1, h, "zC", "LC", "xi1", R(fo, 0, 128), R(fo, 128, 256))
-        send(R(fo), R(fi), home)
+        ops[send(R(fo), R(fi), home)]["lead"] = OPT["lead"][1] * (1 - h)
     counted("m1")
     tt(R("ya1"), R("M", 128, 256), R("m1"), MU)
     tt(R("yas"), R("M", 0, 128), R("ya1"), AD)
@@ -631,7 +653,8 @@ def rank_program(g, core, T, topo):
         fi, kb = "fi%d" % h, "K%d" % h
         a, b = hn(h)
         oz, ol = R("out", 2 * a, 2 * a + 128), R("out", 2 * a + 128, 2 * b)
-        cp(R("out", 2 * a, 2 * b), R(fi, 0, 256))
+        cp(oz, R(fi, 0, 128))
+        copy(ol, R(fi, 128, 256), OPT["s16"])
         dma("Y", T.yz[:, a:b], ap(oz), [oz], [], 1 << 16, chain=False)
         dma("S", T.yl[:, a:b], ap(ol), [ol], [], 1 << 16, chain=False)
         mm(R(kb, 384, 512, 1, (0, 8)), R(fi, 256, 264), I16)
@@ -647,7 +670,7 @@ def rank_program(g, core, T, topo):
     prio = [0.0] * nop
     for i in range(nop - 1, -1, -1):
         o = ops[i]
-        prio[i] += o["cost"] + o["lat"] + (1.8 if o["kind"] == "dma" else 0)
+        prio[i] += o.get("lead", 0) + o["cost"] + o["lat"] + (1.8 if o["kind"] == "dma" else 0)
         for d in o["deps"] | o["order"] | o["soft"]:
             prio[d] = max(prio[d], prio[i] + WAKE)
     users = [[] for _ in ops]
@@ -663,7 +686,7 @@ def rank_program(g, core, T, topo):
         fin, ready = [0.0] * nop, [0.0] * nop
         lastin = {b: {} for b in PS}
         opened, engines, order, queue, more = {}, 0.0, [], [None] * nop, [None] * nop
-        pool, held = [(0.0, "P0", -1), (0.0, "P1", -1)], {}
+        pool, held, cause, before = [(0.0, "P0", -1), (0.0, "P1", -1)], {}, [(None, False)] * nop, {}
         while len(order) < nop:
             best = None
             for q, lst in cand.items():
@@ -691,12 +714,17 @@ def rank_program(g, core, T, topo):
                         pick = x
                 if best is None or pick[0] < best[0] - 1e-9 or (pick[1] == best[1] and pick[0] < best[0] + 1e-9 and q == ops[pick[1]]["q"]):
                     best = pick + (q,)
+            if best is None:
+                return (1e9,)
             start, i, q = best
             o = ops[i]
             for q2 in o["alt"]:
                 cand[q2].remove(i)
             queue[i] = q
             order.append(i)
+            if q != "A" and free[q] > ready[i] and q in before and before[q] not in o["order"]:
+                cause[i] = (before[q], True)
+            before[q] = i
             free[q] = start + o["alt"][q][1]
             if o["kind"] == "dma":
                 engines = fin[i] = max(free[q] + 1.8, engines) + o["lat"]
@@ -716,12 +744,14 @@ def rank_program(g, core, T, topo):
                 opened[o["grp"][0]] = not o["grp"][2]
             for u in users[i]:
                 waits = i in ops[u]["deps"] or ops[u]["kind"] == "land"
-                ready[u] = max(ready[u], fin[i] + WAKE if waits else free[q])
+                if (fin[i] + WAKE if waits else free[q]) >= ready[u]:
+                    ready[u] = fin[i] + WAKE if waits else free[q]
+                    cause[u] = (i, False)
                 left[u] -= 1
                 if left[u] == 0:
                     for q2 in ops[u]["alt"]:
                         cand[q2].append(u)
-        return max(fin), order, queue, more, fin, held
+        return max(fin), order, queue, more, fin, held, cause
 
     def backward(queue, fin):
         left = [len(u) for u in users]
@@ -743,7 +773,7 @@ def rank_program(g, core, T, topo):
             for d in o["deps"] | o["order"]:
                 p = ops[d]
                 waits = d in o["deps"] or o["kind"] == "land"
-                ready[d] = max(ready[d], back[i] + (WAKE + p["lat"] + (1.8 if p["kind"] == "dma" else 0) if waits else 0))
+                ready[d] = max(ready[d], back[i] + p.get("lead", 0) + (WAKE + p["lat"] + (1.8 if p["kind"] == "dma" else 0) if waits else 0))
                 left[d] -= 1
                 if left[d] == 0:
                     cand[queue[d]].append(d)
@@ -754,12 +784,33 @@ def rank_program(g, core, T, topo):
         PLAN["opt"] = repr(OPT)
         PLAN["ops"] = ops
         for _ in range(OPT["rounds"]):
-            plan = forward([p + (OPT["short"] if o["cost"] < 0.3 and o["q"] in "VS" and not o["soft"] else 0) for p, o in zip(prio, ops)])
+            plan = forward(prio)
             PLAN.setdefault("ends", []).append(round(plan[0], 1))
+            if len(plan) == 1:
+                break
             if "plan" not in PLAN or plan[0] < PLAN["plan"][0]:
-                PLAN["plan"] = plan
-            back = backward(plan[2], plan[4])
-            prio = [OPT["mix"] * b + (1 - OPT["mix"]) * p for b, p in zip(back, prio)]
+                PLAN["plan"], keep = plan, prio
+            prio = backward(plan[2], plan[4])
+        plan, rng = PLAN["plan"], np.random.default_rng(OPT["seed"])
+        for step in range(OPT["tries"]):
+            i, pairs = max(range(nop), key=lambda j: plan[4][j]), []
+            while i is not None:
+                j, queued = plan[6][i]
+                if queued:
+                    pairs.append((i, j))
+                i = j
+            prio = list(keep)
+            for k in rng.choice(len(pairs), min(len(pairs), OPT["swap"]), replace=False):
+                i, j = pairs[int(k)]
+                prio[i], prio[j] = max(prio[i], prio[j]) + 0.3 * rng.random(), min(prio[i], prio[j]) - 0.3 * rng.random()
+            if step % 8 == 7:
+                prio = backward(plan[2], plan[4])
+            new = forward(prio)
+            if new[0] <= plan[0] + OPT["tol"]:
+                plan, keep = new, prio
+            if new[0] < PLAN["plan"][0]:
+                PLAN["plan"] = new
+                PLAN["ends"].append(round(new[0], 1))
     order, queue, more = PLAN["plan"][1:4]
     for i, o in enumerate(ops):
         o["q"] = queue[i]

@@ -4,15 +4,15 @@ from concourse.mybir import AluOpType as OP, ActivationFunctionType as AF
 F, B, I, U, H = "float32", "bfloat16", "int32", "uint16", "float16"
 SB = {
     "I16": (128, H), "B8h": (8, H), "gm32": (256, F), "zw": (4096, B), "sh": (4096, B), "so": (4096, B), "zT2": (256, B), "es": (1024, B),
-    "Lp": (256, U), "Lq": (256, H),
-    "eS": (2176, I), "xS": (2048, B), "zA": (256, B), "LA": (256, I), "vA": (16, I), "ef": (2048, H),
+    "Lp": (256, U), "Lq": (256, H), "nI16": (128, H), "ROT": (128, H), "Sel0": (128, H), "nE": (256, F),
+    "eS": (2304, I), "xS": (2048, B), "zA": (256, B), "LA": (256, I), "vA": (16, I), "ef": (2048, H),
     "t0": (512, I), "tf": (512, H), "el": (256, U), "ys": (384, F),
     "iC": (8, I), "iN": (32, I), "zl": (32, U), "col": (48, F), "iD": (128, B), "gp": (16, B), "kk": (256, B), "ck": (256, B),
-    "KLc": (128, B), "io": (144, B), "g16": (8, B), "mg": (128, B), "e32": (512, B), "EXP": (512, B), "io2k": (2176, F),
+    "KLc": (128, B), "io": (144, B), "g16": (8, B), "mg": (128, B), "e32": (512, B), "EXP": (512, B), "io2k": (2304, F),
     "ones": (128, B), "cq": (256, B), "c175": (256, B), "wrow": (256, F), "maskJ": (256, B), "IM": (768, B), "If": (128, F),
     "RST": (256, B), "RSD": (128, F), "W16": (16, B), "B8": (16, B), "W8": (16, B), "B8f": (16, F), "BB4": (128, B),
     "SelC": (32, H), "WY": (24, H), "B128": (8, B), "B8i": (8, H),
-    "XB": (2048, B), "HI": (2176, B), "LO": (2176, B), "m0": (128, B), "Sb": (128, B), "m1": (128, B),
+    "XB": (2048, B), "HI": (2304, B), "LO": (2304, B), "m0": (128, B), "Sb": (128, B), "m1": (128, B),
     "zT": (256, B), "xg": (4096, B), "ab": (4096, B), "c16": (256, U), "cf": (256, H), "H": (256, B), "ad": (256, B),
     "mk": (256, B), "R": (512, F), "wi": (32, I), "wa": (32, I), "wb": (32, B), "wT": (512, B),
     "vlA": (16, U), "v1o0": (16, U), "v2o0": (16, U), "v1o1": (16, U), "v2o1": (16, U), "vlB": (16, U), "loB": (16, U),
@@ -20,10 +20,12 @@ SB = {
     "zx0": (4096, B), "zx1": (4096, B), "mh": (4096, B), "ml": (4096, B), "eh": (512, B), "en": (512, B), "Lf": (256, H),
     "r1": (256, H), "r2": (256, H), "ab2": (256, B), "hb": (256, B), "sl": (256, B), "tl": (256, B), "sc": (256, B),
     "w": (256, B), "fk": (256, B), "R2": (256, F), "flag": (256, B), "e2": (256, H), "NP": (128, H), "ce": (256, H),
-    "qs": (256, F), "qi": (128, I), "qb": (96, B), "ul": (16, U), "ulo": (16, U), "OH": (4096, B), "gm": (768, H),
+    "qs": (256, F), "qi": (128, I), "qb": (96, B), "ul": (16, U), "ulo": (16, U), "OH": (2048, B), "gm": (768, H),
     "adu": (256, B), "ad2": (256, B), "mn": (256, B), "e12": (32, U), "u2": (16, U), "nB": (256, B), "nH": (256, B),
     "nL": (256, B), "Lo0": (256, U), "zo1": (256, B), "Lo1": (256, U), "fo0": (264, H), "fo1": (264, H), "out": (512, F),
-    "zB": (256, B), "LB": (256, U), "v1i0": (16, U), "v2i0": (16, U), "xi0": (256, B), "zC": (256, B), "LC": (256, U),
+    "wzB": (768, B), "LB": (256, U), "v1i0": (16, U), "v2i0": (16, U), "xi0": (256, B), "wzC": (768, B), "LC": (256, U),
+    "zs": (16, U), "gu": (512, H), "gl": (256, H), "B64": (16, H), "g32": (8, B), "OHh": (256, B), "wcol": (2, B),
+    "nW16": (16, B), "St": (128, B), "m0t": (128, B), "yat": (128, F),
     "v1i1": (16, U), "v2i1": (16, U), "xi1": (256, B), "fi0": (264, H), "fi1": (264, H),
     "yvs": (256, F), "ya1": (128, F), "ya2": (128, F), "yas": (128, F),
 }
@@ -43,8 +45,8 @@ for _d in _use:
 for _n, _w in PS.items():
     SCRATCH[_n] = ("psum", [128, _w], "float32")
 SEMAPHORES = ["cV", "cS", "cT", "cG"] + ["d%d" % i for i in range(30)] + ["a%d" % i for i in range(30)] + ["l%d" % i for i in range(30)]
-OPT = {"tch": 512, "look": 0.35, "ef": "G", "exp": ("SG", "GS"), "load": ("0zv", "1XLE"), "ahead": 2, "short": 0, "cyT": 0.6e-3, "f": 1.15, "ga": 1.56, "wake": 0.13, "rate": 230e3, "land": 1.7, "s16": "V", "lead": (0.0, 5.0), "enS": ((1, 0), (1, 0)), "patch": ((0, 0), (0, 0)),
-       "xg": (("S", "S"), ("S", "S")), "sm": "SV", "expw": ("GS", "GS"), "B": "S", "vx": ((1, 1), (0, 1)), "gS": ((0, 2), (1, 2)), "rounds": 4, "tries": 120, "swap": 10, "tol": 0.2, "seed": 0}
+OPT = {"tch": 512, "look": 0.35, "ef": "G", "exp": ("SG", "G"), "load": ("0zv", "1LXE"), "ahead": 2, "short": 0, "cyT": 0.6e-3, "f": 1.15, "ga": 1.56, "wake": 0.13, "rate": 230e3, "land": 1.7, "s16": "SV", "lead": (0.0, 5.0), "enS": ((1, 0), (0, 0)), "patch": ((0, 0), (0, 0)),
+       "xg": (("S", "S"), ("S", "S")), "sm": "SV", "expw": ("S", "G"), "B": "S", "vx": ((1, 1), (0, 1)), "gS": ((0, 2), (1, 2)), "rounds": 4, "tries": 100, "swap": 10, "tol": 0.2, "seed": 0, "starts": 12, "eps": 2.0, "up": 3.0, "win": 8.0, "rot": 2, "rl": ((0, 0), (0, 0)), "tabS": 0, "Lo0": "V", "cfG": (0, 0), "one": 1}
 PLAN = {}
 
 
@@ -91,6 +93,8 @@ def rank_program(g, core, T, topo):
         return me
 
     def R(name, a=0, b=None, st=1, p=None):
+        if name in ("zB", "zC"):
+            return ("w" + name, a + 256, (256 if b is None else b) + 256, st, p)
         if b is None:
             b = SB[name][0] if name in SB else 512
         return (name, a, b, st, p)
@@ -269,12 +273,13 @@ def rank_program(g, core, T, topo):
     iota(R("gp"), [[0, 2], [1, 8]], 0, 0)
     iota(R("kk"), [[0, 16], [1, 16]], 0, 0)
     iota(R("e32"), [[1, 32], [0, 16]], 0, 0)
-    iota(R("ck", p=ROW), [[16640, 2], [0, 8], [256, 16]], 0, 0)
     iota(R("io"), [[1, 144]], 0, 0)
     iota(R("KLc", p=ROW), [[0, 8], [4096, 16]], 65536, 0)
     iota(R("g16"), [[16, 8]], 0, 0)
+    iota(R("g32"), [[32, 8]], 0, 0)
     iota(R("mg"), [[1, 8], [0, 16]], 0, 0)
-    iota(R("io2k"), [[1, 2176]], 0, 0)
+    for c in range(0, 2304, 384):
+        iota(R("io2k", c, c + 384), [[1, 384]], c, 0)
     cp(R("zl"), R("iN"))
     ts(R("iC", 1, 2), R("iC", 0, 1), 4, SH)
     ts(R("iC", 2, 3), R("iC", 0, 1), 15, AN)
@@ -290,9 +295,13 @@ def rank_program(g, core, T, topo):
     ts(C(20), PK, 1.0, MU, 0.5, AD)
     ts(C(21), PK, -1.0, MU, -0.5, AD)
     ts(C(22), PK, -2.0, MU, -63.5 / 64, AD)
-    ts(C(25), PP, 2048.0, AD)
-    ts(C(26), PP, 65536.0 + 2048.0, AD)
-    ts(C(27), PK, 2048.0, AD)
+    ts(C(25), PP, 2.0, MU, 2048.0, AD)
+    ts(C(26), PP, 2.0, MU, 65536.0 + 2048.0, AD)
+    ts(C(27), PK, 2.0, MU, 2048.0, AD)
+    for h in range(2):
+        ts(C(36 + h), PK, 64.0 + 128.0 * h, AD)
+        ts(R("B64", *hm(h)), R("gp", 0, 8), PG, EQ, 64.0 - 128.0 * h, MU)
+    fill(R("eS", 2048, 2304), 0)
     ts(C(28), PK, 1.0, AD)
     ts(C(29), C(8), 16.0, MU, -1.0, AD)
     tt(C(31), C(9), C(8), SU)
@@ -301,14 +310,19 @@ def rank_program(g, core, T, topo):
     fill(R("cq"), -0.25)
     fill(R("c175", p=ROW), 1.75)
     fill(R("NP"), 0.0)
-    for j, c in enumerate((1.0 / 128, -1.0, 1.0, 0.5, -0.5, 0.25)):
+    for j, c in enumerate((1.0 / 128, -1.0, 1.0, 0.5)):
         ts(R("IM", 128 * j, 128 * j + 128), R("iD"), 0.0, EQ, c, MU)
-    PHI, nI, Ib, Ih, nIh, Iq = [R("IM", 0, 256)] + [R("IM", 128 * j, 128 * j + 128) for j in range(1, 6)]
+    PHI, nI, Ib, Ih = [R("IM", 0, 256)] + [R("IM", 128 * j, 128 * j + 128) for j in range(1, 4)]
     If = R("If")
     ts(If, R("iD"), 0.0, EQ)
     ts(R("EXP"), R("e32"), P32, EQ)
     ts(R("W16"), R("gp"), PG, EQ, 4096.0, MU)
-    ts(R("RST"), R("kk"), 0.0, EQ, 33554432.0, MU)
+    ts(R("nW16"), R("gp"), PG, EQ, -4096.0, MU)
+    ts(R("maskJ"), R("kk"), 0.0, EQ, 33554432.0, MU)
+    ts(R("RST"), R("maskJ"), -256.0, AD)
+    ts(R("nI16"), R("iD"), 0.0, EQ, -1.0, MU)
+    ts(R("ROT"), R("iD"), C(29), EQ)
+    ts(R("Sel0"), R("mg"), PG, EQ, C(8), MU)
     ts(R("RSD"), R("kk", 0, 128), 0.0, EQ, C(26), MU)
     ts(R("maskJ"), R("kk"), PK, EQ)
     ts(R("B128"), R("gp", 0, 8), PG, EQ, 128.0, MU)
@@ -325,12 +339,12 @@ def rank_program(g, core, T, topo):
     scan(R("wrow", p=ROW), R("c175", p=ROW), R("cq", p=ROW), 2.0 ** -120 / 1.75, MU, MX)
     for h in range(2):
         mm(R("N1", 256 + h, 257 + h), R("wrow", *hn(h), 1, ROW), R("If", 0, 1, 1, ROW))
-    cp(R("col", 32, 34), R("N1", 256, 258))
-    ts(R("col", 34, 36), R("col", 32, 34), 2.54, MU)
+    cp(R("wcol"), R("N1", 256, 258))
+    ts(R("col", 34, 36), R("wcol"), 2.54, MU)
 
     cp(R("vlA"), R("vA"))
     send(R("zA"), R("zB"), nxt)
-    cp(R("Lo0"), R("LA"))
+    copy(R("Lo0"), R("LA"), OPT["Lo0"])
     send(R("Lo0"), R("LB"), nxt)
     for k in range(2):
         cp(R("tf", 256 * k, 256 * k + 256, 1, (0, 64)), R("t0", 256 * k, 256 * k + 256, 1, (0, 64)))
@@ -341,15 +355,22 @@ def rank_program(g, core, T, topo):
     for b in range(4):
         c = R("XB", 512 * b, 512 * b + 512)
         copy(c, IND(R("xS"), R("el", 64 * b + 32, 64 * b + 64)), OPT["B"])
+        if b >= 4 - OPT["tabS"]:
+            a, r = R("sh", 512 * b, 512 * b + 512), R("so", 512 * b, 512 * b + 512)
+            act(a, IND(R("xS"), R("el", 64 * b, 64 * b + 32)), AF.Copy)
+            for j, (u, v, sign, f, dst) in enumerate(((a, c, nI, AF.Relu, r), (c, r, Ib, AF.Copy, R("HI", b, 2048, 4)),
+                                                      (a, r, nI, AF.Copy, R("LO", b, 2048, 4)))):
+                bank = ("K0", "K1", "N1")[j]
+                mm(R(bank), sign, v, True, False)
+                mm(R(bank), Ib, u, False, True)
+                act(dst, R(bank), f)
+            continue
         for tab, op in (("HI", MX), ("LO", MN)):
             ids.append(tt(R(tab, b, 2048, 4), IND(R("xS"), R("el", 64 * b, 64 * b + 32)), c, op))
     chain(ids)
     chain([copy(R("ef", c, c + 256), R("eS", c, c + 256), OPT["ef"]) for c in range(0, 2048, 256)])
     for hi in range(16):
         mm(R("M", hi, 384, 16), R("ef", 128 * hi, 128 * hi + 128), R("WY"))
-    copy(R("ys"), R("M", 0, 384), "SV")
-    for j in range(3):
-        mm(R("M", *hn(j)), R("ys", *hn(j)), If)
 
     pb = [0]
 
@@ -387,7 +408,7 @@ def rank_program(g, core, T, topo):
             o = R(kb, slot + 8 * j, slot + 8 * j + 8)
             mm(o, R(gm, at + 128 * j, at + 128 * j + 128), one, True, not base)
             if base:
-                mm(o, R("ones", p=ROW), R("g16", p=ROW), False, True)
+                mm(o, R("ones", p=ROW), R("g32", p=ROW), False, True)
 
     def minus_z(src, b, zT, f, dst):
         bank = "P#%d" % pb[0]
@@ -408,10 +429,13 @@ def rank_program(g, core, T, topo):
 
     behind = []
 
-    def walk(t, step, h, vl, lo, out, outlo):
+    def walk(t, step, h, vl, lo, out, outlo=None):
         n, m, kb = hn(h), hm(h), "K%d" % h
         cp(R("c16", *n), IND(R("eS", 0, 2048), R(vl, *m)))
-        ts(R("cf", *n), R("c16", *n), 0.0, AD)
+        if OPT["cfG"][t]:
+            either(lambda: gcopy(R("cf", *n), R("c16", *n)), lambda: ts(R("cf", *n), R("c16", *n), 0.0, AD))
+        else:
+            ts(R("cf", *n), R("c16", *n), 0.0, AD)
         ts(R("H", *n), R("c16", *n), 16448.5, AD)
         onV = OPT["vx"][t][step]
         for j in range(4):
@@ -423,18 +447,23 @@ def rank_program(g, core, T, topo):
                 behind.append(minus_z(R("xg", b, b + 512), b, "zT", AF.Abs, R("ab", b, b + 512)))
             else:
                 tt(R("xg", b, b + 512), x, R("zw", b, b + 512), SU)
-                act(R("ab", b, b + 512), R("xg", b, b + 512), AF.Abs)
+                if OPT["rl"][t][step]:
+                    ts(R("ab", b, b + 512), R("xg", b, b + 512), 0.0, MX, 2.0, MU)
+                else:
+                    act(R("ab", b, b + 512), R("xg", b, b + 512), AF.Abs)
         mm(R(kb, 0, 256), R("H", *n), PHI, True, False)
-        mm(R(kb, 0, 256), R("ones", p=ROW), R("ck", p=ROW), False, False)
+        if onV and OPT["rl"][t][step]:
+            for k in range(16):
+                mm(R(kb, k, 256, 16, (128 - 32 * onV, 128)), R("xg", 2048 * h + 2048 - 512 * onV + k, 2048 * h + 2048, 16), R("nW16"), False, False)
         mm(R(kb, 128, 256), R("cf", *n), I16, False, False)
-        if t:
+        if lo:
             apart(R("ad", *n), R(vl, *m))
             tt(R("mk", *n), IND(R("m0"), R(lo, *m)), R("ad", *n), GT)
         for k in range(16):
-            mm(R(kb, k, 256, 16), R("ab", 2048 * h + k, 2048 * h + 2048, 16), R("W16"), False, k == 15 and not t)
-        if t:
+            mm(R(kb, k, 256, 16), R("ab", 2048 * h + k, 2048 * h + 2048, 16), R("W16"), False, k == 15 and not lo)
+        if lo:
             mm(R(kb, 0, 256, 16), R("mk", *n), R("W16"), False, True)
-        scan(R("R", 256 * h, 256 * h + 256), R("RST"), R(kb, 0, 256), 0.0, MX, MN)
+        scan(R("R", 256 * h, 256 * h + 256), R("RST"), R(kb, 0, 256), 0.0, AD, MN)
         a = (16 * h, 16 * h + 16)
         cp(R("wi", *a), R("R", 256 * h + 15, 256 * h + 256, 16))
         ts(R("wa", *a), R("wi", *a), 127, AN)
@@ -466,11 +495,17 @@ def rank_program(g, core, T, topo):
                 else:
                     act(R(sb, *a), x, AF.Copy)
                     minus_z(R(sb, *a), a[0], "zT2", AF.Relu, R(dst, *a))
-        for k in range(16):
-            if k // 2 != t or k % 2 < known:
-                o = R("G", 128 * h + k, 128 * h + 128, 16)
-                mm(o, R("mh", 2048 * h + k, 2048 * h + 2048, 16), B8p, True, False)
-                mm(o, R("ml", 2048 * h + k, 2048 * h + 2048, 16), B8n, False, True)
+        ks = [k for k in range(16) if k // 2 != t or k % 2 < known]
+        if OPT["one"]:
+            for src, w in (("mh", B8p), ("ml", B8n)):
+                for k in ks:
+                    mm(R("G", 128 * h + k, 128 * h + 128, 16), R(src, 2048 * h + k, 2048 * h + 2048, 16), w, src == "mh" and k == ks[0],
+                       src == "ml" and k == ks[-1])
+            return
+        for k in ks:
+            o = R("G", 128 * h + k, 128 * h + 128, 16)
+            mm(o, R("mh", 2048 * h + k, 2048 * h + 2048, 16), B8p, True, False)
+            mm(o, R("ml", 2048 * h + k, 2048 * h + 2048, 16), B8n, False, True)
 
     def entry(t, h, e, z, vl):
         a = (256 * e + 128 * h, 256 * e + 128 * h + 128)
@@ -509,7 +544,8 @@ def rank_program(g, core, T, topo):
             for i, (l, r) in enumerate(pairs):
                 last = mm(o, l, r, i == 0, i == len(pairs) - 1, after)
             return last
-        zz, x, ab, hb, tl, sl = R(z, *n), R(xi, *n), R("ab2", *n), R("hb", *n), R("tl", *n), R("sl", *n)
+        zz, x, sl = R(z, *n), R(xi, *n), R("sl", *n)
+        ab, hb = R("w" + z, 640 * h, 640 * h + 128), R("w" + z, 128 + 384 * h, 256 + 384 * h)
         r2 = R("r2", *n)
         log = [R(r, *n) for r in (("r2", "r1", "Lf"), ("r2", "Lq"), ("Lq",))[OPT["patch"][t][h]]]
         acc(s0, [(Ib, x), (nI, zz)])
@@ -526,11 +562,8 @@ def rank_program(g, core, T, topo):
         tt(QI(0), R(nb, 272, 280), Q(1), AD)
         ts(QI(1), QI(0), 2047, AN)
         cp(R("NP", 0, 128, 16), QI(1))
-        early = [mm(s3, R("NP"), I16)]
-        cp(R("eS", 2048, 2176), s3)
-        acc(s1, [(Ib, ab), (nI, hb)])
-        tt(tl, s1, sl, MU)
-        early.append(acc(s0, [(nIh, tl), (Ib, zz), (nIh, ab), (nIh, hb)]))
+        mm(s3, R("NP"), I16)
+        cp(R("eS", 2048, 2304, 2), s3)
         either(lambda: act(R("fk", *n), R("G", *n), AF.Relu, 262144.0 * (TAU[t] + 0.5), -262144.0),
                lambda: ts(R("fk", *n), R("G", *n), float(TAU[t]), LE, 131072.0, MU))
         key = R(kb, 0, 128)
@@ -538,16 +571,26 @@ def rank_program(g, core, T, topo):
         scan(R("R2", *n), R("RSD"), key, 0.0, MX, MN)
         end = R("R2", 128 * h + 15, 128 * h + 128, 16)
         cp(QI(2), end)
+        ts(QI(5), QI(2), 4095, AN)
+        ts(Q(7), end, 65536.0, LT, 2.0, MU)
+        tt(QI(6), Q(7), Q(0), SU)
+        ul, ce = R("ul", *m), R("ce", *n)
+        tt(R("gu", 256 * h, 256 * h + 256), IND(QI(5, 16), R("zl", 0, 16)), R("maskJ"), MU)
+        mm(R(kb, 256, 264), R("gu", 256 * h, 256 * h + 128), R("B8h"))
+        cp(ul, R(kb, 256, 264))
+        cp(ce, IND(R("eS"), ul))
         ts(QI(3), QI(2), 7, SH, 31, AN)
         ts(QI(4), QI(2), 127, AN)
-        cp(QB(0, 16), QI(3, 16))
-        tolist(h, QI(3, 16), "ul", 0.0, "ulo")
-        ul, ce = R("ul", *m), R("ce", *n)
-        cp(ce, IND(R("eS"), ul))
-        act(R("sc", *n), IND(R("io2k"), ul), AF.Sign, 2047.5, -1.0)
+        cp(QB(0), QI(4))
+        acc(R(kb, 312, 320), [(R("gu", 256 * h + 128, 256 * h + 256), R("B64", *m)), (R("ones", p=ROW), R("g16", p=ROW))])
+        ts(R("zs", *m), R(kb, 312, 320), C(36 + h), AD)
+        copy(zo, IND(R("w" + z, 384 * h, 384 * h + 384), R("zs", *m)), OPT["s16"] if t else "SV")
         tt(R("flag", *n), key, R("R2", *n), EQ)
-        apart(R("adu", *n), ul)
         if t == 0:
+            tt(R("gl", *n), IND(QI(4), R("zl", 0, 8)), R("maskJ", 0, 128), MU)
+            mm(R(kb, 264, 272), R("gl", *n), R("B8h"))
+            cp(R("ulo", *m), R(kb, 264, 272))
+            apart(R("adu", *n), ul)
             mm(R(kb, 128, 152), ce, R("SelC", 8, 32))
             copy(Q(2, 24), R(kb, 128, 152), "SV")
             vo = Q(2)
@@ -557,29 +600,18 @@ def rank_program(g, core, T, topo):
             ts(R("vi", 16 * h + 8, 16 * h + 16), R("vi", 16 * h, 16 * h + 8), 127, AN)
             cp(R("loB", *m), R("vi", 16 * h + 8, 16 * h + 16))
         else:
-            tt(R("mn", *n), IND(R("m0"), R("ulo", *m)), R("adu", *n), GT)
-            mm(R(kb, 128, 144), ce, R("SelC", 0, 16))
-            mm(R(kb, 152, 160), R("mn", *n), B8p)
-            copy(Q(2), R(kb, 152, 160), "SV")
-            tt(Q(3), R(kb, 128, 136), Q(2), MU)
-            vo = R("fo%d" % h, 256, 264)
-            tt(vo, R(kb, 136, 144), Q(3), AD)
-        tt(R("w", *n), s0, R("sc", *n), MU)
-        acc(s1, [(Ih, zz), (Iq, ab), (Iq, hb), (Iq, tl), (Ih, R("w", *n))], early)
-        copy(zo, s1, OPT["s16"] if t else "SV")
-        ts(QI(5), QI(2), 4095, AN)
-        tt(Q(5), vo, QI(5), SU)
-        tt(R("e2", *n), IND(Q(5), R("zl", 0, 8)), R("flag", *n), MU)
+            mm(R(kb, 128, 136), ce, R("SelC", 8, 16))
+            cp(R("fo%d" % h, 256, 264), R(kb, 128, 136))
+        acc(R(kb, 384, 512), [(ce, R("Sel0"))] + [(r, R("nI16")) for r in log])
+        tt(R("e2", *n), R(kb, 384, 512), R("flag", *n), MU)
         acc(s3, [(R("e2", *n), I16)] + [(I16, r) for r in log])
         copy(Lo, s3, OPT["s16"] if t else "V")
-        tt(QB(2), QB(0), R("g16"), AD)
-        ts(QB(3), end, 65536.0, LT, C(32 + h) if t == 0 else 1.0, MU)
+        tt(R("OHh", *n), IND(QI(3), R("zl", 0, 8)), R("kk", 0, 128), EQ)
         ids = []
         for c in range(8):
-            a = 2048 * h + 256 * c
-            ids.append(ts(R("OH", a, a + 128), R("io", 0, 128), R("qb", 48 * h + 16 + c, 48 * h + 17 + c), EQ, R("qb", 48 * h + 24 + c, 48 * h + 25 + c), MU))
-            ids.append(ts(R("OH", a + 128, a + 256), R("io", 0, 128), R("qb", 48 * h + 8 + c, 48 * h + 9 + c), EQ))
-            mm(R("M", 384, 512), R("OH", a, a + 128), R("OH", a + 128, a + 256), h == 0 and c == 0, h == 1 and c == 7)
+            a = R("OH", 1024 * h + 128 * c, 1024 * h + 128 * c + 128)
+            ids.append(ts(a, R("io", 0, 128), R("qb", 48 * h + c, 48 * h + c + 1), EQ, R("wcol", h, h + 1) if t == 0 else 1.0, MU))
+            mm(R("M", 384 + 16 * c, 400 + 16 * c), a, R("OHh", 128 * h + 16 * c, 128 * h + 16 * c + 16), h == 0 and c == 0, h == 1 and c == 7)
         chain(ids)
         if t == 0:
             masked(h, Q(3, 16), 384 * h + 128, 280, 2)
@@ -590,6 +622,8 @@ def rank_program(g, core, T, topo):
             either(lambda: act(R("ad2", *n), R("adu", *n), AF.Relu, 9e29, -9e29),
                    lambda: ts(R("ad2", *n), R("adu", *n), 1.0, LT, 9e29, MU))
             ts(Q(6), QI(5), C(25), SU)
+            mm(s0, R("ROT"), ce)
+            copy(R("nE", *n), s0, "SV")
 
     def turn(h):
         n, m, kb = hn(h), hm(h), "K%d" % h
@@ -603,13 +637,21 @@ def rank_program(g, core, T, topo):
         cp(IND(R("HI"), R("u2", *m)), R("nH", *n))
         cp(IND(R("LO"), R("u2", *m)), R("nL", *n))
 
+    def rotate():
+        for h in range(2):
+            cp(IND(R("eS"), R("u2", *hm(h))), R("nE", *hn(h)))
+
     def visit(t, vl, lo, v1, v2, xo, z, L16, zx, ini):
         expand(t, zx, z, "zo1" if t else "zA")
         for h in range(2):
-            walk(t, 0, h, vl, lo, v1, "lo1" if t else None)
+            walk(t, 0, h, vl, lo, v1, "lo1" if t and h < OPT["rot"] else None)
         send(R(v1), R(ini[0]), nxt)
         for h in range(2):
-            walk(t, 1, h, v1, "lo1", v2, None)
+            if t and h == OPT["rot"]:
+                rotate()
+            walk(t, 1, h, v1, "lo1" if t and h < OPT["rot"] else None, v2)
+            if t and h == 1 and OPT["rot"] == 2:
+                rotate()
             send(R(v2, *hm(h)), R(ini[1], *hm(h)), nxt)
             copy(R(xo, *hn(h)), IND(R("xS"), R(v2, *hm(h))), "SV")
             send(R(xo, *hn(h)), R(ini[2], *hn(h)), nxt)
@@ -629,14 +671,18 @@ def rank_program(g, core, T, topo):
         send(R("zo1", *hn(h)), R("zC", *hn(h)), nxt)
         minus_zT("zo1", h)
         send(R("Lo1", *hn(h)), R("LC", *hn(h)), nxt)
-    def counted(out):
-        either(lambda: act(R(out), R("M", 384, 512), AF.Sign), lambda: ts(R(out), R("M", 384, 512), 0.0, GT))
-    counted("m0")
-    copy(R("Sb"), R("M", 384, 512), "SV")
+
+    def counted(out, a):
+        either(lambda: act(R(out), a, AF.Sign), lambda: ts(R(out), a, 0.0, GT))
+    copy(R("St"), R("M", 384, 512), "SV")
+    mm(R("G", 256, 384), R("St"), Ib)
+    counted("m0", R("G", 256, 384))
+    copy(R("Sb"), R("G", 256, 384), "SV")
+    counted("m0t", R("M", 384, 512))
     for h in range(2):
         turn(h)
-    tt(R("ya1"), R("M", 128, 256), R("m0"), MU)
-    tt(R("ya2"), R("M", 256, 384), R("m0"), MU)
+    tt(R("ya1"), R("M", 128, 256), R("m0t"), MU)
+    tt(R("ya2"), R("M", 256, 384), R("m0t"), MU)
     tt(R("M", 0, 128), R("M", 0, 128), R("ya1"), AD)
     tt(R("M", 128, 256), R("M", 128, 256), R("ya2"), AD)
 
@@ -645,9 +691,11 @@ def rank_program(g, core, T, topo):
         fo, fi, kb = "fo%d" % h, "fi%d" % h, "K%d" % h
         decide(1, h, "zC", "LC", "xi1", R(fo, 0, 128), R(fo, 128, 256))
         ops[send(R(fo), R(fi), home)]["lead"] = OPT["lead"][1] * (1 - h)
-    counted("m1")
+    counted("m1", R("M", 384, 512))
     tt(R("ya1"), R("M", 128, 256), R("m1"), MU)
-    tt(R("yas"), R("M", 0, 128), R("ya1"), AD)
+    tt(R("yat"), R("M", 0, 128), R("ya1"), AD)
+    mm(R("G", 256, 384), R("yat"), If)
+    copy(R("yas"), R("G", 256, 384), "SV")
     dma("Y", T.ya[:], ap(R("yas")), [R("yas")], [], 1 << 16, chain=False)
     for h in range(2):
         fi, kb = "fi%d" % h, "K%d" % h
@@ -783,15 +831,18 @@ def rank_program(g, core, T, topo):
         PLAN.clear()
         PLAN["opt"] = repr(OPT)
         PLAN["ops"] = ops
-        for _ in range(OPT["rounds"]):
-            plan = forward(prio)
-            PLAN.setdefault("ends", []).append(round(plan[0], 1))
-            if len(plan) == 1:
-                break
-            if "plan" not in PLAN or plan[0] < PLAN["plan"][0]:
-                PLAN["plan"], keep = plan, prio
-            prio = backward(plan[2], plan[4])
-        plan, rng = PLAN["plan"], np.random.default_rng(OPT["seed"])
+        rng, chains = np.random.default_rng(OPT["seed"]), prio
+        for start in range(OPT["starts"]):
+            prio = [p + OPT["eps"] * rng.random() * (start > 0) for p in chains]
+            for _ in range(OPT["rounds"]):
+                plan = forward(prio)
+                if len(plan) == 1:
+                    break
+                if "plan" not in PLAN or plan[0] < PLAN["plan"][0]:
+                    PLAN["plan"], keep = plan, prio
+                    PLAN.setdefault("ends", []).append(round(plan[0], 1))
+                prio = backward(plan[2], plan[4])
+        plan = PLAN["plan"]
         for step in range(OPT["tries"]):
             i, pairs = max(range(nop), key=lambda j: plan[4][j]), []
             while i is not None:
@@ -803,7 +854,18 @@ def rank_program(g, core, T, topo):
             for k in rng.choice(len(pairs), min(len(pairs), OPT["swap"]), replace=False):
                 i, j = pairs[int(k)]
                 prio[i], prio[j] = max(prio[i], prio[j]) + 0.3 * rng.random(), min(prio[i], prio[j]) - 0.3 * rng.random()
-            if step % 8 == 7:
+            if step % 2:
+                prio, up = list(keep), OPT["up"] * rng.random()
+                i = pairs[int(rng.integers(len(pairs)))][0]
+                todo, seen = [i], {i}
+                while todo:
+                    j = todo.pop()
+                    prio[j] += up
+                    for d in ops[j]["deps"] | ops[j]["order"]:
+                        if d not in seen and plan[4][d] > plan[4][i] - OPT["win"]:
+                            seen.add(d)
+                            todo.append(d)
+            if step % 16 == 14:
                 prio = backward(plan[2], plan[4])
             new = forward(prio)
             if new[0] <= plan[0] + OPT["tol"]:

@@ -11,21 +11,21 @@ SB = {
     "KLc": (128, B), "io": (144, B), "g16": (8, B), "mg": (128, B), "e32": (512, B), "EXP": (512, B), "io2k": (2304, F),
     "ones": (128, B), "cq": (256, B), "c175": (256, B), "wrow": (256, F), "maskJ": (256, B), "IM": (768, B), "If": (128, F),
     "RST": (256, B), "RSD": (128, F), "W16": (16, B), "B8": (16, B), "W8": (16, B), "B8f": (16, F), "BB4": (128, B),
-    "SelC": (32, H), "WY": (24, H), "B128": (8, B), "B8i": (8, H),
-    "XB": (2048, B), "HI": (2304, B), "LO": (2304, B), "m0": (128, B), "Sb": (128, B), "m1": (128, B),
+    "flagN": (256, B), "SelC": (16, H), "WY": (24, H), "B128": (8, B), "B8i": (8, H),
+    "XB": (2304, B), "HI": (2304, B), "LO": (2304, B), "m0": (128, B), "Sb": (128, B), "m1": (128, B),
     "zT": (256, B), "xg": (4096, B), "ab": (4096, B), "c16": (256, U), "cf": (256, H), "H": (256, B), "ad": (256, B),
-    "mk": (256, B), "R": (512, F), "wi": (32, I), "wa": (32, I), "wb": (32, B), "wT": (512, B),
+    "mk": (256, B), "R": (512, I), "wi": (32, I), "wa": (32, I), "wb": (32, B), "wT": (512, B),
     "vlA": (16, U), "v1o0": (16, U), "v2o0": (16, U), "v1o1": (16, U), "v2o1": (16, U), "vlB": (16, U), "loB": (16, U),
     "lo1": (16, U), "vi": (32, I), "xo0": (256, B), "xo1": (256, B),
     "zx0": (4096, B), "zx1": (4096, B), "mh": (4096, B), "ml": (4096, B), "eh": (512, B), "en": (512, B), "Lf": (256, H),
     "r1": (256, H), "r2": (256, H), "ab2": (256, B), "hb": (256, B), "sl": (256, B), "tl": (256, B), "sc": (256, B),
-    "w": (256, B), "fk": (256, B), "R2": (256, F), "flag": (256, B), "e2": (256, H), "NP": (128, H), "ce": (256, H),
+    "w": (256, B), "fk": (256, B), "R2": (256, I), "flag": (256, B), "e2": (256, H), "NP": (128, H), "ce": (256, H),
     "qs": (256, F), "qi": (128, I), "qb": (96, B), "ul": (16, U), "ulo": (16, U), "OH": (2048, B), "gm": (768, H),
     "adu": (256, B), "ad2": (256, B), "mn": (256, B), "e12": (32, U), "u2": (16, U), "nB": (256, B), "nH": (256, B),
     "nL": (256, B), "Lo0": (256, U), "zo1": (256, B), "Lo1": (256, U), "fo0": (264, H), "fo1": (264, H), "out": (512, F),
     "wzB": (768, B), "LB": (256, U), "v1i0": (16, U), "v2i0": (16, U), "xi0": (256, B), "wzC": (768, B), "LC": (256, U),
     "zs": (16, U), "gu": (512, H), "gl": (256, H), "B64": (16, H), "g32": (8, B), "OHh": (256, B), "wcol": (2, B),
-    "nW16": (16, B), "St": (128, B), "m0t": (128, B), "yat": (128, F),
+    "Z2": (144, B), "St": (128, B), "m0t": (128, B), "yat": (128, F),
     "v1i1": (16, U), "v2i1": (16, U), "xi1": (256, B), "fi0": (264, H), "fi1": (264, H),
     "yvs": (256, F), "ya1": (128, F), "ya2": (128, F), "yas": (128, F),
 }
@@ -45,8 +45,8 @@ for _d in _use:
 for _n, _w in PS.items():
     SCRATCH[_n] = ("psum", [128, _w], "float32")
 SEMAPHORES = ["cV", "cS", "cT", "cG"] + ["d%d" % i for i in range(30)] + ["a%d" % i for i in range(30)] + ["l%d" % i for i in range(30)]
-OPT = {"tch": 512, "look": 0.35, "ef": "G", "exp": ("SG", "G"), "load": ("0zv", "1LXE"), "ahead": 2, "short": 0, "cyT": 0.6e-3, "f": 1.15, "ga": 1.56, "wake": 0.13, "rate": 230e3, "land": 1.7, "s16": "SV", "lead": (0.0, 5.0), "enS": ((1, 0), (0, 0)), "patch": ((0, 0), (0, 0)),
-       "xg": (("S", "S"), ("S", "S")), "sm": "SV", "expw": ("S", "G"), "B": "S", "vx": ((1, 1), (0, 1)), "gS": ((0, 2), (1, 2)), "rounds": 4, "tries": 100, "swap": 10, "tol": 0.2, "seed": 0, "starts": 12, "eps": 2.0, "up": 3.0, "win": 8.0, "rot": 2, "rl": ((0, 0), (0, 0)), "tabS": 0, "Lo0": "V", "cfG": (0, 0), "one": 1}
+OPT = {"tch": 512, "look": 0.35, "ef": "G", "exp": ("SG", "G"), "load": ("0zvL", "1XE"), "ahead": 2, "short": 0, "cyT": 0.6e-3, "f": 1.15, "ga": 1.56, "wake": 0.13, "fixS": 0.0, "rate": 230e3, "land": 1.7, "s16": "SV", "lead": (0.0, 4.0), "enS": ((0, 0), (0, 0)), "patch": ((0, 0), (0, 0)),
+       "xg": (("S", "S"), ("S", "S")), "sm": "SV", "expw": ("S", "G"), "gfix": 0.23, "also": ((0.9, 0.75), (0.9, 1.0), (1.2, 1.25), (1.2, 0.8)), "B": "S", "vx": ((2, 1), (0, 1)), "gS": ((0, 2), (1, 2)), "rounds": 4, "tries": 250, "swap": 4, "tol": 0.15, "seed": 0, "starts": 16, "eps": 2.0, "up": 3.0, "win": 8.0, "rot": 0, "tr": ((0, 0, 0, 0), (0, 0, 0, 0)), "cut": (0, 0), "sx": 1, "two": (1, 1), "gw": ((32,), (32,)), "split": (0, 0), "rl": ((0, 0), (0, 0)), "tabS": 1, "Lo0": "V", "cfG": (0, 0), "one": 1}
 PLAN = {}
 
 
@@ -126,7 +126,7 @@ def rank_program(g, core, T, topo):
     def do(q, ins, out, fn, cyc, **kw):
         reads, writes = [], []
         n = size(out)
-        cost = max(64, n * cyc) * CY
+        cost = OPT["fixS"] + n * CY if q == "S" and OPT["fixS"] else max(64, n * cyc) * CY
         for r in ins:
             if isinstance(r, tuple):
                 if r[0] == "ind":
@@ -140,7 +140,9 @@ def rank_program(g, core, T, topo):
             cost = 0.05 + n * SCAT * CY
         else:
             writes.append(out)
-        return record(q, reads, writes, fn, kw.pop("cost", cost), **kw)
+        i = record(q, reads, writes, fn, kw.pop("cost", cost), **kw)
+        ops[i]["ind"] = n * (SCAT if out[0] == "ind" else GA if any(isinstance(r, tuple) and r[0] == "ind" for r in ins) else 0) * CY
+        return i
 
     def half(*rs):
         return 0.5 if all(narrow(r) for r in rs) else 1
@@ -189,12 +191,17 @@ def rank_program(g, core, T, topo):
 
     def gcopy(out, a):
         n = size(out)
-        return do("G", [a], out, lambda: g.affine_select(ap(out), ap(a), [[0, n]], OP.is_ge, 0.0, 0, 0), 1, cost=0.17 + 2 * n * CY)
+        return do("G", [a], out, lambda: g.affine_select(ap(out), ap(a), [[0, n]], OP.is_ge, 0.0, 0, 0), 1, cost=OPT["gfix"] + 2 * n * CY)
 
     def copy(out, a, qs, scale=None):
         ways = {"G": lambda: gcopy(out, a), "S": lambda: act(out, a, AF.Copy, None, scale),
                 "V": lambda: cp(out, a) if scale is None else ts(out, a, scale, OP.mult)}
         return either(*[ways[q] for q in qs])
+
+    def plus(out, a, c=0.0):
+        if not OPT["sx"]:
+            return ts(out, a, c, OP.add)
+        return either(lambda: ts(out, a, c, OP.add), lambda: act(out, a, AF.Identity, c, 1.0))
 
     def either(*ways):
         first = len(ops)
@@ -302,6 +309,7 @@ def rank_program(g, core, T, topo):
         ts(C(36 + h), PK, 64.0 + 128.0 * h, AD)
         ts(R("B64", *hm(h)), R("gp", 0, 8), PG, EQ, 64.0 - 128.0 * h, MU)
     fill(R("eS", 2048, 2304), 0)
+    fill(R("XB", 2048, 2304), 0.0)
     ts(C(28), PK, 1.0, AD)
     ts(C(29), C(8), 16.0, MU, -1.0, AD)
     tt(C(31), C(9), C(8), SU)
@@ -317,7 +325,9 @@ def rank_program(g, core, T, topo):
     ts(If, R("iD"), 0.0, EQ)
     ts(R("EXP"), R("e32"), P32, EQ)
     ts(R("W16"), R("gp"), PG, EQ, 4096.0, MU)
-    ts(R("nW16"), R("gp"), PG, EQ, -4096.0, MU)
+    ts(C(23), P7, 16.0, MU, 16.0, AD)
+    ts(C(24), KY, -127.0, MU, 128.0, AD)
+    ts(R("Z2"), R("io"), C(23), EQ, C(24), MU)
     ts(R("maskJ"), R("kk"), 0.0, EQ, 33554432.0, MU)
     ts(R("RST"), R("maskJ"), -256.0, AD)
     ts(R("nI16"), R("iD"), 0.0, EQ, -1.0, MU)
@@ -331,8 +341,8 @@ def rank_program(g, core, T, topo):
     ts(R("B8h"), R("gp", 0, 8), PG, EQ)
     ts(R("BB4"), R("mg"), PG, EQ, 4096.0, MU)
     for out, c in ((R("B8", 0, 8), 1.0), (R("B8", 8, 16), -1.0), (R("W8", 0, 8), C(20)), (R("W8", 8, 16), C(21)),
-                   (R("B8f", 0, 8), 1.0), (R("B8i"), 0.5), (R("SelC", 0, 8), C(31)), (R("SelC", 8, 16), C(8)),
-                   (R("SelC", 16, 24), C(9)), (R("SelC", 24, 32), C(10)), (R("WY", 0, 8), C(28)), (R("WY", 8, 16), C(29)),
+                   (R("B8f", 0, 8), 1.0), (R("B8i"), 0.5), (R("SelC", 0, 8), C(8)),
+                   (R("SelC", 8, 16), C(10)), (R("WY", 0, 8), C(28)), (R("WY", 8, 16), C(29)),
                    (R("WY", 16, 24), C(30))):
         ts(out, R("gp", 0, 8), PG, EQ, c, MU)
     B8p, B8n = R("B8", 0, 8), R("B8", 8, 16)
@@ -353,17 +363,13 @@ def rank_program(g, core, T, topo):
         mm(R("N0", 64 * b, 64 * b + 64), R("tf", b, 512, 4, (0, 64)), R("I16", 0, 64, 1, (0, 64)))
     cp(R("el"), R("N0", 0, 256))
     for b in range(4):
-        c = R("XB", 512 * b, 512 * b + 512)
+        c = R("XB", b, 2048, 4)
         copy(c, IND(R("xS"), R("el", 64 * b + 32, 64 * b + 64)), OPT["B"])
         if b >= 4 - OPT["tabS"]:
-            a, r = R("sh", 512 * b, 512 * b + 512), R("so", 512 * b, 512 * b + 512)
+            a, bank = R("sh", 512 * b, 512 * b + 512), R("K%d" % (b % 2))
             act(a, IND(R("xS"), R("el", 64 * b, 64 * b + 32)), AF.Copy)
-            for j, (u, v, sign, f, dst) in enumerate(((a, c, nI, AF.Relu, r), (c, r, Ib, AF.Copy, R("HI", b, 2048, 4)),
-                                                      (a, r, nI, AF.Copy, R("LO", b, 2048, 4)))):
-                bank = ("K0", "K1", "N1")[j]
-                mm(R(bank), sign, v, True, False)
-                mm(R(bank), Ib, u, False, True)
-                act(dst, R(bank), f)
+            mm(bank, Ib, a)
+            ids += [tt(R("HI", b, 2048, 4), bank, c, MX), tt(R("LO", b, 2048, 4), bank, c, MN)]
             continue
         for tab, op in (("HI", MX), ("LO", MN)):
             ids.append(tt(R(tab, b, 2048, 4), IND(R("xS"), R("el", 64 * b, 64 * b + 32)), c, op))
@@ -385,21 +391,36 @@ def rank_program(g, core, T, topo):
             if a < b:
                 ids += [copy(R(zx, 16 * a + k, 16 * b, 16), R(z, a, b), OPT["exp"][t]) for k in range(16)]
         chain(ids)
-        for h in range(2):
-            a, b = 128 * h + 128 - 32 * max(OPT["vx"][t]), 128 * h + 128
-            if a < b:
-                chain([copy(R("zw", 16 * a + k, 16 * b, 16), R(zwalk, a, b), OPT["expw"][t]) for k in range(16)])
+        a, b = 128 - 32 * max(OPT["vx"][t]), 128 + 32 * max(OPT["vx"][t])
+        if OPT["expw"][t] == "G":
+            chain([gcopy(R("zw", 16 * a + k, 16 * b, 16), R(zwalk, a, b)) for k in range(16 * (a < b))])
+        else:
+            for c in range(a, b, 32):
+                copy(R("zw", 16 * c, 16 * c + 512), IND(R(zwalk, c, c + 32), R("zl")), OPT["expw"][t])
 
-    def tolist(h, parts, out, add, lo=None):
+    def tolist(h, parts, out, add, lo, byT):
         kb = "K%d" % h
         a = 256 * h
+        if byT:
+            P16, n = (0, 16), 2 if lo else 1
+            cp(R("wb", 16 * h, 16 * h + 16), parts)
+            mm(R(kb, 384, 512, 1, P16), R("wb", 16 * h, 16 * h + 16), Ib)
+            copy(R("wT", a, a + 128, 1, P16), R(kb, 384, 512, 1, P16), "SV")
+            if lo:
+                copy(R("wT", a + 128, a + 256, 1, P16), R(kb, 384, 512, 1, P16), "SV", R("col", 4, 5, 1, P16))
+            for j in range(16):
+                mm(R(kb, 256, 256 + 8 * n), R("Z2", 16 - j, 144 - j, 1, P16), R("wT", a + j, a + 128 * n, 16, P16), j == 0, j == 15)
+            ts(R(out, *hm(h)), R(kb, 256, 264), add, AD)
+            if lo:
+                cp(R(lo, *hm(h)), R(kb, 264, 272))
+            return
         tt(R("wT", a, a + 256), IND(parts, R("zl", 0, 16)), R("maskJ"), MU)
         mm(R(kb, 256, 264), R("wT", a, a + 128), R("B128"), True, False)
         mm(R(kb, 256, 264), R("wT", a + 128, a + 256), B8p, False, True)
-        ts(R(out, *hm(h)), R(kb, 256, 264), add, AD)
+        plus(R(out, *hm(h)), R(kb, 256, 264), add)
         if lo:
             mm(R(kb, 264, 272), R("wT", a + 128, a + 256), B8p)
-            cp(R(lo, *hm(h)), R(kb, 264, 272))
+            plus(R(lo, *hm(h)), R(kb, 264, 272))
 
     def masked(h, win, at, slot, n=1, base=False):
         kb, gm, one = "K%d" % h, "gm32" if base else "gm", R("B8f" if base else "B8h", 0, 8)
@@ -431,49 +452,45 @@ def rank_program(g, core, T, topo):
 
     def walk(t, step, h, vl, lo, out, outlo=None):
         n, m, kb = hn(h), hm(h), "K%d" % h
-        cp(R("c16", *n), IND(R("eS", 0, 2048), R(vl, *m)))
+        plus(R("c16", *n), IND(R("eS", 0, 2048), R(vl, *m)))
         if OPT["cfG"][t]:
             either(lambda: gcopy(R("cf", *n), R("c16", *n)), lambda: ts(R("cf", *n), R("c16", *n), 0.0, AD))
         else:
-            ts(R("cf", *n), R("c16", *n), 0.0, AD)
-        ts(R("H", *n), R("c16", *n), 16448.5, AD)
+            plus(R("cf", *n), R("c16", *n))
+        plus(R("H", *n), R("c16", *n), 16448.5)
         onV = OPT["vx"][t][step]
         for j in range(4):
             b = 2048 * h + 512 * j
             x = IND(R("xS"), R("c16", b // 16, b // 16 + 32))
-            if j < 4 - onV:
-                i = copy(R("xg", b, b + 512), x, OPT["xg"][t][step])
-                ops[i]["order" if OPT["xg"][t][step] == "S" else "deps"].update(behind[-OPT["ahead"]:][:1])
+            if (j >= onV if h else j < 4 - onV):
+                ops[act(R("xg", b, b + 512), x, AF.Copy)]["order"].update(behind[-OPT["ahead"]:][:1])
                 behind.append(minus_z(R("xg", b, b + 512), b, "zT", AF.Abs, R("ab", b, b + 512)))
             else:
                 tt(R("xg", b, b + 512), x, R("zw", b, b + 512), SU)
-                if OPT["rl"][t][step]:
-                    ts(R("ab", b, b + 512), R("xg", b, b + 512), 0.0, MX, 2.0, MU)
-                else:
-                    act(R("ab", b, b + 512), R("xg", b, b + 512), AF.Abs)
+                act(R("ab", b, b + 512), R("xg", b, b + 512), AF.Abs)
         mm(R(kb, 0, 256), R("H", *n), PHI, True, False)
-        if onV and OPT["rl"][t][step]:
-            for k in range(16):
-                mm(R(kb, k, 256, 16, (128 - 32 * onV, 128)), R("xg", 2048 * h + 2048 - 512 * onV + k, 2048 * h + 2048, 16), R("nW16"), False, False)
         mm(R(kb, 128, 256), R("cf", *n), I16, False, False)
         if lo:
             apart(R("ad", *n), R(vl, *m))
             tt(R("mk", *n), IND(R("m0"), R(lo, *m)), R("ad", *n), GT)
-        for k in range(16):
-            mm(R(kb, k, 256, 16), R("ab", 2048 * h + k, 2048 * h + 2048, 16), R("W16"), False, k == 15 and not lo)
+        for p in ((0, 96), (96, 128)) if OPT["cut"][t] else ((0, 128),):
+            for k in range(16):
+                i = mm(R(kb, k, 256, 16, p), R("ab", 2048 * h + 16 * p[0] + k, 2048 * h + 16 * p[1], 16), R("W16"), False,
+                       k == 15 and not lo)
+                if p[1] < 128:
+                    ops[i]["grp"] = (kb, False, False)
         if lo:
             mm(R(kb, 0, 256, 16), R("mk", *n), R("W16"), False, True)
         scan(R("R", 256 * h, 256 * h + 256), R("RST"), R(kb, 0, 256), 0.0, AD, MN)
         a = (16 * h, 16 * h + 16)
-        cp(R("wi", *a), R("R", 256 * h + 15, 256 * h + 256, 16))
-        ts(R("wa", *a), R("wi", *a), 127, AN)
-        tolist(h, R("wa", *a), out, -128.0, outlo)
+        ts(R("wa", *a), R("R", 256 * h + 15, 256 * h + 256, 16), 127, AN)
+        tolist(h, R("wa", *a), out, -128.0, outlo, OPT["tr"][t][2 * step + h])
 
     gaps = []
 
     def gap(t, h, z, L16, zx, ini):
         onS, known, n = OPT["gS"][t][h], OPT["patch"][t][h], hn(h)
-        ts(R("Lf", *n), R(L16, *n), C(18 + t), MU)
+        copy(R("Lf", *n), R(L16, *n), "VS" if OPT["sx"] else "V", C(18 + t))
         for e in range(2):
             copy(R("r%d" % (e + 1), *n), IND(R("io2k"), R(ini[e], *hm(h))), OPT["s16"], C(8 + 2 * t + e))
         if known:
@@ -491,7 +508,11 @@ def rank_program(g, core, T, topo):
             for tab, dst, sb in (("HI", "mh", "sh"), ("LO", "ml", "so")):
                 x = IND(R(tab, 0, 2048), R(L16, n0, n0 + 32))
                 if j < 4 - onS:
-                    gaps.append(tt(R(dst, *a), x, R(zx, *a), MX))
+                    at = n0
+                    for w in OPT["gw"][t]:
+                        c = (16 * at, 16 * (at + w))
+                        gaps.append(tt(R(dst, *c), IND(R(tab, 0, 2048), R(L16, at, at + w)), R(zx, *c), MX))
+                        at += w
                 else:
                     act(R(sb, *a), x, AF.Copy)
                     minus_z(R(sb, *a), a[0], "zT2", AF.Relu, R(dst, *a))
@@ -561,51 +582,61 @@ def rank_program(g, core, T, topo):
         tt(Q(1), R(nb, 264, 272), Q(0), MU)
         tt(QI(0), R(nb, 272, 280), Q(1), AD)
         ts(QI(1), QI(0), 2047, AN)
-        cp(R("NP", 0, 128, 16), QI(1))
+        plus(R("NP", 0, 128, 16), QI(1))
         mm(s3, R("NP"), I16)
-        cp(R("eS", 2048, 2304, 2), s3)
+        plus(R("eS", 2048, 2304, 2), s3)
         either(lambda: act(R("fk", *n), R("G", *n), AF.Relu, 262144.0 * (TAU[t] + 0.5), -262144.0),
                lambda: ts(R("fk", *n), R("G", *n), float(TAU[t]), LE, 131072.0, MU))
         key = R(kb, 0, 128)
         acc(key, [(r, I16) for r in log] + [(R("ones", p=ROW), R("KLc", p=ROW)), (sl, R("BB4")), (Ib, R("fk", *n))])
         scan(R("R2", *n), R("RSD"), key, 0.0, MX, MN)
         end = R("R2", 128 * h + 15, 128 * h + 128, 16)
-        cp(QI(2), end)
-        ts(QI(5), QI(2), 4095, AN)
+        ts(QI(5), end, 4095, AN)
         ts(Q(7), end, 65536.0, LT, 2.0, MU)
         tt(QI(6), Q(7), Q(0), SU)
         ul, ce = R("ul", *m), R("ce", *n)
-        tt(R("gu", 256 * h, 256 * h + 256), IND(QI(5, 16), R("zl", 0, 16)), R("maskJ"), MU)
+        if OPT["two"][t]:
+            for j in range(2):
+                tt(R("gu", 256 * h + 128 * j, 256 * h + 128 * j + 128), IND(QI(5 + j), R("zl", 0, 8)), R("maskJ", 0, 128), MU)
+        else:
+            tt(R("gu", 256 * h, 256 * h + 256), IND(QI(5, 16), R("zl", 0, 16)), R("maskJ"), MU)
         mm(R(kb, 256, 264), R("gu", 256 * h, 256 * h + 128), R("B8h"))
-        cp(ul, R(kb, 256, 264))
-        cp(ce, IND(R("eS"), ul))
-        ts(QI(3), QI(2), 7, SH, 31, AN)
-        ts(QI(4), QI(2), 127, AN)
+        plus(ul, R(kb, 256, 264))
+        plus(ce, IND(R("eS"), ul))
+        ts(QI(3), end, 7, SH, 31, AN)
+        ts(QI(4), end, 127, AN)
         cp(QB(0), QI(4))
         acc(R(kb, 312, 320), [(R("gu", 256 * h + 128, 256 * h + 256), R("B64", *m)), (R("ones", p=ROW), R("g16", p=ROW))])
-        ts(R("zs", *m), R(kb, 312, 320), C(36 + h), AD)
+        plus(R("zs", *m), R(kb, 312, 320), C(36 + h))
         copy(zo, IND(R("w" + z, 384 * h, 384 * h + 384), R("zs", *m)), OPT["s16"] if t else "SV")
         tt(R("flag", *n), key, R("R2", *n), EQ)
         if t == 0:
             tt(R("gl", *n), IND(QI(4), R("zl", 0, 8)), R("maskJ", 0, 128), MU)
             mm(R(kb, 264, 272), R("gl", *n), R("B8h"))
-            cp(R("ulo", *m), R(kb, 264, 272))
+            plus(R("ulo", *m), R(kb, 264, 272))
             apart(R("adu", *n), ul)
-            mm(R(kb, 128, 152), ce, R("SelC", 8, 32))
-            copy(Q(2, 24), R(kb, 128, 152), "SV")
+            mm(R(kb, 128, 144), ce, R("SelC"))
+            copy(Q(2, 16), R(kb, 128, 144), "SV")
             vo = Q(2)
             masked(h, vo, 384 * h, 272)
-            ts(R("vlB", *m), R(kb, 272, 280), 0.0, AD)
-            cp(R("vi", 16 * h, 16 * h + 8), R(kb, 272, 280))
+            plus(R("vlB", *m), R(kb, 272, 280))
+            plus(R("vi", 16 * h, 16 * h + 8), R(kb, 272, 280))
             ts(R("vi", 16 * h + 8, 16 * h + 16), R("vi", 16 * h, 16 * h + 8), 127, AN)
-            cp(R("loB", *m), R("vi", 16 * h + 8, 16 * h + 16))
+            plus(R("loB", *m), R("vi", 16 * h + 8, 16 * h + 16))
         else:
-            mm(R(kb, 128, 136), ce, R("SelC", 8, 16))
-            cp(R("fo%d" % h, 256, 264), R(kb, 128, 136))
-        acc(R(kb, 384, 512), [(ce, R("Sel0"))] + [(r, R("nI16")) for r in log])
-        tt(R("e2", *n), R(kb, 384, 512), R("flag", *n), MU)
-        acc(s3, [(R("e2", *n), I16)] + [(I16, r) for r in log])
-        copy(Lo, s3, OPT["s16"] if t else "V")
+            mm(R(kb, 128, 136), ce, R("SelC", 0, 8))
+            copy(R("fo%d" % h, 128, 136), R(kb, 128, 136), OPT["s16"])
+        if t == 0:
+            acc(R(kb, 384, 512), [(ce, R("Sel0"))] + [(r, R("nI16")) for r in log])
+            tt(R("e2", *n), R(kb, 384, 512), R("flag", *n), MU)
+            acc(s3, [(R("e2", *n), I16)] + [(I16, r) for r in log])
+            plus(Lo, s3)
+        else:
+            first = [acc(s1, [(I16, r) for r in log]), mm(s3, R("flag", *n), Ib)]
+            copy(R("flagN", *n), s3, "SV")
+            acc(s0, [(R("nI16"), r) for r in log] + [(R("Sel0"), ce)], first)
+            tt(R("e2", *n), s0, R("flagN", *n), MU)
+            tt(Lo, s1, R("e2", *n), AD)
         tt(R("OHh", *n), IND(QI(3), R("zl", 0, 8)), R("kk", 0, 128), EQ)
         ids = []
         for c in range(8):
@@ -614,11 +645,11 @@ def rank_program(g, core, T, topo):
             mm(R("M", 384 + 16 * c, 400 + 16 * c), a, R("OHh", 128 * h + 16 * c, 128 * h + 16 * c + 16), h == 0 and c == 0, h == 1 and c == 7)
         chain(ids)
         if t == 0:
-            masked(h, Q(3, 16), 384 * h + 128, 280, 2)
-            ts(R("e12", 16 * h, 16 * h + 16), R(kb, 280, 296), 0.0, AD)
-            copy(R("nB", *n), IND(R("xS"), R("e12", 16 * h + 8, 16 * h + 16)), "SV")
-            tt(R("nH", *n), IND(R("xS"), R("e12", 16 * h, 16 * h + 8)), R("nB", *n), MX)
-            tt(R("nL", *n), IND(R("xS"), R("e12", 16 * h, 16 * h + 8)), R("nB", *n), MN)
+            masked(h, Q(3), 384 * h + 128, 280)
+            plus(R("e12", *m), R(kb, 280, 288))
+            copy(R("nB", *n), IND(R("xS"), R("e12", *m)), "SV")
+            tt(R("nH", *n), IND(R("XB"), ul), R("nB", *n), MX)
+            tt(R("nL", *n), IND(R("XB"), ul), R("nB", *n), MN)
             either(lambda: act(R("ad2", *n), R("adu", *n), AF.Relu, 9e29, -9e29),
                    lambda: ts(R("ad2", *n), R("adu", *n), 1.0, LT, 9e29, MU))
             ts(Q(6), QI(5), C(25), SU)
@@ -633,7 +664,7 @@ def rank_program(g, core, T, topo):
         ts(R("qs", a + 56, a + 64), R(kb, 296, 304), C(34 + h), LE)
         tt(R("qs", a + 64, a + 72), R("qs", a + 56, a + 64), R("qs", a + 48, a + 56), MU)
         masked(h, R("qs", a + 64, a + 72), 128 * h, 304, 1, True)
-        ts(R("u2", *m), R(kb, 304, 312), C(27), AD)
+        plus(R("u2", *m), R(kb, 304, 312), C(27))
         cp(IND(R("HI"), R("u2", *m)), R("nH", *n))
         cp(IND(R("LO"), R("u2", *m)), R("nL", *n))
 
@@ -689,8 +720,9 @@ def rank_program(g, core, T, topo):
     visit(1, "vlB", "loB", "v1o1", "v2o1", "xo1", "zC", "LC", "zx1", ("v1i1", "v2i1", "xi1"))
     for h in range(2):
         fo, fi, kb = "fo%d" % h, "fi%d" % h, "K%d" % h
-        decide(1, h, "zC", "LC", "xi1", R(fo, 0, 128), R(fo, 128, 256))
-        ops[send(R(fo), R(fi), home)]["lead"] = OPT["lead"][1] * (1 - h)
+        decide(1, h, "zC", "LC", "xi1", R(fo, 0, 128), R(fo, 136, 264))
+        for a, b in ((0, 136), (136, 264)) if OPT["split"][h] else ((0, 264),):
+            ops[send(R(fo, a, b), R(fi, a, b), home)]["lead"] = OPT["lead"][1] * (1 - h)
     counted("m1", R("M", 384, 512))
     tt(R("ya1"), R("M", 128, 256), R("m1"), MU)
     tt(R("yat"), R("M", 0, 128), R("ya1"), AD)
@@ -702,10 +734,10 @@ def rank_program(g, core, T, topo):
         a, b = hn(h)
         oz, ol = R("out", 2 * a, 2 * a + 128), R("out", 2 * a + 128, 2 * b)
         cp(oz, R(fi, 0, 128))
-        copy(ol, R(fi, 128, 256), OPT["s16"])
+        copy(ol, R(fi, 136, 264), OPT["s16"])
         dma("Y", T.yz[:, a:b], ap(oz), [oz], [], 1 << 16, chain=False)
         dma("S", T.yl[:, a:b], ap(ol), [ol], [], 1 << 16, chain=False)
-        mm(R(kb, 384, 512, 1, (0, 8)), R(fi, 256, 264), I16)
+        mm(R(kb, 384, 512, 1, (0, 8)), R(fi, 128, 136), I16)
         copy(R("yvs", a, b, 1, (0, 8)), R(kb, 384, 512, 1, (0, 8)), "SV")
         dma("Y", T.yv[:, a:b], ap(R("yvs", a, b, 1, (0, 8))), [R("yvs", a, b)], [], 1 << 12, chain=False)
 
@@ -827,6 +859,30 @@ def rank_program(g, core, T, topo):
                     cand[queue[d]].append(d)
         return back
 
+    def spread(plan):
+        if len(plan) == 1:
+            return 1e9
+        total = 0.0
+        for f, ga in OPT["also"]:
+            free, fin, engines = {}, [0.0] * nop, 0.0
+            for i in plan[1]:
+                o, q = ops[i], plan[2][i]
+                t = free.get(q, 0.0) if q != "A" else max(fin[d] for d in o["order"])
+                for d in o["deps"]:
+                    t = max(t, fin[d] + WAKE)
+                for d in plan[3][i]:
+                    t = max(t, fin[d] + WAKE)
+                c = o["alt"][q][1]
+                if o["kind"] == "op":
+                    c = c + o["ind"] * (f * ga - 1) if o["ind"] else c * f
+                free[q] = t + c
+                if o["kind"] == "dma":
+                    engines = fin[i] = max(free[q] + 1.8, engines) + o["lat"]
+                else:
+                    fin[i] = free[q] + o["lat"]
+            total += max(fin) / (f * (1 + ga) / 2 + 0.2)
+        return total / len(OPT["also"])
+
     if PLAN.get("opt") != repr(OPT):
         PLAN.clear()
         PLAN["opt"] = repr(OPT)
@@ -838,6 +894,7 @@ def rank_program(g, core, T, topo):
                 plan = forward(prio)
                 if len(plan) == 1:
                     break
+                plan = (spread(plan),) + plan[1:]
                 if "plan" not in PLAN or plan[0] < PLAN["plan"][0]:
                     PLAN["plan"], keep = plan, prio
                     PLAN.setdefault("ends", []).append(round(plan[0], 1))
@@ -868,6 +925,7 @@ def rank_program(g, core, T, topo):
             if step % 16 == 14:
                 prio = backward(plan[2], plan[4])
             new = forward(prio)
+            new = (spread(new),) + new[1:]
             if new[0] <= plan[0] + OPT["tol"]:
                 plan, keep = new, prio
             if new[0] < PLAN["plan"][0]:

import numpy as np
from concourse.mybir import AluOpType as OP, ActivationFunctionType as AF

F, B, I, U, H = "float32", "bfloat16", "int32", "uint16", "float16"
SB = {
    "I16": (128, H), "B8h": (8, H), "gm32": (256, F), "zw": (4096, B), "sh": (4096, B), "so": (4096, B), "zT2": (256, B), "es": (1024, B),
    "Lp": (256, U), "Lq": (256, H), "nI16": (128, H), "ROT": (128, H), "Sel0": (128, H), "nE": (256, F),
    "eS": (2304, I), "xS": (2048, B), "zA": (256, B), "LA": (256, I), "vA": (16, I), "ef": (2048, H),
    "t0": (512, I), "tf": (512, H), "el": (256, U), "ys": (384, F),
    "iC": (8, I), "iN": (32, I), "zl": (32, U), "col": (48, F), "iD": (128, B), "gp": (16, B), "kk": (256, B), "ck": (256, B),
    "KLc": (128, B), "io": (144, B), "g16": (8, B), "mg": (128, B), "e32": (512, B), "EXP": (512, B), "io2k": (2304, F),
    "ones": (128, B), "cq": (256, B), "c175": (256, B), "wrow": (256, F), "maskJ": (256, B), "IM": (768, B), "If": (128, F),
    "RST": (256, B), "RSD": (128, F), "W16": (16, B), "B8": (16, B), "W8": (16, B), "B8f": (16, F), "BB4": (128, B),
    "flagN": (256, B), "SelC": (16, H), "WY": (24, H), "B128": (8, B), "B8i": (8, H),
    "XB": (2304, B), "HI": (2304, B), "LO": (2304, B), "m0": (128, B), "Sb": (128, B), "m1": (128, B),
    "zT": (256, B), "xg": (4096, B), "ab": (4096, B), "c16": (256, U), "cf": (256, H), "H": (256, B), "ad": (256, B),
    "mk": (256, B), "R": (512, I), "wi": (32, I), "wa": (32, I), "wb": (32, B), "wT": (512, B),
    "vlA": (16, U), "v1o0": (16, U), "v2o0": (16, U), "v1o1": (16, U), "v2o1": (16, U), "vlB": (16, U), "loB": (16, U),
    "lo1": (16, U), "vi": (32, I), "xo0": (256, B), "xo1": (256, B),
    "zx0": (4096, B), "zx1": (4096, B), "mh": (4096, B), "ml": (4096, B), "eh": (512, B), "en": (512, B), "Lf": (256, H),
    "r1": (256, H), "r2": (256, H), "ab2": (256, B), "hb": (256, B), "sl": (256, B), "tl": (256, B), "sc": (256, B),
    "w": (256, B), "fk": (256, B), "R2": (256, I), "flag": (256, B), "e2": (256, H), "NP": (128, H), "ce": (256, H),
    "qs": (256, F), "qi": (128, I), "qb": (96, B), "ul": (16, U), "ulo": (16, U), "OH": (2048, B), "gm": (768, H),
    "adu": (256, B), "ad2": (256, B), "mn": (256, B), "e12": (32, U), "u2": (16, U), "nB": (256, B), "nH": (256, B),
    "nL": (256, B), "Lo0": (256, U), "zo1": (256, B), "Lo1": (256, U), "fo0": (264, H), "fo1": (264, H), "out": (512, F),
    "wzB": (768, B), "LB": (256, U), "v1i0": (16, U), "v2i0": (16, U), "xi0": (256, B), "wzC": (768, B), "LC": (256, U),
    "zs": (16, U), "gu": (512, H), "gl": (256, H), "B64": (16, H), "g32": (8, B), "OHh": (256, B), "wcol": (2, B),
    "Z2": (144, B), "St": (128, B), "m0t": (128, B), "yat": (128, F),
    "v1i1": (16, U), "v2i1": (16, U), "xi1": (256, B), "fi0": (264, H), "fi1": (264, H),
    "yvs": (256, F), "ya1": (128, F), "ya2": (128, F), "yas": (128, F),
}
PS = {"P0": 512, "P1": 512, "K0": 512, "K1": 512, "N0": 512, "N1": 512, "G": 512, "M": 512}
SCRATCH = {}
PLACE = {}
_use = {F: 0, B: 0, I: 0, U: 0, H: 0}
for _n, (_w, _d) in SB.items():
    if _w > 600:
        SCRATCH[_n] = ("sbuf", [128, _w], _d)
        PLACE[_n] = (_n, 0)
    else:
        PLACE[_n] = ("all_" + _d, _use[_d])
        _use[_d] += -(-_w // 32) * 32
for _d in _use:
    SCRATCH["all_" + _d] = ("sbuf", [128, _use[_d]], _d)
for _n, _w in PS.items():
    SCRATCH[_n] = ("psum", [128, _w], "float32")
SEMAPHORES = ["cV", "cS", "cT", "cG"] + ["d%d" % i for i in range(30)] + ["a%d" % i for i in range(30)] + ["l%d" % i for i in range(30)]
OPT = {"tch": 512, "look": 0.35, "ef": "G", "exp": ("SG", "G"), "load": ("0zvL", "1XE"), "ahead": 2, "short": 0, "cyT": 0.6e-3, "f": 1.15, "ga": 1.56, "wake": 0.13, "fixS": 0.0, "rate": 230e3, "land": 1.7, "s16": "SV", "lead": (0.0, 4.0), "enS": ((0, 0), (0, 0)), "patch": ((0, 0), (0, 0)),
       "xg": (("S", "S"), ("S", "S")), "sm": "SV", "expw": ("S", "G"), "gfix": 0.23, "also": ((0.9, 0.75), (0.9, 1.0), (1.2, 1.25), (1.2, 0.8)), "B": "S", "vx": ((2, 1), (0, 1)), "gS": ((0, 2), (1, 2)), "rounds": 4, "tries": 250, "swap": 4, "tol": 0.15, "seed": 0, "starts": 16, "eps": 2.0, "up": 3.0, "win": 8.0, "rot": 0, "tr": ((0, 0, 0, 0), (0, 0, 0, 0)), "cut": (0, 0), "sx": 1, "two": (1, 1), "gw": ((32,), (32,)), "split": (0, 0), "rl": ((0, 0), (0, 0)), "tabS": 1, "Lo0": "V", "cfG": (0, 0), "one": 1}
PLAN = {}


def rank_program(g, core, T, topo):
    rank = T.rank_of(core)
    if rank is None:
        return
    nR = len(T.cores)
    HOP = 3
    TH, TAU = 1020, (1020, 1530)
    nxt, home = T.cores[(rank + HOP) % nR], T.cores[(rank - 2 * HOP) % nR]
    CY, GA, SCAT, WAKE = 0.83e-3 * OPT["f"], OPT["ga"], 3.8, OPT["wake"]

    QS = {"V": g.vector, "S": g.scalar, "T": g.tensor, "G": g, "Y": g.sync}
    ops = []
    hist = {}

    def track(name):
        if name not in hist:
            hist[name] = {"w": np.full(SB[name][0] if name in SB else 512, -1), "r": {}}
        return hist[name]

    def record(q, reads, writes, fn, cost, kind="op", lat=0.0, grp=None, after=(), sem=None, inc=1):
        me = len(ops)
        deps = set()
        for r in reads + writes:
            deps.update(int(i) for i in np.unique(track(r[0])["w"][r[1]:r[2]:r[3]]))
        deps.discard(-1)
        for r in writes:
            h = track(r[0])
            h["w"][r[1]:r[2]:r[3]] = me
            for j, cols in list(h["r"].items()):
                if cols[r[1]:r[2]:r[3]].any():
                    deps.add(j)
                    cols[r[1]:r[2]:r[3]] = False
                    if not cols.any():
                        del h["r"][j]
        for r in reads:
            h = track(r[0])
            h["r"].setdefault(me, np.zeros(len(h["w"]), bool))[r[1]:r[2]:r[3]] = True
        ops.append({"q": q, "fn": fn, "cost": cost, "kind": kind, "lat": lat, "deps": deps, "order": set(after), "grp": grp,
                    "banks": set(r[0] for r in reads + writes if r[0] in PS), "sem": sem, "inc": inc, "soft": set(),
                    "name": (writes + reads)[0][:2]})
        return me

    def R(name, a=0, b=None, st=1, p=None):
        if name in ("zB", "zC"):
            return ("w" + name, a + 256, (256 if b is None else b) + 256, st, p)
        if b is None:
            b = SB[name][0] if name in SB else 512
        return (name, a, b, st, p)

    def IND(win, off):
        return ("ind", win, off)

    def ap(r):
        if r[0] == "ind":
            return ap(r[1]).indirect(ap(r[2]))
        n, a, b, st, p = r
        if "#" in n:
            n = PLAN["plan"][5][n]
        if n in PLACE:
            n, at = PLACE[n]
            a, b = a + at, b + at
        c = slice(a, b) if st == 1 else slice(a, b, st)
        return T[n][:, c] if p is None else T[n][p[0]:p[1], c]

    def size(r):
        return 16 * size(r[2]) if r[0] == "ind" else len(range(r[1], r[2], r[3]))

    def narrow(r):
        return r[0] in SB and SB[r[0]][1] in (B, U, H)

    def val(s):
        return ap(s) if isinstance(s, tuple) else s

    def do(q, ins, out, fn, cyc, **kw):
        reads, writes = [], []
        n = size(out)
        cost = OPT["fixS"] + n * CY if q == "S" and OPT["fixS"] else max(64, n * cyc) * CY
        for r in ins:
            if isinstance(r, tuple):
                if r[0] == "ind":
                    reads += [r[1], r[2]]
                    cost = 0.06 + n * GA * CY
                else:
                    reads.append(r)
        if out[0] == "ind":
            reads.append(out[2])
            writes.append(out[1])
            cost = 0.05 + n * SCAT * CY
        else:
            writes.append(out)
        i = record(q, reads, writes, fn, kw.pop("cost", cost), **kw)
        ops[i]["ind"] = n * (SCAT if out[0] == "ind" else GA if any(isinstance(r, tuple) and r[0] == "ind" for r in ins) else 0) * CY
        return i

    def half(*rs):
        return 0.5 if all(narrow(r) for r in rs) else 1

    def tt(out, a, b, op):
        return do("V", [a, b], out, lambda: g.vector.tensor_tensor(ap(out), ap(a), ap(b), op), 1 if a[0] in PS or b[0] in PS else 2)

    def ts(out, a, s1, op0, s2=None, op1=None):
        if op1 is None:
            return do("V", [a, s1], out, lambda: g.vector.tensor_scalar(ap(out), ap(a), val(s1), None, op0), half(out, a))
        return do("V", [a, s1, s2], out, lambda: g.vector.tensor_scalar(ap(out), ap(a), val(s1), val(s2), op0, op1), half(out, a))

    def cp(out, a):
        return do("V", [a], out, lambda: g.vector.tensor_copy(ap(out), ap(a)), half(out, a))

    def fill(out, c):
        return do("V", [], out, lambda: g.vector.memset(ap(out), c), half(out))

    def scan(out, d0, d1, init, op0, op1):
        return do("V", [d0, d1], out, lambda: g.vector.tensor_tensor_scan(ap(out), ap(d0), ap(d1), init, op0, op1), 1)

    def act(out, a, f, bias=None, scale=None):
        def fn():
            if bias is None and scale is None:
                return g.scalar.activation(ap(out), ap(a), f)
            if bias is None:
                return g.scalar.activation(ap(out), ap(a), f, scale=val(scale))
            return g.scalar.activation(ap(out), ap(a), f, bias=val(bias), scale=val(scale))
        return do("S", [a, bias, scale], out, fn, 1)

    group = {}

    def mm(out, l, r, start=True, stop=True, after=()):
        bank = out[0]
        prev = list(after) if start else [group[bank]]
        cost = max(min(64, size(l)), size(r)) * (4 if SB[l[0]][1] == F else 1) * OPT["cyT"] * OPT["f"]
        group[bank] = do("T", [l, r], out, lambda: g.tensor.matmul(ap(out), ap(l), ap(r), start, stop), 1, cost=cost,
                         grp=(bank, start, stop), after=prev)
        return group[bank]

    def iota(out, pat, base, cm):
        cost = 0.13 + 2 * size(out) * CY
        if SB[out[0]][1] != I:
            return do("G", [], out, lambda: g.iota(ap(out), pat, base, cm, allow_small_or_imprecise_dtypes=True), 1, cost=cost)
        return do("G", [], out, lambda: g.iota(ap(out), pat, base, cm), 1, cost=cost)

    def gcopy(out, a):
        n = size(out)
        return do("G", [a], out, lambda: g.affine_select(ap(out), ap(a), [[0, n]], OP.is_ge, 0.0, 0, 0), 1, cost=OPT["gfix"] + 2 * n * CY)

    def copy(out, a, qs, scale=None):
        ways = {"G": lambda: gcopy(out, a), "S": lambda: act(out, a, AF.Copy, None, scale),
                "V": lambda: cp(out, a) if scale is None else ts(out, a, scale, OP.mult)}
        return either(*[ways[q] for q in qs])

    def plus(out, a, c=0.0):
        if not OPT["sx"]:
            return ts(out, a, c, OP.add)
        return either(lambda: ts(out, a, c, OP.add), lambda: act(out, a, AF.Identity, c, 1.0))

    def either(*ways):
        first = len(ops)
        alt = {}
        for way in ways:
            way()
            alt[ops[-1]["q"]] = (ops[-1]["fn"], ops[-1]["cost"])
            if len(ops) > first + 1:
                for h in hist.values():
                    h["w"][h["w"] == first + 1] = first
                    h["r"].pop(first + 1, None)
                ops.pop()
        ops[first]["alt"] = alt
        return first

    nd, nm, lastdma = [0], [0], {}

    def newsem():
        nd[0] += 1
        return "d%d" % (nd[0] - 1)

    def dma(q, out, in_, reads, writes, nbytes, sem=None, chain=True):
        i = record(q, reads, writes, lambda: QS[q].dma_start(out, in_), 0.1, kind="dma", lat=nbytes / OPT["rate"], sem=sem or newsem(),
                   inc=16, after=[lastdma[q]] if chain and q in lastdma else [])
        lastdma[q] = i
        return i

    def send(src, dst, to):
        k = nm[0]
        nm[0] += 1
        engs = topo.engines(core, to)[:8]
        rid, pid, _s = topo.addr(to)
        nb = 128 * size(src) * (2 if narrow(src) else 4)

        def fn():
            return g.remote_dma(out_ap=ap(dst), in_ap=ap(src), remote_sem=T.sem["a%d" % k], local_sem=T.sem["l%d" % k], pid=pid,
                                routing_id=rid, dma_engine_mask=sum(1 << e for e in engs))
        i = record("G", [src], [], fn, 0.4 if k else 2.4, kind="send", lat=0.5 + nb / 40e3, sem="l%d" % k, inc=len(engs))
        record("A", [], [dst], None, 0.0, kind="land", lat=OPT["land"], sem="a%d" % k, inc=len(engs), after=[i])
        return i

    def chain(ids):
        for a, b in zip(ids, ids[1:]):
            ops[b]["soft"].add(a)

    def C(i):
        return R("col", i, i + 1)

    SH, AN = OP.arith_shift_right, OP.bitwise_and
    EQ, MU, AD, SU, MX, MN, LE, GT, LT = OP.is_equal, OP.mult, OP.add, OP.subtract, OP.max, OP.min, OP.is_le, OP.is_gt, OP.is_lt
    ROW = (0, 1)

    def hn(h):
        return (128 * h, 128 * h + 128)

    def hm(h):
        return (8 * h, 8 * h + 8)

    def edges(k, q):
        s = newsem()
        for gg in range(4 * k, 4 * k + 4):
            c = R("t0", 64 * gg, 64 * gg + 64, 1, (0, 64))
            dma(q, ap(c), T.E[16 * gg:16 * gg + 2, :], [], [c], 38000, s)
    whole = {"z": ("zA", T.z0, 100000), "L": ("LA", T.L0, 170000), "v": ("vA", T.v0, 50000), "X": ("xS", T.X, 560000), "E": ("eS", T.E, 1090000)}
    for q, names in zip("SY", OPT["load"]):
        for c in names:
            if c in whole:
                to = R(whole[c][0], 0, whole[c][1].shape[1])
                dma(q, ap(to), whole[c][1][:], [], [to], whole[c][2])
            else:
                edges(int(c), q)

    iota(R("iC", 0, 1), [[0, 1]], 0, 1)
    iota(R("iD"), [[1, 128]], 0, -1)
    iota(R("iN"), [[1, 32]], 0, 0)
    iota(R("gp"), [[0, 2], [1, 8]], 0, 0)
    iota(R("kk"), [[0, 16], [1, 16]], 0, 0)
    iota(R("e32"), [[1, 32], [0, 16]], 0, 0)
    iota(R("io"), [[1, 144]], 0, 0)
    iota(R("KLc", p=ROW), [[0, 8], [4096, 16]], 65536, 0)
    iota(R("g16"), [[16, 8]], 0, 0)
    iota(R("g32"), [[32, 8]], 0, 0)
    iota(R("mg"), [[1, 8], [0, 16]], 0, 0)
    for c in range(0, 2304, 384):
        iota(R("io2k", c, c + 384), [[1, 384]], c, 0)
    cp(R("zl"), R("iN"))
    ts(R("iC", 1, 2), R("iC", 0, 1), 4, SH)
    ts(R("iC", 2, 3), R("iC", 0, 1), 15, AN)
    ts(R("iC", 3, 4), R("iC", 0, 1), 7, AN)
    ts(R("iC", 4, 5), R("iC", 0, 1), 3, SH, 1, AN)
    ts(R("iC", 5, 6), R("iC", 0, 1), 31, AN)
    cp(R("col", 0, 6), R("iC", 0, 6))
    PP, PG, PK, P7, KY, P32 = C(0), C(1), C(2), C(3), C(4), C(5)
    ts(R("col", 8, 16), R("gp", 0, 8), PK, EQ)
    for t in range(2):
        tt(C(16 + t), C(8 + 2 * t), C(9 + 2 * t), AD)
    ts(R("col", 18, 20), R("col", 16, 18), -1.0, MU, 1.0, AD)
    ts(C(20), PK, 1.0, MU, 0.5, AD)
    ts(C(21), PK, -1.0, MU, -0.5, AD)
    ts(C(22), PK, -2.0, MU, -63.5 / 64, AD)
    ts(C(25), PP, 2.0, MU, 2048.0, AD)
    ts(C(26), PP, 2.0, MU, 65536.0 + 2048.0, AD)
    ts(C(27), PK, 2.0, MU, 2048.0, AD)
    for h in range(2):
        ts(C(36 + h), PK, 64.0 + 128.0 * h, AD)
        ts(R("B64", *hm(h)), R("gp", 0, 8), PG, EQ, 64.0 - 128.0 * h, MU)
    fill(R("eS", 2048, 2304), 0)
    fill(R("XB", 2048, 2304), 0.0)
    ts(C(28), PK, 1.0, AD)
    ts(C(29), C(8), 16.0, MU, -1.0, AD)
    tt(C(31), C(9), C(8), SU)
    ts(C(30), C(31), 16.0, MU)
    fill(R("ones"), 1.0)
    fill(R("cq"), -0.25)
    fill(R("c175", p=ROW), 1.75)
    fill(R("NP"), 0.0)
    for j, c in enumerate((1.0 / 128, -1.0, 1.0, 0.5)):
        ts(R("IM", 128 * j, 128 * j + 128), R("iD"), 0.0, EQ, c, MU)
    PHI, nI, Ib, Ih = [R("IM", 0, 256)] + [R("IM", 128 * j, 128 * j + 128) for j in range(1, 4)]
    If = R("If")
    ts(If, R("iD"), 0.0, EQ)
    ts(R("EXP"), R("e32"), P32, EQ)
    ts(R("W16"), R("gp"), PG, EQ, 4096.0, MU)
    ts(C(23), P7, 16.0, MU, 16.0, AD)
    ts(C(24), KY, -127.0, MU, 128.0, AD)
    ts(R("Z2"), R("io"), C(23), EQ, C(24), MU)
    ts(R("maskJ"), R("kk"), 0.0, EQ, 33554432.0, MU)
    ts(R("RST"), R("maskJ"), -256.0, AD)
    ts(R("nI16"), R("iD"), 0.0, EQ, -1.0, MU)
    ts(R("ROT"), R("iD"), C(29), EQ)
    ts(R("Sel0"), R("mg"), PG, EQ, C(8), MU)
    ts(R("RSD"), R("kk", 0, 128), 0.0, EQ, C(26), MU)
    ts(R("maskJ"), R("kk"), PK, EQ)
    ts(R("B128"), R("gp", 0, 8), PG, EQ, 128.0, MU)
    I16 = R("I16")
    ts(I16, R("iD"), 0.0, EQ)
    ts(R("B8h"), R("gp", 0, 8), PG, EQ)
    ts(R("BB4"), R("mg"), PG, EQ, 4096.0, MU)
    for out, c in ((R("B8", 0, 8), 1.0), (R("B8", 8, 16), -1.0), (R("W8", 0, 8), C(20)), (R("W8", 8, 16), C(21)),
                   (R("B8f", 0, 8), 1.0), (R("B8i"), 0.5), (R("SelC", 0, 8), C(8)),
                   (R("SelC", 8, 16), C(10)), (R("WY", 0, 8), C(28)), (R("WY", 8, 16), C(29)),
                   (R("WY", 16, 24), C(30))):
        ts(out, R("gp", 0, 8), PG, EQ, c, MU)
    B8p, B8n = R("B8", 0, 8), R("B8", 8, 16)
    scan(R("wrow", p=ROW), R("c175", p=ROW), R("cq", p=ROW), 2.0 ** -120 / 1.75, MU, MX)
    for h in range(2):
        mm(R("N1", 256 + h, 257 + h), R("wrow", *hn(h), 1, ROW), R("If", 0, 1, 1, ROW))
    cp(R("wcol"), R("N1", 256, 258))
    ts(R("col", 34, 36), R("wcol"), 2.54, MU)

    cp(R("vlA"), R("vA"))
    send(R("zA"), R("zB"), nxt)
    copy(R("Lo0"), R("LA"), OPT["Lo0"])
    send(R("Lo0"), R("LB"), nxt)
    for k in range(2):
        cp(R("tf", 256 * k, 256 * k + 256, 1, (0, 64)), R("t0", 256 * k, 256 * k + 256, 1, (0, 64)))
    ids = []
    for b in range(4):
        mm(R("N0", 64 * b, 64 * b + 64), R("tf", b, 512, 4, (0, 64)), R("I16", 0, 64, 1, (0, 64)))
    cp(R("el"), R("N0", 0, 256))
    for b in range(4):
        c = R("XB", b, 2048, 4)
        copy(c, IND(R("xS"), R("el", 64 * b + 32, 64 * b + 64)), OPT["B"])
        if b >= 4 - OPT["tabS"]:
            a, bank = R("sh", 512 * b, 512 * b + 512), R("K%d" % (b % 2))
            act(a, IND(R("xS"), R("el", 64 * b, 64 * b + 32)), AF.Copy)
            mm(bank, Ib, a)
            ids += [tt(R("HI", b, 2048, 4), bank, c, MX), tt(R("LO", b, 2048, 4), bank, c, MN)]
            continue
        for tab, op in (("HI", MX), ("LO", MN)):
            ids.append(tt(R(tab, b, 2048, 4), IND(R("xS"), R("el", 64 * b, 64 * b + 32)), c, op))
    chain(ids)
    chain([copy(R("ef", c, c + 256), R("eS", c, c + 256), OPT["ef"]) for c in range(0, 2048, 256)])
    for hi in range(16):
        mm(R("M", hi, 384, 16), R("ef", 128 * hi, 128 * hi + 128), R("WY"))

    pb = [0]

    def minus_zT(z, h, zT="zT"):
        mm(R("N%d" % h, 0, 128), R(z, *hn(h)), nI)
        copy(R(zT, *hn(h)), R("N%d" % h, 0, 128), OPT["sm"])

    def expand(t, zx, z, zwalk):
        ids = []
        for h in range(2):
            a, b = 128 * h, 128 * h + 128 - 32 * OPT["gS"][t][h]
            if a < b:
                ids += [copy(R(zx, 16 * a + k, 16 * b, 16), R(z, a, b), OPT["exp"][t]) for k in range(16)]
        chain(ids)
        a, b = 128 - 32 * max(OPT["vx"][t]), 128 + 32 * max(OPT["vx"][t])
        if OPT["expw"][t] == "G":
            chain([gcopy(R("zw", 16 * a + k, 16 * b, 16), R(zwalk, a, b)) for k in range(16 * (a < b))])
        else:
            for c in range(a, b, 32):
                copy(R("zw", 16 * c, 16 * c + 512), IND(R(zwalk, c, c + 32), R("zl")), OPT["expw"][t])

    def tolist(h, parts, out, add, lo, byT):
        kb = "K%d" % h
        a = 256 * h
        if byT:
            P16, n = (0, 16), 2 if lo else 1
            cp(R("wb", 16 * h, 16 * h + 16), parts)
            mm(R(kb, 384, 512, 1, P16), R("wb", 16 * h, 16 * h + 16), Ib)
            copy(R("wT", a, a + 128, 1, P16), R(kb, 384, 512, 1, P16), "SV")
            if lo:
                copy(R("wT", a + 128, a + 256, 1, P16), R(kb, 384, 512, 1, P16), "SV", R("col", 4, 5, 1, P16))
            for j in range(16):
                mm(R(kb, 256, 256 + 8 * n), R("Z2", 16 - j, 144 - j, 1, P16), R("wT", a + j, a + 128 * n, 16, P16), j == 0, j == 15)
            ts(R(out, *hm(h)), R(kb, 256, 264), add, AD)
            if lo:
                cp(R(lo, *hm(h)), R(kb, 264, 272))
            return
        tt(R("wT", a, a + 256), IND(parts, R("zl", 0, 16)), R("maskJ"), MU)
        mm(R(kb, 256, 264), R("wT", a, a + 128), R("B128"), True, False)
        mm(R(kb, 256, 264), R("wT", a + 128, a + 256), B8p, False, True)
        plus(R(out, *hm(h)), R(kb, 256, 264), add)
        if lo:
            mm(R(kb, 264, 272), R("wT", a + 128, a + 256), B8p)
            plus(R(lo, *hm(h)), R(kb, 264, 272))

    def masked(h, win, at, slot, n=1, base=False):
        kb, gm, one = "K%d" % h, "gm32" if base else "gm", R("B8f" if base else "B8h", 0, 8)
        tt(R(gm, at, at + 128 * n), IND(win, R("zl", 0, 8 * n)), R("maskJ", 0, 128 * n), MU)
        for j in range(n):
            o = R(kb, slot + 8 * j, slot + 8 * j + 8)
            mm(o, R(gm, at + 128 * j, at + 128 * j + 128), one, True, not base)
            if base:
                mm(o, R("ones", p=ROW), R("g32", p=ROW), False, True)

    def minus_z(src, b, zT, f, dst):
        bank = "P#%d" % pb[0]
        pb[0] += 1
        q, n = 32 * (b // 512 % 4), hn(b // 2048)
        first = mm(R(bank), Ib, src, True, False, pb[1:] if zT == "zT" else ())
        ops[first]["take"] = bank
        if zT == "zT":
            pb[1:] = [first]
        second = mm(R(bank), R(zT, *n, 1, (q, q + 32)), R("EXP", p=(q, q + 32)), False, True)
        ops[first]["deps"] |= ops[second]["deps"] - {first}
        last = act(dst, R(bank), f)
        ops[last]["give"] = bank
        return last

    def apart(out, lst):
        act(out, IND(R("io2k"), lst), AF.Abs, C(22), 1.0 / 64)

    behind = []

    def walk(t, step, h, vl, lo, out, outlo=None):
        n, m, kb = hn(h), hm(h), "K%d" % h
        plus(R("c16", *n), IND(R("eS", 0, 2048), R(vl, *m)))
        if OPT["cfG"][t]:
            either(lambda: gcopy(R("cf", *n), R("c16", *n)), lambda: ts(R("cf", *n), R("c16", *n), 0.0, AD))
        else:
            plus(R("cf", *n), R("c16", *n))
        plus(R("H", *n), R("c16", *n), 16448.5)
        onV = OPT["vx"][t][step]
        for j in range(4):
            b = 2048 * h + 512 * j
            x = IND(R("xS"), R("c16", b // 16, b // 16 + 32))
            if (j >= onV if h else j < 4 - onV):
                ops[act(R("xg", b, b + 512), x, AF.Copy)]["order"].update(behind[-OPT["ahead"]:][:1])
                behind.append(minus_z(R("xg", b, b + 512), b, "zT", AF.Abs, R("ab", b, b + 512)))
            else:
                tt(R("xg", b, b + 512), x, R("zw", b, b + 512), SU)
                act(R("ab", b, b + 512), R("xg", b, b + 512), AF.Abs)
        mm(R(kb, 0, 256), R("H", *n), PHI, True, False)
        mm(R(kb, 128, 256), R("cf", *n), I16, False, False)
        if lo:
            apart(R("ad", *n), R(vl, *m))
            tt(R("mk", *n), IND(R("m0"), R(lo, *m)), R("ad", *n), GT)
        for p in ((0, 96), (96, 128)) if OPT["cut"][t] else ((0, 128),):
            for k in range(16):
                i = mm(R(kb, k, 256, 16, p), R("ab", 2048 * h + 16 * p[0] + k, 2048 * h + 16 * p[1], 16), R("W16"), False,
                       k == 15 and not lo)
                if p[1] < 128:
                    ops[i]["grp"] = (kb, False, False)
        if lo:
            mm(R(kb, 0, 256, 16), R("mk", *n), R("W16"), False, True)
        scan(R("R", 256 * h, 256 * h + 256), R("RST"), R(kb, 0, 256), 0.0, AD, MN)
        a = (16 * h, 16 * h + 16)
        ts(R("wa", *a), R("R", 256 * h + 15, 256 * h + 256, 16), 127, AN)
        tolist(h, R("wa", *a), out, -128.0, outlo, OPT["tr"][t][2 * step + h])

    gaps = []

    def gap(t, h, z, L16, zx, ini):
        onS, known, n = OPT["gS"][t][h], OPT["patch"][t][h], hn(h)
        copy(R("Lf", *n), R(L16, *n), "VS" if OPT["sx"] else "V", C(18 + t))
        for e in range(2):
            copy(R("r%d" % (e + 1), *n), IND(R("io2k"), R(ini[e], *hm(h))), OPT["s16"], C(8 + 2 * t + e))
        if known:
            s3, rows = R("N%d" % h, 384, 512), ["r2", "r1", "Lf"][2 - known:]
            for i, r in enumerate(rows):
                mm(s3, I16, R(r, *n), i == 0, i == known)
            L16 = "Lp"
            cp(R(L16, *n), s3)
            ts(R("Lq", *n), R(L16, *n), 0.0, AD)
        if onS:
            minus_zT(z, h, "zT2")
        for j in range(4):
            n0 = 128 * h + 32 * j
            a = (16 * n0, 16 * n0 + 512)
            for tab, dst, sb in (("HI", "mh", "sh"), ("LO", "ml", "so")):
                x = IND(R(tab, 0, 2048), R(L16, n0, n0 + 32))
                if j < 4 - onS:
                    at = n0
                    for w in OPT["gw"][t]:
                        c = (16 * at, 16 * (at + w))
                        gaps.append(tt(R(dst, *c), IND(R(tab, 0, 2048), R(L16, at, at + w)), R(zx, *c), MX))
                        at += w
                else:
                    act(R(sb, *a), x, AF.Copy)
                    minus_z(R(sb, *a), a[0], "zT2", AF.Relu, R(dst, *a))
        ks = [k for k in range(16) if k // 2 != t or k % 2 < known]
        if OPT["one"]:
            for src, w in (("mh", B8p), ("ml", B8n)):
                for k in ks:
                    mm(R("G", 128 * h + k, 128 * h + 128, 16), R(src, 2048 * h + k, 2048 * h + 2048, 16), w, src == "mh" and k == ks[0],
                       src == "ml" and k == ks[-1])
            return
        for k in ks:
            o = R("G", 128 * h + k, 128 * h + 128, 16)
            mm(o, R("mh", 2048 * h + k, 2048 * h + 2048, 16), B8p, True, False)
            mm(o, R("ml", 2048 * h + k, 2048 * h + 2048, 16), B8n, False, True)

    def entry(t, h, e, z, vl):
        a = (256 * e + 128 * h, 256 * e + 128 * h + 128)
        if OPT["enS"][t][e]:
            bank = "P#%d" % pb[0]
            pb[0] += 1
            for j, tab in enumerate(("HI", "LO")):
                act(R("es", 2 * a[0] + 128 * j, 2 * a[0] + 128 * j + 128), IND(R(tab, 0, 2048), R(vl, *hm(h))), AF.Copy)
            ops[mm(R(bank, 0, 256), Ib, R("es", 2 * a[0], 2 * a[1]), True, False)]["take"] = bank
            for j in range(2):
                last = mm(R(bank, 128 * j, 128 * j + 128), nI, R(z, *hn(h)), False, j == 1)
            ops[act(R("eh", *a), R(bank, 0, 128), AF.Relu)]["deps"].add(last)
            ops[act(R("en", *a), R(bank, 128, 256), AF.Relu)]["give"] = bank
            ops[-1]["order"].add(len(ops) - 2)
        else:
            tt(R("eh", *a), IND(R("HI", 0, 2048), R(vl, *hm(h))), R(z, *hn(h)), MX)
            tt(R("en", *a), IND(R("LO", 0, 2048), R(vl, *hm(h))), R(z, *hn(h)), MX)
        o = R("G", 128 * h + 2 * t + e, 128 * h + 128, 16)
        mm(o, R("eh", *a), B8p, True, False)
        mm(o, R("en", *a), B8n, False, True)

    def decide(t, h, z, L16, xi, zo, Lo):
        n, m, kb, nb = hn(h), hm(h), "K%d" % h, "N%d" % h
        s0, s1, s3 = R(nb, 0, 128), R(nb, 128, 256), R(nb, 384, 512)

        def Q(i, w=8):
            return R("qs", 128 * h + 8 * i, 128 * h + 8 * i + w)

        def QI(i, w=8):
            return R("qi", 64 * h + 8 * i, 64 * h + 8 * i + w)

        def QB(i, w=8):
            return R("qb", 48 * h + 8 * i, 48 * h + 8 * i + w)

        def acc(o, pairs, after=()):
            for i, (l, r) in enumerate(pairs):
                last = mm(o, l, r, i == 0, i == len(pairs) - 1, after)
            return last
        zz, x, sl = R(z, *n), R(xi, *n), R("sl", *n)
        ab, hb = R("w" + z, 640 * h, 640 * h + 128), R("w" + z, 128 + 384 * h, 256 + 384 * h)
        r2 = R("r2", *n)
        log = [R(r, *n) for r in (("r2", "r1", "Lf"), ("r2", "Lq"), ("Lq",))[OPT["patch"][t][h]]]
        acc(s0, [(Ib, x), (nI, zz)])
        acc(s1, [(Ih, x), (R("cq", 0, 128, 1, ROW), R("ones", p=ROW)), (Ih, zz)])
        act(ab, s0, AF.Abs)
        ts(hb, s1, 12582912.0, AD, -12582912.0, AD)
        mm(s0, R("BB4"), ab)
        act(sl, s0, AF.Sign, TH + 0.5, -1.0 / 4096)
        mm(R(nb, 256, 264), ab, B8p)
        acc(R(nb, 264, 272), [(hb, R("W8", 8, 16)), (r2, R("B8i"))])
        acc(R(nb, 272, 280), [(hb, R("W8", 0, 8)), (r2, R("B8i"))])
        act(Q(0), R(nb, 256, 264), AF.Sign, TH + 0.5, -1.0)
        tt(Q(1), R(nb, 264, 272), Q(0), MU)
        tt(QI(0), R(nb, 272, 280), Q(1), AD)
        ts(QI(1), QI(0), 2047, AN)
        plus(R("NP", 0, 128, 16), QI(1))
        mm(s3, R("NP"), I16)
        plus(R("eS", 2048, 2304, 2), s3)
        either(lambda: act(R("fk", *n), R("G", *n), AF.Relu, 262144.0 * (TAU[t] + 0.5), -262144.0),
               lambda: ts(R("fk", *n), R("G", *n), float(TAU[t]), LE, 131072.0, MU))
        key = R(kb, 0, 128)
        acc(key, [(r, I16) for r in log] + [(R("ones", p=ROW), R("KLc", p=ROW)), (sl, R("BB4")), (Ib, R("fk", *n))])
        scan(R("R2", *n), R("RSD"), key, 0.0, MX, MN)
        end = R("R2", 128 * h + 15, 128 * h + 128, 16)
        ts(QI(5), end, 4095, AN)
        ts(Q(7), end, 65536.0, LT, 2.0, MU)
        tt(QI(6), Q(7), Q(0), SU)
        ul, ce = R("ul", *m), R("ce", *n)
        if OPT["two"][t]:
            for j in range(2):
                tt(R("gu", 256 * h + 128 * j, 256 * h + 128 * j + 128), IND(QI(5 + j), R("zl", 0, 8)), R("maskJ", 0, 128), MU)
        else:
            tt(R("gu", 256 * h, 256 * h + 256), IND(QI(5, 16), R("zl", 0, 16)), R("maskJ"), MU)
        mm(R(kb, 256, 264), R("gu", 256 * h, 256 * h + 128), R("B8h"))
        plus(ul, R(kb, 256, 264))
        plus(ce, IND(R("eS"), ul))
        ts(QI(3), end, 7, SH, 31, AN)
        ts(QI(4), end, 127, AN)
        cp(QB(0), QI(4))
        acc(R(kb, 312, 320), [(R("gu", 256 * h + 128, 256 * h + 256), R("B64", *m)), (R("ones", p=ROW), R("g16", p=ROW))])
        plus(R("zs", *m), R(kb, 312, 320), C(36 + h))
        copy(zo, IND(R("w" + z, 384 * h, 384 * h + 384), R("zs", *m)), OPT["s16"] if t else "SV")
        tt(R("flag", *n), key, R("R2", *n), EQ)
        if t == 0:
            tt(R("gl", *n), IND(QI(4), R("zl", 0, 8)), R("maskJ", 0, 128), MU)
            mm(R(kb, 264, 272), R("gl", *n), R("B8h"))
            plus(R("ulo", *m), R(kb, 264, 272))
            apart(R("adu", *n), ul)
            mm(R(kb, 128, 144), ce, R("SelC"))
            copy(Q(2, 16), R(kb, 128, 144), "SV")
            vo = Q(2)
            masked(h, vo, 384 * h, 272)
            plus(R("vlB", *m), R(kb, 272, 280))
            plus(R("vi", 16 * h, 16 * h + 8), R(kb, 272, 280))
            ts(R("vi", 16 * h + 8, 16 * h + 16), R("vi", 16 * h, 16 * h + 8), 127, AN)
            plus(R("loB", *m), R("vi", 16 * h + 8, 16 * h + 16))
        else:
            mm(R(kb, 128, 136), ce, R("SelC", 0, 8))
            copy(R("fo%d" % h, 128, 136), R(kb, 128, 136), OPT["s16"])
        if t == 0:
            acc(R(kb, 384, 512), [(ce, R("Sel0"))] + [(r, R("nI16")) for r in log])
            tt(R("e2", *n), R(kb, 384, 512), R("flag", *n), MU)
            acc(s3, [(R("e2", *n), I16)] + [(I16, r) for r in log])
            plus(Lo, s3)
        else:
            first = [acc(s1, [(I16, r) for r in log]), mm(s3, R("flag", *n), Ib)]
            copy(R("flagN", *n), s3, "SV")
            acc(s0, [(R("nI16"), r) for r in log] + [(R("Sel0"), ce)], first)
            tt(R("e2", *n), s0, R("flagN", *n), MU)
            tt(Lo, s1, R("e2", *n), AD)
        tt(R("OHh", *n), IND(QI(3), R("zl", 0, 8)), R("kk", 0, 128), EQ)
        ids = []
        for c in range(8):
            a = R("OH", 1024 * h + 128 * c, 1024 * h + 128 * c + 128)
            ids.append(ts(a, R("io", 0, 128), R("qb", 48 * h + c, 48 * h + c + 1), EQ, R("wcol", h, h + 1) if t == 0 else 1.0, MU))
            mm(R("M", 384 + 16 * c, 400 + 16 * c), a, R("OHh", 128 * h + 16 * c, 128 * h + 16 * c + 16), h == 0 and c == 0, h == 1 and c == 7)
        chain(ids)
        if t == 0:
            masked(h, Q(3), 384 * h + 128, 280)
            plus(R("e12", *m), R(kb, 280, 288))
            copy(R("nB", *n), IND(R("xS"), R("e12", *m)), "SV")
            tt(R("nH", *n), IND(R("XB"), ul), R("nB", *n), MX)
            tt(R("nL", *n), IND(R("XB"), ul), R("nB", *n), MN)
            either(lambda: act(R("ad2", *n), R("adu", *n), AF.Relu, 9e29, -9e29),
                   lambda: ts(R("ad2", *n), R("adu", *n), 1.0, LT, 9e29, MU))
            ts(Q(6), QI(5), C(25), SU)
            mm(s0, R("ROT"), ce)
            copy(R("nE", *n), s0, "SV")

    def turn(h):
        n, m, kb = hn(h), hm(h), "K%d" % h
        tt(R("mn", *n), IND(R("Sb"), R("ulo", *m)), R("ad2", *n), MN)
        mm(R(kb, 296, 304), R("mn", *n), B8p)
        a = 128 * h
        ts(R("qs", a + 56, a + 64), R(kb, 296, 304), C(34 + h), LE)
        tt(R("qs", a + 64, a + 72), R("qs", a + 56, a + 64), R("qs", a + 48, a + 56), MU)
        masked(h, R("qs", a + 64, a + 72), 128 * h, 304, 1, True)
        plus(R("u2", *m), R(kb, 304, 312), C(27))
        cp(IND(R("HI"), R("u2", *m)), R("nH", *n))
        cp(IND(R("LO"), R("u2", *m)), R("nL", *n))

    def rotate():
        for h in range(2):
            cp(IND(R("eS"), R("u2", *hm(h))), R("nE", *hn(h)))

    def visit(t, vl, lo, v1, v2, xo, z, L16, zx, ini):
        expand(t, zx, z, "zo1" if t else "zA")
        for h in range(2):
            walk(t, 0, h, vl, lo, v1, "lo1" if t and h < OPT["rot"] else None)
        send(R(v1), R(ini[0]), nxt)
        for h in range(2):
            if t and h == OPT["rot"]:
                rotate()
            walk(t, 1, h, v1, "lo1" if t and h < OPT["rot"] else None, v2)
            if t and h == 1 and OPT["rot"] == 2:
                rotate()
            send(R(v2, *hm(h)), R(ini[1], *hm(h)), nxt)
            copy(R(xo, *hn(h)), IND(R("xS"), R(v2, *hm(h))), "SV")
            send(R(xo, *hn(h)), R(ini[2], *hn(h)), nxt)
        del gaps[:]
        for h in range(2):
            gap(t, h, z, L16, zx, ini)
        chain(gaps)
        for h in range(2):
            for e in range(OPT["patch"][t][h], 2):
                entry(t, h, e, z, ini[e])

    for h in range(2):
        minus_zT("zA", h)
    visit(0, "vlA", None, "v1o0", "v2o0", "xo0", "zB", "LB", "zx0", ("v1i0", "v2i0", "xi0"))
    for h in range(2):
        decide(0, h, "zB", "LB", "xi0", R("zo1", *hn(h)), R("Lo1", *hn(h)))
        send(R("zo1", *hn(h)), R("zC", *hn(h)), nxt)
        minus_zT("zo1", h)
        send(R("Lo1", *hn(h)), R("LC", *hn(h)), nxt)

    def counted(out, a):
        either(lambda: act(R(out), a, AF.Sign), lambda: ts(R(out), a, 0.0, GT))
    copy(R("St"), R("M", 384, 512), "SV")
    mm(R("G", 256, 384), R("St"), Ib)
    counted("m0", R("G", 256, 384))
    copy(R("Sb"), R("G", 256, 384), "SV")
    counted("m0t", R("M", 384, 512))
    for h in range(2):
        turn(h)
    tt(R("ya1"), R("M", 128, 256), R("m0t"), MU)
    tt(R("ya2"), R("M", 256, 384), R("m0t"), MU)
    tt(R("M", 0, 128), R("M", 0, 128), R("ya1"), AD)
    tt(R("M", 128, 256), R("M", 128, 256), R("ya2"), AD)

    visit(1, "vlB", "loB", "v1o1", "v2o1", "xo1", "zC", "LC", "zx1", ("v1i1", "v2i1", "xi1"))
    for h in range(2):
        fo, fi, kb = "fo%d" % h, "fi%d" % h, "K%d" % h
        decide(1, h, "zC", "LC", "xi1", R(fo, 0, 128), R(fo, 136, 264))
        for a, b in ((0, 136), (136, 264)) if OPT["split"][h] else ((0, 264),):
            ops[send(R(fo, a, b), R(fi, a, b), home)]["lead"] = OPT["lead"][1] * (1 - h)
    counted("m1", R("M", 384, 512))
    tt(R("ya1"), R("M", 128, 256), R("m1"), MU)
    tt(R("yat"), R("M", 0, 128), R("ya1"), AD)
    mm(R("G", 256, 384), R("yat"), If)
    copy(R("yas"), R("G", 256, 384), "SV")
    dma("Y", T.ya[:], ap(R("yas")), [R("yas")], [], 1 << 16, chain=False)
    for h in range(2):
        fi, kb = "fi%d" % h, "K%d" % h
        a, b = hn(h)
        oz, ol = R("out", 2 * a, 2 * a + 128), R("out", 2 * a + 128, 2 * b)
        cp(oz, R(fi, 0, 128))
        copy(ol, R(fi, 136, 264), OPT["s16"])
        dma("Y", T.yz[:, a:b], ap(oz), [oz], [], 1 << 16, chain=False)
        dma("S", T.yl[:, a:b], ap(ol), [ol], [], 1 << 16, chain=False)
        mm(R(kb, 384, 512, 1, (0, 8)), R(fi, 128, 136), I16)
        copy(R("yvs", a, b, 1, (0, 8)), R(kb, 384, 512, 1, (0, 8)), "SV")
        dma("Y", T.yv[:, a:b], ap(R("yvs", a, b, 1, (0, 8))), [R("yvs", a, b)], [], 1 << 12, chain=False)

    nop = len(ops)
    for o in ops:
        if o["q"] == "T":
            same = {d for d in o["deps"] if ops[d]["q"] == "T"}
            o["deps"] -= same
            o["order"] |= same
    prio = [0.0] * nop
    for i in range(nop - 1, -1, -1):
        o = ops[i]
        prio[i] += o.get("lead", 0) + o["cost"] + o["lat"] + (1.8 if o["kind"] == "dma" else 0)
        for d in o["deps"] | o["order"] | o["soft"]:
            prio[d] = max(prio[d], prio[i] + WAKE)
    users = [[] for _ in ops]
    for i, o in enumerate(ops):
        o.setdefault("alt", {o["q"]: (o["fn"], o["cost"])})
        for d in o["deps"] | o["order"]:
            users[d].append(i)

    def forward(prio):
        left = [len(o["deps"] | o["order"]) for o in ops]
        cand = {q: [i for i in range(nop) if left[i] == 0 and q in ops[i]["alt"]] for q in "VSTGYA"}
        free = {q: 0.0 for q in cand}
        fin, ready = [0.0] * nop, [0.0] * nop
        lastin = {b: {} for b in PS}
        opened, engines, order, queue, more = {}, 0.0, [], [None] * nop, [None] * nop
        pool, held, cause, before = [(0.0, "P0", -1), (0.0, "P1", -1)], {}, [(None, False)] * nop, {}
        while len(order) < nop:
            best = None
            for q, lst in cand.items():
                at = []
                for i in lst:
                    o = ops[i]
                    if o["grp"] and o["grp"][1] and opened.get(o["grp"][0]):
                        continue
                    r = ready[i]
                    if "take" in o:
                        if not pool:
                            continue
                        r = max(r, min(pool)[0])
                    for b in o["banks"]:
                        for q2, j in lastin[b].items():
                            if q2 != q:
                                r = max(r, fin[j] + WAKE)
                    at.append((max(r, free[q]) if q != "A" else r, i))
                if not at:
                    continue
                t0 = min(at)[0]
                pick = max((x for x in at if x[0] <= t0 + 1e-9), key=lambda x: prio[x[1]])
                for x in at:
                    if prio[x[1]] > prio[pick[1]] and x[0] <= t0 + OPT["look"] * ops[pick[1]]["alt"][q][1]:
                        pick = x
                if best is None or pick[0] < best[0] - 1e-9 or (pick[1] == best[1] and pick[0] < best[0] + 1e-9 and q == ops[pick[1]]["q"]):
                    best = pick + (q,)
            if best is None:
                return (1e9,)
            start, i, q = best
            o = ops[i]
            for q2 in o["alt"]:
                cand[q2].remove(i)
            queue[i] = q
            order.append(i)
            if q != "A" and free[q] > ready[i] and q in before and before[q] not in o["order"]:
                cause[i] = (before[q], True)
            before[q] = i
            free[q] = start + o["alt"][q][1]
            if o["kind"] == "dma":
                engines = fin[i] = max(free[q] + 1.8, engines) + o["lat"]
            else:
                fin[i] = free[q] + o["lat"]
            more[i] = set()
            if "take" in o:
                _t, held[o["take"]], last = min(pool)
                pool.remove(min(pool))
                more[i] = {last} - {-1}
            if "give" in o:
                pool.append((fin[i] + WAKE, held[o["give"]], i))
            for b in o["banks"]:
                more[i] |= {j for q2, j in lastin[b].items() if q2 != q}
                lastin[b][q] = i
            if o["grp"]:
                opened[o["grp"][0]] = not o["grp"][2]
            for u in users[i]:
                waits = i in ops[u]["deps"] or ops[u]["kind"] == "land"
                if (fin[i] + WAKE if waits else free[q]) >= ready[u]:
                    ready[u] = fin[i] + WAKE if waits else free[q]
                    cause[u] = (i, False)
                left[u] -= 1
                if left[u] == 0:
                    for q2 in ops[u]["alt"]:
                        cand[q2].append(u)
        return max(fin), order, queue, more, fin, held, cause

    def backward(queue, fin):
        left = [len(u) for u in users]
        cand = {q: [i for i in range(nop) if left[i] == 0 and queue[i] == q] for q in "VSTGYA"}
        free = {q: 0.0 for q in cand}
        back, ready = [0.0] * nop, [o["lat"] + (1.8 if o["kind"] == "dma" else 0) for o in ops]
        for _ in range(nop):
            best = None
            for q, lst in cand.items():
                if lst:
                    t0 = max(min(ready[i] for i in lst), free[q] if q != "A" else 0.0)
                    pick = max((i for i in lst if ready[i] <= t0 + 1e-9), key=lambda i: fin[i])
                    if best is None or t0 < best[0]:
                        best = (t0, pick, q)
            start, i, q = best
            o = ops[i]
            cand[q].remove(i)
            free[q] = back[i] = start + o["alt"][q][1]
            for d in o["deps"] | o["order"]:
                p = ops[d]
                waits = d in o["deps"] or o["kind"] == "land"
                ready[d] = max(ready[d], back[i] + p.get("lead", 0) + (WAKE + p["lat"] + (1.8 if p["kind"] == "dma" else 0) if waits else 0))
                left[d] -= 1
                if left[d] == 0:
                    cand[queue[d]].append(d)
        return back

    def spread(plan):
        if len(plan) == 1:
            return 1e9
        total = 0.0
        for f, ga in OPT["also"]:
            free, fin, engines = {}, [0.0] * nop, 0.0
            for i in plan[1]:
                o, q = ops[i], plan[2][i]
                t = free.get(q, 0.0) if q != "A" else max(fin[d] for d in o["order"])
                for d in o["deps"]:
                    t = max(t, fin[d] + WAKE)
                for d in plan[3][i]:
                    t = max(t, fin[d] + WAKE)
                c = o["alt"][q][1]
                if o["kind"] == "op":
                    c = c + o["ind"] * (f * ga - 1) if o["ind"] else c * f
                free[q] = t + c
                if o["kind"] == "dma":
                    engines = fin[i] = max(free[q] + 1.8, engines) + o["lat"]
                else:
                    fin[i] = free[q] + o["lat"]
            total += max(fin) / (f * (1 + ga) / 2 + 0.2)
        return total / len(OPT["also"])

    if PLAN.get("opt") != repr(OPT):
        PLAN.clear()
        PLAN["opt"] = repr(OPT)
        PLAN["ops"] = ops
        rng, chains = np.random.default_rng(OPT["seed"]), prio
        for start in range(OPT["starts"]):
            prio = [p + OPT["eps"] * rng.random() * (start > 0) for p in chains]
            for _ in range(OPT["rounds"]):
                plan = forward(prio)
                if len(plan) == 1:
                    break
                plan = (spread(plan),) + plan[1:]
                if "plan" not in PLAN or plan[0] < PLAN["plan"][0]:
                    PLAN["plan"], keep = plan, prio
                    PLAN.setdefault("ends", []).append(round(plan[0], 1))
                prio = backward(plan[2], plan[4])
        plan = PLAN["plan"]
        for step in range(OPT["tries"]):
            i, pairs = max(range(nop), key=lambda j: plan[4][j]), []
            while i is not None:
                j, queued = plan[6][i]
                if queued:
                    pairs.append((i, j))
                i = j
            prio = list(keep)
            for k in rng.choice(len(pairs), min(len(pairs), OPT["swap"]), replace=False):
                i, j = pairs[int(k)]
                prio[i], prio[j] = max(prio[i], prio[j]) + 0.3 * rng.random(), min(prio[i], prio[j]) - 0.3 * rng.random()
            if step % 2:
                prio, up = list(keep), OPT["up"] * rng.random()
                i = pairs[int(rng.integers(len(pairs)))][0]
                todo, seen = [i], {i}
                while todo:
                    j = todo.pop()
                    prio[j] += up
                    for d in ops[j]["deps"] | ops[j]["order"]:
                        if d not in seen and plan[4][d] > plan[4][i] - OPT["win"]:
                            seen.add(d)
                            todo.append(d)
            if step % 16 == 14:
                prio = backward(plan[2], plan[4])
            new = forward(prio)
            new = (spread(new),) + new[1:]
            if new[0] <= plan[0] + OPT["tol"]:
                plan, keep = new, prio
            if new[0] < PLAN["plan"][0]:
                PLAN["plan"] = new
                PLAN["ends"].append(round(new[0], 1))
    order, queue, more = PLAN["plan"][1:4]
    for i, o in enumerate(ops):
        o["q"] = queue[i]
        o["fn"] = o["alt"][queue[i]][0]
        o["deps"] |= more[i]

    total = {}
    for o in ops:
        if o["kind"] == "dma":
            total[o["sem"]] = total.get(o["sem"], 0) + 16
    count, tok = {}, {}
    known = {q: {} for q in QS}
    for i in order:
        o = ops[i]
        q = o["q"]
        s = o["sem"] or "c" + q
        count[s] = count.get(s, 0) + o["inc"]
        v = total[s] if o["kind"] == "dma" else count[s]
        if o["kind"] == "land":
            tok[i] = (s, v, {})
            continue
        kn = known[q]
        want = {}
        for d in o["deps"]:
            if kn.get(tok[d][0], 0) < tok[d][1]:
                want[tok[d][0]] = max(want.get(tok[d][0], 0), tok[d][1])
        for s1 in list(want):
            for d in o["deps"]:
                s2 = tok[d][0]
                if s2 != s1 and s2 in want and tok[d][2].get(s1, 0) >= want[s1]:
                    want.pop(s1)
                    break
        for s1, v1 in want.items():
            QS[q].wait_ge(T.sem[s1], v1)
        for d in o["deps"]:
            for s1, v1 in list(tok[d][2].items()) + [tok[d][:2]]:
                kn[s1] = max(kn.get(s1, 0), v1)
        call = o["fn"]()
        if o["kind"] != "send":
            call.then_inc(T.sem[s], o["inc"])
        tok[i] = (s, v, dict(kn))
    for s, v in count.items():
        if known["G"].get(s, 0) < v:
            g.wait_ge(T.sem[s], v)
